import numpy as np
import ml_dtypes


def mxq(x, axis, fmt="e4m3"):
    dtype, down = {"e4m3": (ml_dtypes.float8_e4m3fn, 7), "e5m2": (ml_dtypes.float8_e5m2, 14)}[fmt]
    v = np.moveaxis(np.asarray(x, np.float32).astype(ml_dtypes.bfloat16).astype(np.float64), axis, -1)
    blocks = v.reshape(v.shape[:-1] + (-1, 32))
    amax = np.abs(blocks).max(-1, keepdims=True)
    byte = np.maximum(np.where(amax > 0, np.frexp(amax)[1] - 1 + 127, 0) - down, 1)
    scale = np.exp2(byte - 127.0)
    codes = (blocks / scale).astype(np.float32).astype(dtype).astype(np.float64)
    return np.moveaxis((codes * scale).reshape(v.shape), -1, axis)


WIDE = False


def mx_kscale(k):
    if not WIDE:
        return np.ones(k)
    levels = np.array([10, -10, 5, -5, 0])
    if k % 512:
        return np.exp2(np.random.permutation(np.resize(levels, k // 32))).repeat(32)
    a = np.empty((k // 512, 16))
    for p in range(k // 512):
        a[p, :8] = np.random.permutation(np.resize(levels, 8))
        for g in range(8):
            far = levels[np.abs(levels - a[p, g]) >= 10]
            a[p, g + 8] = far[np.random.randint(len(far))]
    return np.exp2(a.ravel()).repeat(32)


def f64(x):
    return np.asarray(x).astype(np.float64)


def striped(idx):
    return np.tile(idx.reshape(-1, 16).T, (8, 1)).astype(np.uint16)


def unstriped(offs):
    return offs[:16].T.reshape(-1).astype(np.int64)


E2M1 = np.array([0.0, 0.5, 1.0, 1.5, 2.0, 3.0, 4.0, 6.0, -0.0, -0.5, -1.0, -1.5, -2.0, -3.0, -4.0, -6.0])


def pack_weight(w, fmt):
    k, n = w.shape
    w = f64(np.asarray(w, np.float32).astype(ml_dtypes.bfloat16)).reshape(k // 32, 32, n)
    amax = np.abs(w).max(1)
    if fmt == "e4m3":
        byte = np.frexp(amax)[1] - 1 + 127 - 7
    else:
        mant, ex = np.frexp(amax / 6.0)
        byte = np.where(mant > 0.5, ex, ex - 1) + 127
    byte = np.clip(np.where(amax > 0, byte, 1), 1, 254)
    scaled = (w * np.exp2(127.0 - byte)[:, None, :]).reshape(k, n).astype(np.float32)
    by_word = np.ascontiguousarray(scaled.reshape(k // 512, 128, 4, n).transpose(0, 1, 3, 2))
    if fmt == "e4m3":
        words = by_word.astype(ml_dtypes.float8_e4m3fn).view(np.uint8)
    else:
        c = by_word.astype(ml_dtypes.float4_e2m1fn).view(np.uint8) & 0xF
        words = (c[..., 0::2] | (c[..., 1::2] << 4)).reshape(k // 512, 128, 2 * n)
    return np.ascontiguousarray(words), np.ascontiguousarray(byte.astype(np.uint8).reshape(k // 512, 16, n))


def unpack_weight(words, scales, fmt):
    g, _, n = scales.shape
    words = np.ascontiguousarray(words).reshape(g, 128, n, -1)
    if fmt == "e4m3":
        vals = words.view(ml_dtypes.float8_e4m3fn).astype(np.float64)
    else:
        nib = np.empty((g, 128, n, 4), np.uint8)
        nib[..., 0::2] = words & 0xF
        nib[..., 1::2] = words >> 4
        vals = E2M1[nib]
    vals = vals * np.repeat(np.exp2(scales.astype(np.float64) - 127.0), 8, axis=1)[..., None]
    return vals.transpose(0, 1, 3, 2).reshape(g * 512, n)


def silu(v):
    return v / (1.0 + np.exp(-np.maximum(v, -700.0)))


K, T, E, C, H, N = 1536, 1024, 16, 128, 512, 128


def by_expert(wq, xq):
    return np.concatenate([wq[e].T @ xq[:, e * C:(e + 1) * C] for e in range(E)], axis=1)


def setup_inputs():
    n = np.random.standard_normal
    s = mx_kscale(K)
    u = mx_kscale(H)
    first = np.random.permutation(np.repeat(np.arange(E), T // E))
    second = (first + 1 + np.random.permutation(np.repeat(np.arange(E - 1), -(-T // (E - 1)))[:T])) % E
    while np.bincount(second, minlength=E).max() != T // E:
        load = np.bincount(second, minlength=E); hi, lo = int(load.argmax()), int(load.argmin())
        t = np.flatnonzero((second == hi) & (first != lo))[0]; second[t] = lo
    slot_token = np.empty(E * C, np.int64); pos = np.empty((2, T), np.int64); fill = np.zeros(E, np.int64)
    place = np.stack([np.random.permutation(C) for _ in range(E)])
    for r, deal in enumerate((first, second)):
        for t in np.random.permutation(T):
            e = deal[t]; j = e * C + place[e, fill[e]]; fill[e] += 1; slot_token[j] = t; pos[r, t] = j
    g = np.random.uniform(0.2, 0.8, T)
    x = pack_weight(n((K, T)) * s[:, None], "e4m3")
    w1 = pack_weight(n((K, H)) / np.sqrt(K) / s[:, None], "e2m1")
    w3 = pack_weight(n((K, H)) / np.sqrt(K) / s[:, None] * u, "e2m1")
    w2 = [pack_weight(m, "e2m1") for m in n((E, H, N)) / np.sqrt(H) / u[None, :, None]]
    return {
        "x_words": x[0],
        "x_scales": x[1],
        "w1_words": w1[0],
        "w1_scales": w1[1],
        "w3_words": w3[0],
        "w3_scales": w3[1],
        "w2_words": np.stack([m[0] for m in w2]),
        "w2_scales": np.stack([m[1] for m in w2]),
        "gate": np.stack([np.tile(g, (128, 1)), np.tile(1.0 - g, (128, 1))]).astype(np.float32),
        "offs": striped(slot_token),
        "pos1": striped(pos[0]),
        "pos2": striped(pos[1]),
    }


def reference(x_words, x_scales, w1_words, w1_scales, w3_words, w3_scales, w2_words, w2_scales, gate, offs, pos1, pos2):
    w1 = unpack_weight(w1_words, w1_scales, "e2m1")
    w3 = unpack_weight(w3_words, w3_scales, "e2m1")
    w2 = np.stack([unpack_weight(w2_words[e], w2_scales[e], "e2m1") for e in range(E)])
    idx = unstriped(offs)
    x = unpack_weight(x_words, x_scales, "e4m3")
    h = silu(w1.T @ x) * (w3.T @ x)
    y = by_expert(w2, mxq(h[:, idx], 0, "e4m3"))
    out = sum(f64(gate[r, :1]) * y[:, unstriped(p)] for r, p in enumerate((pos1, pos2)))
    return out

@@ -1,0 +1,223 @@
+from contextlib import ExitStack
+
+import concourse.mybir as mybir
+
+K, T, E, C, H, N = 1536, 1024, 16, 128, 512, 128
+FLOPS = 2 * (2 * K * H * T + H * N * E * C)
+
+F32 = mybir.dt.float32
+BF16 = mybir.dt.bfloat16
+I32 = mybir.dt.int32
+U32 = mybir.dt.uint32
+U16 = mybir.dt.uint16
+U8 = mybir.dt.uint8
+FP8X4 = mybir.dt.float8_e4m3fn_x4
+FP4X4 = mybir.dt.float4_e2m1fn_x4
+MULT = mybir.AluOpType.mult
+ADD = mybir.AluOpType.add
+SILU = mybir.ActivationFunctionType.Silu
+
+P = 128
+PASSES = K // 512
+HALF = 512
+SLOT_CHUNKS = (512, 512, 512, 512)
+TOKEN_CHUNKS = (512, 384, 128)
+
+
+def starts(widths):
+    return [sum(widths[:i]) for i in range(len(widths))]
+
+
+def load_scale_rows(queue, plane, rows):
+    for r in range(4):
+        queue.dma_start(out=plane[r:P:32, :, :].bitcast(I32), in_=rows[r])
+
+
+def tile_moe_sup_glu_silu_kernel(
+    tc, x_words, x_scales, w1_words, w1_scales, w3_words, w3_scales, w2_words, w2_scales, gate, offs, pos1, pos2, out
+):
+    nc = tc.nc
+    with ExitStack() as ctx:
+        keep = ctx.enter_context(tc.tile_pool(name="keep", bufs=1))
+        ring = ctx.enter_context(tc.tile_pool(name="ring", bufs=4))
+        psum = ctx.enter_context(tc.psum_pool(name="psum", bufs=8))
+
+        offs_sb = keep.tile([P, E * C // 16], U16, name="offs_sb")
+        pos_sb = [keep.tile([P, T // 16], U16, name="pos_sb%d" % r) for r in range(2)]
+
+        raw_scales = [
+            keep.tile([P, PASSES, H], U8, name="raw_scales%d" % m, tag="scale_stage%d" % m, align_bytes=64)
+            for m in range(2)
+        ]
+        x_plane = keep.tile([P, PASSES, T], U8, name="x_plane", align_bytes=64)
+        w2_plane = keep.tile([P, E, N], U8, name="w2_plane", align_bytes=64)
+        nc.vector.memset(raw_scales[0][:].bitcast(I32), 0)
+        nc.vector.memset(x_plane[:].bitcast(I32), 0)
+        nc.vector.memset(raw_scales[1][:].bitcast(I32), 0)
+        nc.vector.memset(w2_plane[:].bitcast(I32), 0)
+
+        raw_words = [
+            keep.tile([P, PASSES, H // 2], I32, name="raw_words%d" % m, tag="word_stage%d" % m, align_bytes=64)
+            for m in range(2)
+        ]
+        x_first = [keep.tile([P, HALF], I32, name="x_first%d" % s, align_bytes=64) for s in range(PASSES)]
+
+        x_view = x_words.rearrange("s p t d -> p s (t d)").bitcast(I32)
+        by_row = "a (q r) w -> r q a w"
+        load_scale_rows(nc.sync, raw_scales[0], w1_scales.bitcast(I32).rearrange(by_row, r=4))
+        load_scale_rows(nc.sync, x_plane, x_scales.bitcast(I32).rearrange(by_row, r=4))
+        nc.sync.dma_start(out=raw_words[0][:], in_=w1_words.bitcast(I32).rearrange("s p w -> p s w"))
+        for s in range(PASSES):
+            nc.sync.dma_start(out=x_first[s][:], in_=x_view[:, s, 0:HALF])
+        nc.sync.dma_start(out=raw_words[1][:], in_=w3_words.bitcast(I32).rearrange("s p w -> p s w"))
+        load_scale_rows(nc.sync, raw_scales[1], w3_scales.bitcast(I32).rearrange(by_row, r=4))
+
+        def x_pass(h, s):
+            return x_first[s][:] if h == 0 else x_second[:, s, :]
+
+        picked_words = {}
+        picked_plane = {}
+
+        def pick_plane(m, u):
+            plane = keep.tile([P, 2, PASSES * P], U8, name="plane%d_%d" % (m, u), align_bytes=64)
+            source = raw_scales[m][:].rearrange("p s c -> p (s c)").rearrange("p (b i j) -> p b j i", i=16, j=4)
+            nc.vector.tensor_copy(
+                out=plane[:].rearrange("p e (b i) -> p b e i", i=16), in_=source[:, :, 2 * u : 2 * u + 2, :]
+            )
+            picked_plane[(m, u)] = plane
+
+        def pick_words(m, u):
+            words = keep.tile([P, 2, PASSES * 2 * P], U8, name="words%d_%d" % (m, u), align_bytes=64)
+            flat = raw_words[m][:].bitcast(U16).rearrange("p s c -> p (s c)")
+            source = flat.rearrange("p (b i j) -> p b j i", i=8, j=4)
+            nc.vector.tensor_copy(
+                out=words[:].bitcast(U16).rearrange("p e (b i) -> p b e i", i=8),
+                in_=source[:, :, 2 * u : 2 * u + 2, :],
+            )
+            picked_words[(m, u)] = words
+
+        pick_words(0, 0)
+        pick_plane(0, 0)
+        pick_plane(0, 1)
+        x_second = keep.tile([P, PASSES, HALF], I32, name="x_second", tag="scale_stage0", align_bytes=64)
+        nc.sync.dma_start(out=x_second[:], in_=x_view[:, :, HALF:T])
+        pick_words(1, 0)
+        pick_plane(1, 0)
+
+        def first_layer(m, j, h):
+            words, plane = picked_words[(m, j // 2)], picked_plane[(m, j // 2)]
+            acc = psum.tile([P, HALF], F32, name="acc")
+            for s in range(PASSES):
+                nc.tensor.matmul_mx(
+                    out=acc[:],
+                    lhsT=words[:, j % 2, 2 * P * s : 2 * P * (s + 1)].bitcast(FP4X4),
+                    lhsT_scale=plane[:, j % 2, P * s : P * (s + 1)],
+                    rhs=x_pass(h, s).bitcast(FP8X4),
+                    rhs_scale=x_plane[:, s, h * HALF : (h + 1) * HALF],
+                    start=(s == 0),
+                    stop=(s == PASSES - 1),
+                )
+            return acc
+
+        pairs = [keep.tile([P, T, 2], BF16, name="pairs%d" % u, align_bytes=64) for u in range(2)]
+        gathered = {}
+
+        def gather(u, c):
+            a, n = starts(SLOT_CHUNKS)[c], SLOT_CHUNKS[c]
+            if u == 0:
+                gathered[c] = keep.tile([P, 2, n], U32, name="gathered%d" % c, tag="chunk%d" % c, align_bytes=64)
+            window = pairs[u][:].rearrange("p t e -> p (t e)").bitcast(U32)
+            nc.vector.tensor_copy(gathered[c][:, u, :], window.indirect(offs_sb[:, a // 16 : (a + n) // 16]))
+
+        def hidden(target, a_acc, b_acc, tag=None):
+            if tag is None:
+                act = ring.tile([P, HALF], F32, name="act")
+            else:
+                act = keep.tile([P, HALF], F32, name="act_" + tag, tag=tag, align_bytes=64)
+            nc.scalar.activation(act[:], a_acc[:], SILU)
+            nc.vector.tensor_tensor(target, b_acc[:], act[:], MULT)
+
+        a_accs = [first_layer(0, e, 0) for e in range(2)]
+        for e in range(2):
+            hidden(pairs[0][:, 0:HALF, e], a_accs[e], first_layer(1, e, 0))
+        pick_words(0, 1)
+        pick_words(1, 1)
+        pick_plane(1, 1)
+
+        w2_sb = keep.tile([P, E, N // 2], I32, name="w2_sb", tag="word_stage0", align_bytes=64)
+        gate_sb = [
+            keep.tile([P, T], F32, name="gate_sb%d" % r, tag=tag, align_bytes=64)
+            for r, tag in enumerate(("word_stage1", "scale_stage1"))
+        ]
+        nc.sync.dma_start(offs_sb[:], offs)
+        load_scale_rows(nc.sync, w2_plane, w2_scales.bitcast(I32).rearrange("e o (q r) w -> r q (e o) w", r=4))
+        nc.sync.dma_start(out=w2_sb[:], in_=w2_words.bitcast(I32).rearrange("e o p w -> p (e o) w"))
+        nc.sync.dma_start(pos_sb[0][:], pos1)
+        nc.sync.dma_start(pos_sb[1][:], pos2)
+        for r in range(2):
+            nc.sync.dma_start(out=gate_sb[r][:], in_=gate[r])
+
+        for e in range(2):
+            hidden(pairs[0][:, HALF:T, e], first_layer(0, e, 1), first_layer(1, e, 1))
+        gather(0, 0)
+        apart = keep.tile([P, 2, HALF], BF16, name="apart", align_bytes=64)
+        for e in range(2):
+            hidden(apart[:, e, :], first_layer(0, 2 + e, 0), first_layer(1, 2 + e, 0), tag="chunk%d" % (e + 1))
+            gather(0, e + 1)
+        nc.scalar.copy(pairs[1][:, 0:HALF, :], apart[:].rearrange("p e n -> p n e"))
+        gather(0, 3)
+        for e in range(2):
+            hidden(pairs[1][:, HALF:T, e], first_layer(0, 2 + e, 1), first_layer(1, 2 + e, 1))
+
+        woven = [keep.tile([P, n, 2], U32, name="woven%d" % c, align_bytes=64) for c, n in enumerate(SLOT_CHUNKS)]
+        for c in range(len(SLOT_CHUNKS)):
+            gather(1, c)
+            nc.scalar.copy(woven[c][:], gathered[c][:].rearrange("p u n -> p n u"))
+
+        y = keep.tile([P, E * C], F32, name="y")
+
+        def second_layer(c, first, n):
+            a = starts(SLOT_CHUNKS)[c] + first
+            codes = keep.tile([P, n], U32, name="codes%d" % a, align_bytes=64)
+            h_plane = keep.tile([P, n], U8, name="h_plane%d" % a, align_bytes=64)
+            nc.vector.quantize_mx(
+                out=codes[:].bitcast(FP8X4),
+                scales=h_plane[:],
+                in_=woven[c][:, first : first + n, :].rearrange("p n u -> p (n u)").bitcast(BF16),
+            )
+            acc = psum.tile([P, HALF], F32, name="acc")
+            for k in range(n // C):
+                e = a // C + k
+                nc.tensor.matmul_mx(
+                    out=acc[:, k * C : (k + 1) * C],
+                    lhsT=w2_sb[:, e, :].bitcast(FP4X4),
+                    lhsT_scale=w2_plane[:, e, :],
+                    rhs=codes[:, k * C : (k + 1) * C].bitcast(FP8X4),
+                    rhs_scale=h_plane[:, k * C : (k + 1) * C],
+                    start=True,
+                    stop=True,
+                )
+            nc.scalar.copy(y[:, a : a + n], acc[:, 0:n])
+
+        for c in range(3):
+            second_layer(c, 0, 512)
+        second_layer(3, 0, 256)
+        second_layer(3, 256, 128)
+        second_layer(3, 384, 128)
+
+        def weighted(r, c):
+            a, n = starts(TOKEN_CHUNKS)[c], TOKEN_CHUNKS[c]
+            share = keep.tile([P, n], F32, name="share%d_%d" % (r, c))
+            nc.vector.tensor_tensor(
+                share[:], y[:].indirect(pos_sb[r][:, a // 16 : (a + n) // 16]), gate_sb[r][:, a : a + n], MULT
+            )
+            return share
+
+        def combine(c, shares):
+            a, n = starts(TOKEN_CHUNKS)[c], TOKEN_CHUNKS[c]
+            total = keep.tile([P, n], F32, name="total%d" % c)
+            nc.vector.tensor_tensor(total[:], shares[0][:], shares[1][:], ADD)
+            nc.sync.dma_start(out=out[:, a : a + n], in_=total[:])
+
+        for c in range(len(TOKEN_CHUNKS)):
+            combine(c, [weighted(r, c) for r in range(2)])

@@ -20,7 +20,7 @@ SILU = mybir.ActivationFunctionType.Silu
 P = 128
 PASSES = K // 512
 HALF = 512
-SLOT_CHUNKS = (512, 512, 512, 512)
+SLOT_CHUNKS = (512, 256, 768, 512)
 TOKEN_CHUNKS = (512, 384, 128)
 
 
@@ -45,32 +45,38 @@ def tile_moe_sup_glu_silu_kernel(
         offs_sb = keep.tile([P, E * C // 16], U16, name="offs_sb")
         pos_sb = [keep.tile([P, T // 16], U16, name="pos_sb%d" % r) for r in range(2)]
 
-        raw_scales = [
-            keep.tile([P, PASSES, H], U8, name="raw_scales%d" % m, tag="scale_stage%d" % m, align_bytes=64)
-            for m in range(2)
-        ]
-        x_plane = keep.tile([P, PASSES, T], U8, name="x_plane", align_bytes=64)
+        raw_scales = [keep.tile([P, PASSES, H], U8, name="raw_scales%d" % m, align_bytes=64) for m in range(2)]
+        x_planes = [keep.tile([P, PASSES, HALF], U8, name="x_plane%d" % h, align_bytes=64) for h in range(2)]
         w2_plane = keep.tile([P, E, N], U8, name="w2_plane", align_bytes=64)
-        nc.vector.memset(raw_scales[0][:].bitcast(I32), 0)
-        nc.vector.memset(x_plane[:].bitcast(I32), 0)
-        nc.vector.memset(raw_scales[1][:].bitcast(I32), 0)
-        nc.vector.memset(w2_plane[:].bitcast(I32), 0)
+        for plane in (raw_scales[0], x_planes[0], raw_scales[1], x_planes[1], w2_plane):
+            nc.vector.memset(plane[:].bitcast(I32), 0)
 
-        raw_words = [
-            keep.tile([P, PASSES, H // 2], I32, name="raw_words%d" % m, tag="word_stage%d" % m, align_bytes=64)
-            for m in range(2)
-        ]
+        raw_words = [keep.tile([P, PASSES, H // 2], I32, name="raw_words%d" % m, align_bytes=64) for m in range(2)]
         x_first = [keep.tile([P, HALF], I32, name="x_first%d" % s, align_bytes=64) for s in range(PASSES)]
+        x_second = keep.tile([P, PASSES, HALF], I32, name="x_second", align_bytes=64)
+        w2_sb = keep.tile([P, E, N // 2], I32, name="w2_sb", align_bytes=64)
+        gate_sb = [keep.tile([P, T], F32, name="gate_sb%d" % r) for r in range(2)]
 
         x_view = x_words.rearrange("s p t d -> p s (t d)").bitcast(I32)
         by_row = "a (q r) w -> r q a w"
+        x_rows = x_scales.bitcast(I32).rearrange(by_row, r=4)
         load_scale_rows(nc.sync, raw_scales[0], w1_scales.bitcast(I32).rearrange(by_row, r=4))
-        load_scale_rows(nc.sync, x_plane, x_scales.bitcast(I32).rearrange(by_row, r=4))
+        load_scale_rows(nc.sync, x_planes[0], x_rows[:, :, :, 0 : HALF // 4])
         nc.sync.dma_start(out=raw_words[0][:], in_=w1_words.bitcast(I32).rearrange("s p w -> p s w"))
-        for s in range(PASSES):
+        nc.sync.dma_start(out=x_first[0][:], in_=x_view[:, 0, 0:HALF])
+        nc.sync.dma_start(offs_sb[:], offs)
+        nc.sync.dma_start(pos_sb[0][:], pos1)
+        for s in range(1, PASSES):
             nc.sync.dma_start(out=x_first[s][:], in_=x_view[:, s, 0:HALF])
         nc.sync.dma_start(out=raw_words[1][:], in_=w3_words.bitcast(I32).rearrange("s p w -> p s w"))
         load_scale_rows(nc.sync, raw_scales[1], w3_scales.bitcast(I32).rearrange(by_row, r=4))
+        nc.sync.dma_start(out=x_second[:], in_=x_view[:, :, HALF:T])
+        load_scale_rows(nc.sync, x_planes[1], x_rows[:, :, :, HALF // 4 : T // 4])
+        load_scale_rows(nc.sync, w2_plane, w2_scales.bitcast(I32).rearrange("e o (q r) w -> r q (e o) w", r=4))
+        nc.sync.dma_start(out=w2_sb[:], in_=w2_words.bitcast(I32).rearrange("e o p w -> p (e o) w"))
+        nc.sync.dma_start(pos_sb[1][:], pos2)
+        for r in range(2):
+            nc.sync.dma_start(out=gate_sb[r][:], in_=gate[r])
 
         def x_pass(h, s):
             return x_first[s][:] if h == 0 else x_second[:, s, :]
@@ -96,27 +102,26 @@ def tile_moe_sup_glu_silu_kernel(
             )
             picked_words[(m, u)] = words
 
-        pick_words(0, 0)
-        pick_plane(0, 0)
-        pick_plane(0, 1)
-        x_second = keep.tile([P, PASSES, HALF], I32, name="x_second", tag="scale_stage0", align_bytes=64)
-        nc.sync.dma_start(out=x_second[:], in_=x_view[:, :, HALF:T])
-        pick_words(1, 0)
-        pick_plane(1, 0)
+        for m in range(2):
+            pick_words(m, 0)
+            pick_plane(m, 0)
+
+        def first_layer_pass(acc, m, j, h, s):
+            words, plane = picked_words[(m, j // 2)], picked_plane[(m, j // 2)]
+            nc.tensor.matmul_mx(
+                out=acc[:],
+                lhsT=words[:, j % 2, 2 * P * s : 2 * P * (s + 1)].bitcast(FP4X4),
+                lhsT_scale=plane[:, j % 2, P * s : P * (s + 1)],
+                rhs=x_pass(h, s).bitcast(FP8X4),
+                rhs_scale=x_planes[h][:, s, :],
+                start=(s == 0),
+                stop=(s == PASSES - 1),
+            )
 
         def first_layer(m, j, h):
-            words, plane = picked_words[(m, j // 2)], picked_plane[(m, j // 2)]
             acc = psum.tile([P, HALF], F32, name="acc")
             for s in range(PASSES):
-                nc.tensor.matmul_mx(
-                    out=acc[:],
-                    lhsT=words[:, j % 2, 2 * P * s : 2 * P * (s + 1)].bitcast(FP4X4),
-                    lhsT_scale=plane[:, j % 2, P * s : P * (s + 1)],
-                    rhs=x_pass(h, s).bitcast(FP8X4),
-                    rhs_scale=x_plane[:, s, h * HALF : (h + 1) * HALF],
-                    start=(s == 0),
-                    stop=(s == PASSES - 1),
-                )
+                first_layer_pass(acc, m, j, h, s)
             return acc
 
         pairs = [keep.tile([P, T, 2], BF16, name="pairs%d" % u, align_bytes=64) for u in range(2)]
@@ -137,37 +142,28 @@ def tile_moe_sup_glu_silu_kernel(
             nc.scalar.activation(act[:], a_acc[:], SILU)
             nc.vector.tensor_tensor(target, b_acc[:], act[:], MULT)
 
-        a_accs = [first_layer(0, e, 0) for e in range(2)]
+        a_accs = [psum.tile([P, HALF], F32, name="acc") for e in range(2)]
+        for s in range(PASSES):
+            for e in range(2):
+                first_layer_pass(a_accs[e], 0, e, 0, s)
         for e in range(2):
             hidden(pairs[0][:, 0:HALF, e], a_accs[e], first_layer(1, e, 0))
-        pick_words(0, 1)
-        pick_words(1, 1)
-        pick_plane(1, 1)
-
-        w2_sb = keep.tile([P, E, N // 2], I32, name="w2_sb", tag="word_stage0", align_bytes=64)
-        gate_sb = [
-            keep.tile([P, T], F32, name="gate_sb%d" % r, tag=tag, align_bytes=64)
-            for r, tag in enumerate(("word_stage1", "scale_stage1"))
-        ]
-        nc.sync.dma_start(offs_sb[:], offs)
-        load_scale_rows(nc.sync, w2_plane, w2_scales.bitcast(I32).rearrange("e o (q r) w -> r q (e o) w", r=4))
-        nc.sync.dma_start(out=w2_sb[:], in_=w2_words.bitcast(I32).rearrange("e o p w -> p (e o) w"))
-        nc.sync.dma_start(pos_sb[0][:], pos1)
-        nc.sync.dma_start(pos_sb[1][:], pos2)
-        for r in range(2):
-            nc.sync.dma_start(out=gate_sb[r][:], in_=gate[r])
-
+        for m in range(2):
+            pick_words(m, 1)
+            pick_plane(m, 1)
         for e in range(2):
             hidden(pairs[0][:, HALF:T, e], first_layer(0, e, 1), first_layer(1, e, 1))
         gather(0, 0)
-        apart = keep.tile([P, 2, HALF], BF16, name="apart", align_bytes=64)
-        for e in range(2):
-            hidden(apart[:, e, :], first_layer(0, 2 + e, 0), first_layer(1, 2 + e, 0), tag="chunk%d" % (e + 1))
-            gather(0, e + 1)
-        nc.scalar.copy(pairs[1][:, 0:HALF, :], apart[:].rearrange("p e n -> p n e"))
-        gather(0, 3)
-        for e in range(2):
-            hidden(pairs[1][:, HALF:T, e], first_layer(0, 2 + e, 1), first_layer(1, 2 + e, 1))
+        held_behind = {(0, 0): 1, (0, 1): 2, (1, 1): 3}
+        for h in range(2):
+            apart = keep.tile([P, 2, HALF], BF16, name="apart%d" % h, align_bytes=64)
+            for e in range(2):
+                c = held_behind.get((h, e))
+                tag = None if c is None else "chunk%d" % c
+                hidden(apart[:, e, :], first_layer(0, 2 + e, h), first_layer(1, 2 + e, h), tag=tag)
+                if c is not None:
+                    gather(0, c)
+            nc.scalar.copy(pairs[1][:, h * HALF : (h + 1) * HALF, :], apart[:].rearrange("p e n -> p n e"))
 
         woven = [keep.tile([P, n, 2], U32, name="woven%d" % c, align_bytes=64) for c, n in enumerate(SLOT_CHUNKS)]
         for c in range(len(SLOT_CHUNKS)):
@@ -199,8 +195,10 @@ def tile_moe_sup_glu_silu_kernel(
                 )
             nc.scalar.copy(y[:, a : a + n], acc[:, 0:n])
 
-        for c in range(3):
-            second_layer(c, 0, 512)
+        second_layer(0, 0, 512)
+        second_layer(1, 0, 256)
+        second_layer(2, 0, 512)
+        second_layer(2, 512, 256)
         second_layer(3, 0, 256)
         second_layer(3, 256, 128)
         second_layer(3, 384, 128)
@@ -219,5 +217,9 @@ def tile_moe_sup_glu_silu_kernel(
             nc.vector.tensor_tensor(total[:], shares[0][:], shares[1][:], ADD)
             nc.sync.dma_start(out=out[:, a : a + n], in_=total[:])
 
+        first_share = weighted(0, 0)
         for c in range(len(TOKEN_CHUNKS)):
-            combine(c, [weighted(r, c) for r in range(2)])
+            shares = [first_share, weighted(1, c)]
+            if c + 1 < len(TOKEN_CHUNKS):
+                first_share = weighted(0, c + 1)
+            combine(c, shares)

@@ -20,6 +20,7 @@ SILU = mybir.ActivationFunctionType.Silu
 P = 128
 PASSES = K // 512
 HALF = 512
+WARM_PASSES = 16
 SLOT_CHUNKS = (512, 256, 768, 512)
 TOKEN_CHUNKS = (512, 384, 128)
 
@@ -28,9 +29,9 @@ def starts(widths):
     return [sum(widths[:i]) for i in range(len(widths))]
 
 
-def load_scale_rows(queue, plane, rows):
+def load_scale_rows(queues, plane, rows):
     for r in range(4):
-        queue.dma_start(out=plane[r:P:32, :, :].bitcast(I32), in_=rows[r])
+        queues[r].dma_start(out=plane[r:P:32, :, :].bitcast(I32), in_=rows[r])
 
 
 def tile_moe_sup_glu_silu_kernel(
@@ -52,34 +53,46 @@ def tile_moe_sup_glu_silu_kernel(
             nc.vector.memset(plane[:].bitcast(I32), 0)
 
         raw_words = [keep.tile([P, PASSES, H // 2], I32, name="raw_words%d" % m, align_bytes=64) for m in range(2)]
-        x_first = [keep.tile([P, HALF], I32, name="x_first%d" % s, align_bytes=64) for s in range(PASSES)]
-        x_second = keep.tile([P, PASSES, HALF], I32, name="x_second", align_bytes=64)
+        x_sb = [keep.tile([P, PASSES, HALF], I32, name="x_sb%d" % h, align_bytes=64) for h in range(2)]
         w2_sb = keep.tile([P, E, N // 2], I32, name="w2_sb", align_bytes=64)
         gate_sb = [keep.tile([P, T], F32, name="gate_sb%d" % r) for r in range(2)]
 
         x_view = x_words.rearrange("s p t d -> p s (t d)").bitcast(I32)
         by_row = "a (q r) w -> r q a w"
         x_rows = x_scales.bitcast(I32).rearrange(by_row, r=4)
-        load_scale_rows(nc.sync, raw_scales[0], w1_scales.bitcast(I32).rearrange(by_row, r=4))
-        load_scale_rows(nc.sync, x_planes[0], x_rows[:, :, :, 0 : HALF // 4])
+        on_sync = [nc.sync] * 4
+        load_scale_rows(on_sync, raw_scales[0], w1_scales.bitcast(I32).rearrange(by_row, r=4))
+        load_scale_rows([nc.sync] * 3 + [nc.gpsimd], x_planes[0], x_rows[:, :, :, 0 : HALF // 4])
         nc.sync.dma_start(out=raw_words[0][:], in_=w1_words.bitcast(I32).rearrange("s p w -> p s w"))
-        nc.sync.dma_start(out=x_first[0][:], in_=x_view[:, 0, 0:HALF])
-        nc.sync.dma_start(offs_sb[:], offs)
-        nc.sync.dma_start(pos_sb[0][:], pos1)
-        for s in range(1, PASSES):
-            nc.sync.dma_start(out=x_first[s][:], in_=x_view[:, s, 0:HALF])
+        nc.sync.dma_start(out=x_sb[0][:], in_=x_view[:, :, 0:HALF])
         nc.sync.dma_start(out=raw_words[1][:], in_=w3_words.bitcast(I32).rearrange("s p w -> p s w"))
-        load_scale_rows(nc.sync, raw_scales[1], w3_scales.bitcast(I32).rearrange(by_row, r=4))
-        nc.sync.dma_start(out=x_second[:], in_=x_view[:, :, HALF:T])
-        load_scale_rows(nc.sync, x_planes[1], x_rows[:, :, :, HALF // 4 : T // 4])
-        load_scale_rows(nc.sync, w2_plane, w2_scales.bitcast(I32).rearrange("e o (q r) w -> r q (e o) w", r=4))
+        load_scale_rows(on_sync, raw_scales[1], w3_scales.bitcast(I32).rearrange(by_row, r=4))
+        nc.sync.dma_start(out=x_sb[1][:], in_=x_view[:, :, HALF:T])
+        load_scale_rows(on_sync, x_planes[1], x_rows[:, :, :, HALF // 4 : T // 4])
+        nc.sync.dma_start(offs_sb[:], offs)
+        load_scale_rows(on_sync, w2_plane, w2_scales.bitcast(I32).rearrange("e o (q r) w -> r q (e o) w", r=4))
         nc.sync.dma_start(out=w2_sb[:], in_=w2_words.bitcast(I32).rearrange("e o p w -> p (e o) w"))
+        nc.sync.dma_start(pos_sb[0][:], pos1)
         nc.sync.dma_start(pos_sb[1][:], pos2)
         for r in range(2):
             nc.sync.dma_start(out=gate_sb[r][:], in_=gate[r])
 
-        def x_pass(h, s):
-            return x_first[s][:] if h == 0 else x_second[:, s, :]
+        zeros = keep.tile([P, 4 * P], BF16, name="zeros", align_bytes=64)
+        warm_codes = keep.tile([P, P], U32, name="warm_codes", align_bytes=64)
+        warm_plane = keep.tile([P, P], U8, name="warm_plane", align_bytes=64)
+        nc.vector.memset(zeros[:], 0.0)
+        nc.vector.quantize_mx(out=warm_codes[:].bitcast(FP8X4), scales=warm_plane[:], in_=zeros[:])
+        warm_acc = psum.tile([P, HALF], F32, name="acc")
+        for k in range(WARM_PASSES):
+            nc.tensor.matmul_mx(
+                out=warm_acc[:, (k % 4) * P : (k % 4 + 1) * P],
+                lhsT=raw_words[0][:, 0, 0 : P // 2].bitcast(FP4X4),
+                lhsT_scale=warm_plane[:],
+                rhs=warm_codes[:].bitcast(FP8X4),
+                rhs_scale=warm_plane[:],
+                start=True,
+                stop=True,
+            )
 
         picked_words = {}
         picked_plane = {}
@@ -112,7 +125,7 @@ def tile_moe_sup_glu_silu_kernel(
                 out=acc[:],
                 lhsT=words[:, j % 2, 2 * P * s : 2 * P * (s + 1)].bitcast(FP4X4),
                 lhsT_scale=plane[:, j % 2, P * s : P * (s + 1)],
-                rhs=x_pass(h, s).bitcast(FP8X4),
+                rhs=x_sb[h][:, s, :].bitcast(FP8X4),
                 rhs_scale=x_planes[h][:, s, :],
                 start=(s == 0),
                 stop=(s == PASSES - 1),
@@ -142,10 +155,7 @@ def tile_moe_sup_glu_silu_kernel(
             nc.scalar.activation(act[:], a_acc[:], SILU)
             nc.vector.tensor_tensor(target, b_acc[:], act[:], MULT)
 
-        a_accs = [psum.tile([P, HALF], F32, name="acc") for e in range(2)]
-        for s in range(PASSES):
-            for e in range(2):
-                first_layer_pass(a_accs[e], 0, e, 0, s)
+        a_accs = [first_layer(0, e, 0) for e in range(2)]
         for e in range(2):
             hidden(pairs[0][:, 0:HALF, e], a_accs[e], first_layer(1, e, 0))
         for m in range(2):

@@ -29,8 +29,8 @@ def starts(widths):
     return [sum(widths[:i]) for i in range(len(widths))]
 
 
-def load_scale_rows(queues, plane, rows):
-    for r in range(4):
+def load_scale_rows(queues, plane, rows, which=range(4)):
+    for r in which:
         queues[r].dma_start(out=plane[r:P:32, :, :].bitcast(I32), in_=rows[r])
 
 
@@ -53,7 +53,9 @@ def tile_moe_sup_glu_silu_kernel(
             nc.vector.memset(plane[:].bitcast(I32), 0)
 
         raw_words = [keep.tile([P, PASSES, H // 2], I32, name="raw_words%d" % m, align_bytes=64) for m in range(2)]
-        x_sb = [keep.tile([P, PASSES, HALF], I32, name="x_sb%d" % h, align_bytes=64) for h in range(2)]
+        x_head = keep.tile([P, HALF], I32, name="x_head", align_bytes=64)
+        x_rest = keep.tile([P, PASSES - 1, HALF], I32, name="x_rest", align_bytes=64)
+        x_second = keep.tile([P, PASSES, HALF], I32, name="x_second", align_bytes=64)
         w2_sb = keep.tile([P, E, N // 2], I32, name="w2_sb", align_bytes=64)
         gate_sb = [keep.tile([P, T], F32, name="gate_sb%d" % r) for r in range(2)]
 
@@ -62,12 +64,15 @@ def tile_moe_sup_glu_silu_kernel(
         x_rows = x_scales.bitcast(I32).rearrange(by_row, r=4)
         on_sync = [nc.sync] * 4
         load_scale_rows(on_sync, raw_scales[0], w1_scales.bitcast(I32).rearrange(by_row, r=4))
-        load_scale_rows([nc.sync] * 3 + [nc.gpsimd], x_planes[0], x_rows[:, :, :, 0 : HALF // 4])
+        first_rows = x_rows[:, :, :, 0 : HALF // 4]
+        load_scale_rows([nc.sync] * 3 + [nc.gpsimd], x_planes[0], first_rows, (0, 1, 3))
         nc.sync.dma_start(out=raw_words[0][:], in_=w1_words.bitcast(I32).rearrange("s p w -> p s w"))
-        nc.sync.dma_start(out=x_sb[0][:], in_=x_view[:, :, 0:HALF])
+        nc.sync.dma_start(out=x_head[:], in_=x_view[:, 0, 0:HALF])
+        nc.sync.dma_start(out=x_rest[:], in_=x_view[:, 1:PASSES, 0:HALF])
+        load_scale_rows(on_sync, x_planes[0], first_rows, (2,))
         nc.sync.dma_start(out=raw_words[1][:], in_=w3_words.bitcast(I32).rearrange("s p w -> p s w"))
         load_scale_rows(on_sync, raw_scales[1], w3_scales.bitcast(I32).rearrange(by_row, r=4))
-        nc.sync.dma_start(out=x_sb[1][:], in_=x_view[:, :, HALF:T])
+        nc.sync.dma_start(out=x_second[:], in_=x_view[:, :, HALF:T])
         load_scale_rows(on_sync, x_planes[1], x_rows[:, :, :, HALF // 4 : T // 4])
         nc.sync.dma_start(offs_sb[:], offs)
         load_scale_rows(on_sync, w2_plane, w2_scales.bitcast(I32).rearrange("e o (q r) w -> r q (e o) w", r=4))
@@ -76,6 +81,11 @@ def tile_moe_sup_glu_silu_kernel(
         nc.sync.dma_start(pos_sb[1][:], pos2)
         for r in range(2):
             nc.sync.dma_start(out=gate_sb[r][:], in_=gate[r])
+
+        def x_pass(h, s):
+            if h == 1:
+                return x_second[:, s, :]
+            return x_head[:] if s == 0 else x_rest[:, s - 1, :]
 
         zeros = keep.tile([P, 4 * P], BF16, name="zeros", align_bytes=64)
         warm_codes = keep.tile([P, P], U32, name="warm_codes", align_bytes=64)
@@ -97,35 +107,37 @@ def tile_moe_sup_glu_silu_kernel(
         picked_words = {}
         picked_plane = {}
 
-        def pick_plane(m, u):
-            plane = keep.tile([P, 2, PASSES * P], U8, name="plane%d_%d" % (m, u), align_bytes=64)
+        def pick_plane(m, first, count):
+            plane = keep.tile([P, count, PASSES * P], U8, name="plane%d_%d" % (m, first), align_bytes=64)
             source = raw_scales[m][:].rearrange("p s c -> p (s c)").rearrange("p (b i j) -> p b j i", i=16, j=4)
             nc.vector.tensor_copy(
-                out=plane[:].rearrange("p e (b i) -> p b e i", i=16), in_=source[:, :, 2 * u : 2 * u + 2, :]
+                out=plane[:].rearrange("p e (b i) -> p b e i", i=16), in_=source[:, :, first : first + count, :]
             )
-            picked_plane[(m, u)] = plane
+            for e in range(count):
+                picked_plane[(m, first + e)] = plane[:, e, :]
 
-        def pick_words(m, u):
-            words = keep.tile([P, 2, PASSES * 2 * P], U8, name="words%d_%d" % (m, u), align_bytes=64)
+        def pick_words(m, first, count):
+            words = keep.tile([P, count, PASSES * 2 * P], U8, name="words%d_%d" % (m, first), align_bytes=64)
             flat = raw_words[m][:].bitcast(U16).rearrange("p s c -> p (s c)")
             source = flat.rearrange("p (b i j) -> p b j i", i=8, j=4)
             nc.vector.tensor_copy(
                 out=words[:].bitcast(U16).rearrange("p e (b i) -> p b e i", i=8),
-                in_=source[:, :, 2 * u : 2 * u + 2, :],
+                in_=source[:, :, first : first + count, :],
             )
-            picked_words[(m, u)] = words
+            for e in range(count):
+                picked_words[(m, first + e)] = words[:, e, :]
 
-        for m in range(2):
-            pick_words(m, 0)
-            pick_plane(m, 0)
+        for m, first, count in ((0, 0, 2), (1, 0, 1), (1, 1, 1)):
+            pick_words(m, first, count)
+            pick_plane(m, first, count)
 
         def first_layer_pass(acc, m, j, h, s):
-            words, plane = picked_words[(m, j // 2)], picked_plane[(m, j // 2)]
+            words, plane = picked_words[(m, j)], picked_plane[(m, j)]
             nc.tensor.matmul_mx(
                 out=acc[:],
-                lhsT=words[:, j % 2, 2 * P * s : 2 * P * (s + 1)].bitcast(FP4X4),
-                lhsT_scale=plane[:, j % 2, P * s : P * (s + 1)],
-                rhs=x_sb[h][:, s, :].bitcast(FP8X4),
+                lhsT=words[:, 2 * P * s : 2 * P * (s + 1)].bitcast(FP4X4),
+                lhsT_scale=plane[:, P * s : P * (s + 1)],
+                rhs=x_pass(h, s).bitcast(FP8X4),
                 rhs_scale=x_planes[h][:, s, :],
                 start=(s == 0),
                 stop=(s == PASSES - 1),
@@ -140,12 +152,15 @@ def tile_moe_sup_glu_silu_kernel(
         pairs = [keep.tile([P, T, 2], BF16, name="pairs%d" % u, align_bytes=64) for u in range(2)]
         gathered = {}
 
-        def gather(u, c):
-            a, n = starts(SLOT_CHUNKS)[c], SLOT_CHUNKS[c]
+        def gather(u, c, first=0, count=None):
+            n = SLOT_CHUNKS[c] if count is None else count
+            a = starts(SLOT_CHUNKS)[c] + first
             if u == 0:
                 gathered[c] = keep.tile([P, 2, n], U32, name="gathered%d" % c, tag="chunk%d" % c, align_bytes=64)
             window = pairs[u][:].rearrange("p t e -> p (t e)").bitcast(U32)
-            nc.vector.tensor_copy(gathered[c][:, u, :], window.indirect(offs_sb[:, a // 16 : (a + n) // 16]))
+            nc.vector.tensor_copy(
+                gathered[c][:, u, first : first + n], window.indirect(offs_sb[:, a // 16 : (a + n) // 16])
+            )
 
         def hidden(target, a_acc, b_acc, tag=None):
             if tag is None:
@@ -159,8 +174,8 @@ def tile_moe_sup_glu_silu_kernel(
         for e in range(2):
             hidden(pairs[0][:, 0:HALF, e], a_accs[e], first_layer(1, e, 0))
         for m in range(2):
-            pick_words(m, 1)
-            pick_plane(m, 1)
+            pick_words(m, 2, 2)
+            pick_plane(m, 2, 2)
         for e in range(2):
             hidden(pairs[0][:, HALF:T, e], first_layer(0, e, 1), first_layer(1, e, 1))
         gather(0, 0)
@@ -176,9 +191,11 @@ def tile_moe_sup_glu_silu_kernel(
             nc.scalar.copy(pairs[1][:, h * HALF : (h + 1) * HALF, :], apart[:].rearrange("p e n -> p n e"))
 
         woven = [keep.tile([P, n, 2], U32, name="woven%d" % c, align_bytes=64) for c, n in enumerate(SLOT_CHUNKS)]
-        for c in range(len(SLOT_CHUNKS)):
-            gather(1, c)
-            nc.scalar.copy(woven[c][:], gathered[c][:].rearrange("p u n -> p n u"))
+        for c, first, n in ((1, 0, 256), (0, 0, 512), (2, 0, 768), (3, 0, 256), (3, 256, 256)):
+            gather(1, c, first, n)
+            nc.scalar.copy(
+                woven[c][:, first : first + n, :], gathered[c][:, :, first : first + n].rearrange("p u n -> p n u")
+            )
 
         y = keep.tile([P, E * C], F32, name="y")
 
@@ -203,10 +220,13 @@ def tile_moe_sup_glu_silu_kernel(
                     start=True,
                     stop=True,
                 )
-            nc.scalar.copy(y[:, a : a + n], acc[:, 0:n])
+            if c == len(SLOT_CHUNKS) - 1:
+                nc.vector.tensor_copy(y[:, a : a + n], acc[:, 0:n])
+            else:
+                nc.scalar.copy(y[:, a : a + n], acc[:, 0:n])
 
-        second_layer(0, 0, 512)
         second_layer(1, 0, 256)
+        second_layer(0, 0, 512)
         second_layer(2, 0, 512)
         second_layer(2, 512, 256)
         second_layer(3, 0, 256)

@@ -20,7 +20,6 @@ SILU = mybir.ActivationFunctionType.Silu
 P = 128
 PASSES = K // 512
 HALF = 512
-WARM_PASSES = 16
 SLOT_CHUNKS = (512, 256, 768, 512)
 TOKEN_CHUNKS = (512, 384, 128)
 
@@ -86,23 +85,6 @@ def tile_moe_sup_glu_silu_kernel(
             if h == 1:
                 return x_second[:, s, :]
             return x_head[:] if s == 0 else x_rest[:, s - 1, :]
-
-        zeros = keep.tile([P, 4 * P], BF16, name="zeros", align_bytes=64)
-        warm_codes = keep.tile([P, P], U32, name="warm_codes", align_bytes=64)
-        warm_plane = keep.tile([P, P], U8, name="warm_plane", align_bytes=64)
-        nc.vector.memset(zeros[:], 0.0)
-        nc.vector.quantize_mx(out=warm_codes[:].bitcast(FP8X4), scales=warm_plane[:], in_=zeros[:])
-        warm_acc = psum.tile([P, HALF], F32, name="acc")
-        for k in range(WARM_PASSES):
-            nc.tensor.matmul_mx(
-                out=warm_acc[:, (k % 4) * P : (k % 4 + 1) * P],
-                lhsT=raw_words[0][:, 0, 0 : P // 2].bitcast(FP4X4),
-                lhsT_scale=warm_plane[:],
-                rhs=warm_codes[:].bitcast(FP8X4),
-                rhs_scale=warm_plane[:],
-                start=True,
-                stop=True,
-            )
 
         picked_words = {}
         picked_plane = {}

@@ -20,8 +20,9 @@ SILU = mybir.ActivationFunctionType.Silu
 P = 128
 PASSES = K // 512
 HALF = 512
-SLOT_CHUNKS = (512, 256, 768, 512)
-TOKEN_CHUNKS = (512, 384, 128)
+WARM_PASSES = 3
+SLOTS = E * C
+TOKEN_CHUNKS = (768, 128, 128)
 
 
 def starts(widths):
@@ -52,9 +53,7 @@ def tile_moe_sup_glu_silu_kernel(
             nc.vector.memset(plane[:].bitcast(I32), 0)
 
         raw_words = [keep.tile([P, PASSES, H // 2], I32, name="raw_words%d" % m, align_bytes=64) for m in range(2)]
-        x_head = keep.tile([P, HALF], I32, name="x_head", align_bytes=64)
-        x_rest = keep.tile([P, PASSES - 1, HALF], I32, name="x_rest", align_bytes=64)
-        x_second = keep.tile([P, PASSES, HALF], I32, name="x_second", align_bytes=64)
+        x_halves = [keep.tile([P, PASSES, HALF], I32, name="x_half%d" % h, align_bytes=64) for h in range(2)]
         w2_sb = keep.tile([P, E, N // 2], I32, name="w2_sb", align_bytes=64)
         gate_sb = [keep.tile([P, T], F32, name="gate_sb%d" % r) for r in range(2)]
 
@@ -62,16 +61,16 @@ def tile_moe_sup_glu_silu_kernel(
         by_row = "a (q r) w -> r q a w"
         x_rows = x_scales.bitcast(I32).rearrange(by_row, r=4)
         on_sync = [nc.sync] * 4
-        load_scale_rows(on_sync, raw_scales[0], w1_scales.bitcast(I32).rearrange(by_row, r=4))
         first_rows = x_rows[:, :, :, 0 : HALF // 4]
-        load_scale_rows([nc.sync] * 3 + [nc.gpsimd], x_planes[0], first_rows, (0, 1, 3))
         nc.sync.dma_start(out=raw_words[0][:], in_=w1_words.bitcast(I32).rearrange("s p w -> p s w"))
-        nc.sync.dma_start(out=x_head[:], in_=x_view[:, 0, 0:HALF])
-        nc.sync.dma_start(out=x_rest[:], in_=x_view[:, 1:PASSES, 0:HALF])
-        load_scale_rows(on_sync, x_planes[0], first_rows, (2,))
+        nc.sync.dma_start(out=x_halves[0][:, :, 0:P], in_=x_view[:, :, 0:P])
+        load_scale_rows(on_sync, raw_scales[0], w1_scales.bitcast(I32).rearrange(by_row, r=4))
+        load_scale_rows([nc.sync] * 3 + [nc.gpsimd], x_planes[0], first_rows, (0, 3))
+        nc.sync.dma_start(out=x_halves[0][:, :, P:HALF], in_=x_view[:, :, P:HALF])
+        load_scale_rows(on_sync, x_planes[0], first_rows, (1, 2))
         nc.sync.dma_start(out=raw_words[1][:], in_=w3_words.bitcast(I32).rearrange("s p w -> p s w"))
         load_scale_rows(on_sync, raw_scales[1], w3_scales.bitcast(I32).rearrange(by_row, r=4))
-        nc.sync.dma_start(out=x_second[:], in_=x_view[:, :, HALF:T])
+        nc.sync.dma_start(out=x_halves[1][:], in_=x_view[:, :, HALF:T])
         load_scale_rows(on_sync, x_planes[1], x_rows[:, :, :, HALF // 4 : T // 4])
         nc.sync.dma_start(offs_sb[:], offs)
         load_scale_rows(on_sync, w2_plane, w2_scales.bitcast(I32).rearrange("e o (q r) w -> r q (e o) w", r=4))
@@ -81,10 +80,17 @@ def tile_moe_sup_glu_silu_kernel(
         for r in range(2):
             nc.sync.dma_start(out=gate_sb[r][:], in_=gate[r])
 
-        def x_pass(h, s):
-            if h == 1:
-                return x_second[:, s, :]
-            return x_head[:] if s == 0 else x_rest[:, s - 1, :]
+        warm_acc = psum.tile([P, HALF], F32, name="acc")
+        for k in range(WARM_PASSES):
+            nc.tensor.matmul_mx(
+                out=warm_acc[:],
+                lhsT=x_halves[0][:, 0, 0:P].bitcast(FP8X4),
+                lhsT_scale=raw_scales[0][:, 0, 0:P],
+                rhs=raw_words[0][:, 0, :].bitcast(FP4X4),
+                rhs_scale=raw_scales[0][:, 0, :],
+                start=True,
+                stop=True,
+            )
 
         picked_words = {}
         picked_plane = {}
@@ -109,9 +115,10 @@ def tile_moe_sup_glu_silu_kernel(
             for e in range(count):
                 picked_words[(m, first + e)] = words[:, e, :]
 
-        for m, first, count in ((0, 0, 2), (1, 0, 1), (1, 1, 1)):
-            pick_words(m, first, count)
-            pick_plane(m, first, count)
+        for m in range(2):
+            pick_words(m, 0, 2)
+            pick_plane(m, 0, 1)
+            pick_plane(m, 1, 1)
 
         def first_layer_pass(acc, m, j, h, s):
             words, plane = picked_words[(m, j)], picked_plane[(m, j)]
@@ -119,7 +126,7 @@ def tile_moe_sup_glu_silu_kernel(
                 out=acc[:],
                 lhsT=words[:, 2 * P * s : 2 * P * (s + 1)].bitcast(FP4X4),
                 lhsT_scale=plane[:, P * s : P * (s + 1)],
-                rhs=x_pass(h, s).bitcast(FP8X4),
+                rhs=x_halves[h][:, s, :].bitcast(FP8X4),
                 rhs_scale=x_planes[h][:, s, :],
                 start=(s == 0),
                 stop=(s == PASSES - 1),
@@ -132,64 +139,51 @@ def tile_moe_sup_glu_silu_kernel(
             return acc
 
         pairs = [keep.tile([P, T, 2], BF16, name="pairs%d" % u, align_bytes=64) for u in range(2)]
-        gathered = {}
+        gathered = keep.tile([P, 2 * SLOTS], U32, name="gathered", align_bytes=64)
 
-        def gather(u, c, first=0, count=None):
-            n = SLOT_CHUNKS[c] if count is None else count
-            a = starts(SLOT_CHUNKS)[c] + first
-            if u == 0:
-                gathered[c] = keep.tile([P, 2, n], U32, name="gathered%d" % c, tag="chunk%d" % c, align_bytes=64)
+        def gather(u, a, n):
             window = pairs[u][:].rearrange("p t e -> p (t e)").bitcast(U32)
             nc.vector.tensor_copy(
-                gathered[c][:, u, first : first + n], window.indirect(offs_sb[:, a // 16 : (a + n) // 16])
+                gathered[:, u * SLOTS + a : u * SLOTS + a + n], window.indirect(offs_sb[:, a // 16 : (a + n) // 16])
             )
 
-        def hidden(target, a_acc, b_acc, tag=None):
-            if tag is None:
-                act = ring.tile([P, HALF], F32, name="act")
-            else:
-                act = keep.tile([P, HALF], F32, name="act_" + tag, tag=tag, align_bytes=64)
-            nc.scalar.activation(act[:], a_acc[:], SILU)
-            nc.vector.tensor_tensor(target, b_acc[:], act[:], MULT)
+        def hidden(target, a_acc, b_acc, act=None):
+            if act is None:
+                act = ring.tile([P, HALF], F32, name="act")[:]
+            nc.scalar.activation(act, a_acc[:], SILU)
+            nc.vector.tensor_tensor(target, b_acc[:], act, MULT)
 
         a_accs = [first_layer(0, e, 0) for e in range(2)]
         for e in range(2):
             hidden(pairs[0][:, 0:HALF, e], a_accs[e], first_layer(1, e, 0))
+        a_accs = [first_layer(0, e, 1) for e in range(2)]
+        for e in range(2):
+            hidden(pairs[0][:, HALF:T, e], a_accs[e], first_layer(1, e, 1))
         for m in range(2):
             pick_words(m, 2, 2)
             pick_plane(m, 2, 2)
+        gather(0, 0, 768)
+        gather(0, 768, 768)
+        apart = keep.tile([P, 2, HALF], BF16, name="apart", align_bytes=64)
+        hidden(apart[:, 0, :], first_layer(0, 2, 0), first_layer(1, 2, 0))
+        hidden(apart[:, 1, :], first_layer(0, 3, 0), first_layer(1, 3, 0), gathered[:, 1536:SLOTS].bitcast(F32))
+        gather(0, 1536, 512)
+        nc.scalar.copy(pairs[1][:, 0:HALF, :], apart[:].rearrange("p e n -> p n e"))
         for e in range(2):
-            hidden(pairs[0][:, HALF:T, e], first_layer(0, e, 1), first_layer(1, e, 1))
-        gather(0, 0)
-        held_behind = {(0, 0): 1, (0, 1): 2, (1, 1): 3}
-        for h in range(2):
-            apart = keep.tile([P, 2, HALF], BF16, name="apart%d" % h, align_bytes=64)
-            for e in range(2):
-                c = held_behind.get((h, e))
-                tag = None if c is None else "chunk%d" % c
-                hidden(apart[:, e, :], first_layer(0, 2 + e, h), first_layer(1, 2 + e, h), tag=tag)
-                if c is not None:
-                    gather(0, c)
-            nc.scalar.copy(pairs[1][:, h * HALF : (h + 1) * HALF, :], apart[:].rearrange("p e n -> p n e"))
+            hidden(pairs[1][:, HALF:T, e], first_layer(0, 2 + e, 1), first_layer(1, 2 + e, 1))
 
-        woven = [keep.tile([P, n, 2], U32, name="woven%d" % c, align_bytes=64) for c, n in enumerate(SLOT_CHUNKS)]
-        for c, first, n in ((1, 0, 256), (0, 0, 512), (2, 0, 768), (3, 0, 256), (3, 256, 256)):
-            gather(1, c, first, n)
-            nc.scalar.copy(
-                woven[c][:, first : first + n, :], gathered[c][:, :, first : first + n].rearrange("p u n -> p n u")
-            )
+        woven = keep.tile([P, 2 * SLOTS], U32, name="woven", align_bytes=64)
+        both = gathered[:].rearrange("p (u n) -> p n u", u=2)
 
-        y = keep.tile([P, E * C], F32, name="y")
+        def weave(a, n, target):
+            nc.scalar.copy(target.rearrange("p (n u) -> p n u", u=2), both[:, a : a + n, :])
 
-        def second_layer(c, first, n):
-            a = starts(SLOT_CHUNKS)[c] + first
+        y = keep.tile([P, SLOTS], F32, name="y")
+
+        def second_layer(a, n, source):
             codes = keep.tile([P, n], U32, name="codes%d" % a, align_bytes=64)
             h_plane = keep.tile([P, n], U8, name="h_plane%d" % a, align_bytes=64)
-            nc.vector.quantize_mx(
-                out=codes[:].bitcast(FP8X4),
-                scales=h_plane[:],
-                in_=woven[c][:, first : first + n, :].rearrange("p n u -> p (n u)").bitcast(BF16),
-            )
+            nc.vector.quantize_mx(out=codes[:].bitcast(FP8X4), scales=h_plane[:], in_=source.bitcast(BF16))
             acc = psum.tile([P, HALF], F32, name="acc")
             for k in range(n // C):
                 e = a // C + k
@@ -202,18 +196,17 @@ def tile_moe_sup_glu_silu_kernel(
                     start=True,
                     stop=True,
                 )
-            if c == len(SLOT_CHUNKS) - 1:
+            return acc
+
+        for a, n in ((0, 512), (512, 512), (1024, 512), (1536, 256), (1792, 256)):
+            gather(1, a, n)
+            weave(a, n, woven[:, 2 * a : 2 * (a + n)])
+        for a, n in ((0, 256), (256, 256), (512, 512), (1024, 512), (1536, 256), (1792, 128), (1920, 128)):
+            acc = second_layer(a, n, woven[:, 2 * a : 2 * (a + n)])
+            if a >= 1536:
                 nc.vector.tensor_copy(y[:, a : a + n], acc[:, 0:n])
             else:
                 nc.scalar.copy(y[:, a : a + n], acc[:, 0:n])
-
-        second_layer(1, 0, 256)
-        second_layer(0, 0, 512)
-        second_layer(2, 0, 512)
-        second_layer(2, 512, 256)
-        second_layer(3, 0, 256)
-        second_layer(3, 256, 128)
-        second_layer(3, 384, 128)
 
         def weighted(r, c):
             a, n = starts(TOKEN_CHUNKS)[c], TOKEN_CHUNKS[c]
@@ -229,9 +222,10 @@ def tile_moe_sup_glu_silu_kernel(
             nc.vector.tensor_tensor(total[:], shares[0][:], shares[1][:], ADD)
             nc.sync.dma_start(out=out[:, a : a + n], in_=total[:])
 
-        first_share = weighted(0, 0)
-        for c in range(len(TOKEN_CHUNKS)):
-            shares = [first_share, weighted(1, c)]
-            if c + 1 < len(TOKEN_CHUNKS):
-                first_share = weighted(0, c + 1)
-            combine(c, shares)
+        first = [weighted(0, 0), weighted(1, 0)]
+        second = [weighted(0, 1)]
+        combine(0, first)
+        second.append(weighted(1, 1))
+        third = [weighted(0, 2), weighted(1, 2)]
+        combine(1, second)
+        combine(2, third)

@@ -40,7 +40,6 @@ def tile_moe_sup_glu_silu_kernel(
     nc = tc.nc
     with ExitStack() as ctx:
         keep = ctx.enter_context(tc.tile_pool(name="keep", bufs=1))
-        ring = ctx.enter_context(tc.tile_pool(name="ring", bufs=4))
         psum = ctx.enter_context(tc.psum_pool(name="psum", bufs=8))
 
         offs_sb = keep.tile([P, E * C // 16], U16, name="offs_sb")
@@ -147,30 +146,56 @@ def tile_moe_sup_glu_silu_kernel(
                 gathered[:, u * SLOTS + a : u * SLOTS + a + n], window.indirect(offs_sb[:, a // 16 : (a + n) // 16])
             )
 
-        def hidden(target, a_acc, b_acc, act=None):
-            if act is None:
-                act = ring.tile([P, HALF], F32, name="act")[:]
-            nc.scalar.activation(act, a_acc[:], SILU)
-            nc.vector.tensor_tensor(target, b_acc[:], act, MULT)
+        def first_half(u, acts):
+            apart = keep.tile([P, 2, HALF], BF16, name="apart%d" % u, align_bytes=64)
+            a_accs = [first_layer(0, 2 * u + e, 0) for e in range(2)]
+            for e in range(2):
+                b_acc = first_layer(1, 2 * u + e, 0)
+                nc.scalar.activation(acts[e], a_accs[e][:], SILU)
+                nc.vector.tensor_tensor(apart[:, e, :], b_acc[:], acts[e], MULT)
+            return apart
 
-        a_accs = [first_layer(0, e, 0) for e in range(2)]
-        for e in range(2):
-            hidden(pairs[0][:, 0:HALF, e], a_accs[e], first_layer(1, e, 0))
-        a_accs = [first_layer(0, e, 1) for e in range(2)]
-        for e in range(2):
-            hidden(pairs[0][:, HALF:T, e], a_accs[e], first_layer(1, e, 1))
+        def lay_out(copy, u, apart):
+            copy(pairs[u][:, 0:HALF, :], apart[:].rearrange("p e n -> p n e"))
+
+        def second_half(u, widths):
+            acts = keep.tile([P, 2, HALF], F32, name="acts%d" % u)
+            for e in range(2):
+                nc.scalar.activation(acts[:, e, :], first_layer(0, 2 * u + e, 1)[:], SILU)
+            for a, n in zip(starts(widths), widths):
+                acc = psum.tile([P, HALF], F32, name="acc")
+                for e in range(2):
+                    words, plane = picked_words[(1, 2 * u + e)], picked_plane[(1, 2 * u + e)]
+                    for t in range(a, a + n, P):
+                        for s in range(PASSES):
+                            nc.tensor.matmul_mx(
+                                out=acc[:, e * n + t - a : e * n + t - a + P],
+                                lhsT=words[:, 2 * P * s : 2 * P * (s + 1)].bitcast(FP4X4),
+                                lhsT_scale=plane[:, P * s : P * (s + 1)],
+                                rhs=x_halves[1][:, s, t : t + P].bitcast(FP8X4),
+                                rhs_scale=x_planes[1][:, s, t : t + P],
+                                start=(s == 0),
+                                stop=(s == PASSES - 1),
+                            )
+                nc.vector.tensor_tensor(
+                    pairs[u][:, HALF + a : HALF + a + n, :],
+                    acc[:, 0 : 2 * n].rearrange("p (e n) -> p n e", e=2),
+                    acts[:, :, a : a + n].rearrange("p e n -> p n e"),
+                    MULT,
+                )
+
+        first_acts = keep.tile([P, 2, HALF], F32, name="first_acts")
+        lay_out(nc.vector.tensor_copy, 0, first_half(0, [first_acts[:, e, :] for e in range(2)]))
+        second_half(0, (256, 128, 128))
         for m in range(2):
             pick_words(m, 2, 2)
             pick_plane(m, 2, 2)
         gather(0, 0, 768)
+        apart = first_half(1, [gathered[:, a : a + HALF].bitcast(F32) for a in (1536, 768)])
         gather(0, 768, 768)
-        apart = keep.tile([P, 2, HALF], BF16, name="apart", align_bytes=64)
-        hidden(apart[:, 0, :], first_layer(0, 2, 0), first_layer(1, 2, 0))
-        hidden(apart[:, 1, :], first_layer(0, 3, 0), first_layer(1, 3, 0), gathered[:, 1536:SLOTS].bitcast(F32))
         gather(0, 1536, 512)
-        nc.scalar.copy(pairs[1][:, 0:HALF, :], apart[:].rearrange("p e n -> p n e"))
-        for e in range(2):
-            hidden(pairs[1][:, HALF:T, e], first_layer(0, 2 + e, 1), first_layer(1, 2 + e, 1))
+        lay_out(nc.scalar.copy, 1, apart)
+        second_half(1, (256, 256))
 
         woven = keep.tile([P, 2 * SLOTS], U32, name="woven", align_bytes=64)
         both = gathered[:].rearrange("p (u n) -> p n u", u=2)

@@ -1,6 +1,7 @@
 from contextlib import ExitStack
 
 import concourse.mybir as mybir
+from concourse.masks import make_identity
 
 K, T, E, C, H, N = 1536, 1024, 16, 128, 512, 128
 FLOPS = 2 * (2 * K * H * T + H * N * E * C)
@@ -16,13 +17,14 @@ FP4X4 = mybir.dt.float4_e2m1fn_x4
 MULT = mybir.AluOpType.mult
 ADD = mybir.AluOpType.add
 SILU = mybir.ActivationFunctionType.Silu
+COPY = mybir.ActivationFunctionType.Copy
 
 P = 128
 PASSES = K // 512
 HALF = 512
 WARM_PASSES = 3
 SLOTS = E * C
-TOKEN_CHUNKS = (768, 128, 128)
+TURNED = 512
 
 
 def starts(widths):
@@ -54,7 +56,8 @@ def tile_moe_sup_glu_silu_kernel(
         raw_words = [keep.tile([P, PASSES, H // 2], I32, name="raw_words%d" % m, align_bytes=64) for m in range(2)]
         x_halves = [keep.tile([P, PASSES, HALF], I32, name="x_half%d" % h, align_bytes=64) for h in range(2)]
         w2_sb = keep.tile([P, E, N // 2], I32, name="w2_sb", align_bytes=64)
-        gate_sb = [keep.tile([P, T], F32, name="gate_sb%d" % r) for r in range(2)]
+        gate_sb = [keep.tile([P, T - TURNED], F32, name="gate_sb%d" % r) for r in range(2)]
+        gate_cols = [keep.tile([P, TURNED // P], F32, name="gate_cols%d" % r) for r in range(2)]
 
         x_view = x_words.rearrange("s p t d -> p s (t d)").bitcast(I32)
         by_row = "a (q r) w -> r q a w"
@@ -77,7 +80,12 @@ def tile_moe_sup_glu_silu_kernel(
         nc.sync.dma_start(pos_sb[0][:], pos1)
         nc.sync.dma_start(pos_sb[1][:], pos2)
         for r in range(2):
-            nc.sync.dma_start(out=gate_sb[r][:], in_=gate[r])
+            nc.sync.dma_start(out=gate_sb[r][:], in_=gate[r, :, TURNED:T])
+        with nc.allow_non_contiguous_dma(reason="one gate value a partition"):
+            for r in range(2):
+                nc.sync.dma_start(out=gate_cols[r][:], in_=gate[r, 0, 0:TURNED].rearrange("(c p) -> p c", p=P))
+        ident = keep.tile([P, P], F32, name="ident")
+        make_identity(nc, ident[:])
 
         warm_acc = psum.tile([P, HALF], F32, name="acc")
         for k in range(WARM_PASSES):
@@ -233,24 +241,54 @@ def tile_moe_sup_glu_silu_kernel(
             else:
                 nc.scalar.copy(y[:, a : a + n], acc[:, 0:n])
 
-        def weighted(r, c):
-            a, n = starts(TOKEN_CHUNKS)[c], TOKEN_CHUNKS[c]
-            share = keep.tile([P, n], F32, name="share%d_%d" % (r, c))
-            nc.vector.tensor_tensor(
-                share[:], y[:].indirect(pos_sb[r][:, a // 16 : (a + n) // 16]), gate_sb[r][:, a : a + n], MULT
-            )
-            return share
+        def slots_of(r, a, n):
+            return y[:].indirect(pos_sb[r][:, a // 16 : (a + n) // 16])
 
-        def combine(c, shares):
-            a, n = starts(TOKEN_CHUNKS)[c], TOKEN_CHUNKS[c]
-            total = keep.tile([P, n], F32, name="total%d" % c)
-            nc.vector.tensor_tensor(total[:], shares[0][:], shares[1][:], ADD)
-            nc.sync.dma_start(out=out[:, a : a + n], in_=total[:])
+        fetched = [keep.tile([P, TURNED], F32, name="fetched%d" % r) for r in range(2)]
 
-        first = [weighted(0, 0), weighted(1, 0)]
-        second = [weighted(0, 1)]
-        combine(0, first)
-        second.append(weighted(1, 1))
-        third = [weighted(0, 2), weighted(1, 2)]
-        combine(1, second)
-        combine(2, third)
+        def turn_and_weigh(r, a, n):
+            turned = psum.tile([P, HALF], F32, name="acc")
+            for t in range(0, n, P):
+                nc.tensor.transpose(turned[:, t : t + P], fetched[r][:, a + t : a + t + P], ident[:])
+            weighed = keep.tile([P, n], F32, name="weighed%d_%d" % (r, a))
+            for t in range(0, n, P):
+                c = (a + t) // P
+                nc.scalar.activation(weighed[:, t : t + P], turned[:, t : t + P], COPY, scale=gate_cols[r][:, c : c + 1])
+            return weighed
+
+        def turn_back(a, n, shares):
+            acc = psum.tile([P, HALF], F32, name="acc")
+            for t in range(0, n, P):
+                for r in range(2):
+                    nc.tensor.matmul(
+                        acc[:, t : t + P], shares[r][:, t : t + P], ident[:], start=(r == 0), stop=(r == 1), is_transpose=True
+                    )
+            total = keep.tile([P, n], F32, name="total%d" % a)
+            nc.scalar.copy(total[:], acc[:, 0:n])
+            nc.scalar.dma_start(out=out[:, a : a + n], in_=total[:])
+
+        nc.vector.tensor_copy(fetched[0][:], slots_of(0, 0, TURNED))
+        first = turn_and_weigh(0, 0, TURNED)
+        for a in range(0, TURNED, 256):
+            nc.vector.tensor_copy(fetched[1][:, a : a + 256], slots_of(1, a, 256))
+            turn_back(a, 256, [first[:, a : a + 256], turn_and_weigh(1, a, 256)[:]])
+
+        shares = [keep.tile([P, T - TURNED], F32, name="share%d" % r) for r in range(2)]
+
+        def weighted(r, a, n):
+            nc.vector.tensor_tensor(shares[r][:, a : a + n], slots_of(r, TURNED + a, n), gate_sb[r][:, a : a + n], MULT)
+
+        def combine(a, n):
+            total = keep.tile([P, n], F32, name="total%d" % (TURNED + a))
+            nc.vector.tensor_tensor(total[:], shares[0][:, a : a + n], shares[1][:, a : a + n], ADD)
+            nc.sync.dma_start(out=out[:, TURNED + a : TURNED + a + n], in_=total[:])
+
+        weighted(0, 0, 256)
+        weighted(1, 0, 256)
+        weighted(0, 256, 128)
+        combine(0, 256)
+        weighted(1, 256, 128)
+        weighted(0, 384, 128)
+        weighted(1, 384, 128)
+        combine(256, 128)
+        combine(384, 128)

@@ -67,9 +67,9 @@ def tile_moe_sup_glu_silu_kernel(
         nc.sync.dma_start(out=raw_words[0][:], in_=w1_words.bitcast(I32).rearrange("s p w -> p s w"))
         nc.sync.dma_start(out=x_halves[0][:, :, 0:P], in_=x_view[:, :, 0:P])
         load_scale_rows(on_sync, raw_scales[0], w1_scales.bitcast(I32).rearrange(by_row, r=4))
-        load_scale_rows([nc.sync] * 3 + [nc.gpsimd], x_planes[0], first_rows, (0, 3))
+        load_scale_rows(on_sync, x_planes[0], first_rows, (0,))
         nc.sync.dma_start(out=x_halves[0][:, :, P:HALF], in_=x_view[:, :, P:HALF])
-        load_scale_rows(on_sync, x_planes[0], first_rows, (1, 2))
+        load_scale_rows(on_sync, x_planes[0], first_rows, (1, 2, 3))
         nc.sync.dma_start(out=raw_words[1][:], in_=w3_words.bitcast(I32).rearrange("s p w -> p s w"))
         load_scale_rows(on_sync, raw_scales[1], w3_scales.bitcast(I32).rearrange(by_row, r=4))
         nc.sync.dma_start(out=x_halves[1][:], in_=x_view[:, :, HALF:T])
@@ -84,8 +84,6 @@ def tile_moe_sup_glu_silu_kernel(
         with nc.allow_non_contiguous_dma(reason="one gate value a partition"):
             for r in range(2):
                 nc.sync.dma_start(out=gate_cols[r][:], in_=gate[r, 0, 0:TURNED].rearrange("(c p) -> p c", p=P))
-        ident = keep.tile([P, P], F32, name="ident")
-        make_identity(nc, ident[:])
 
         warm_acc = psum.tile([P, HALF], F32, name="acc")
         for k in range(WARM_PASSES):
@@ -192,12 +190,14 @@ def tile_moe_sup_glu_silu_kernel(
                     MULT,
                 )
 
-        first_acts = keep.tile([P, 2, HALF], F32, name="first_acts")
+        first_acts = keep.tile([P, 2, HALF], F32, name="first_acts", tag="early")
         lay_out(nc.vector.tensor_copy, 0, first_half(0, [first_acts[:, e, :] for e in range(2)]))
         second_half(0, (256, 128, 128))
         for m in range(2):
             pick_words(m, 2, 2)
             pick_plane(m, 2, 2)
+        ident = keep.tile([P, P], F32, name="ident", tag="early")
+        make_identity(nc, ident[:])
         gather(0, 0, 768)
         apart = first_half(1, [gathered[:, a : a + HALF].bitcast(F32) for a in (1536, 768)])
         gather(0, 768, 768)

@@ -25,6 +25,7 @@ HALF = 512
 WARM_PASSES = 3
 SLOTS = E * C
 TURNED = 512
+ON_VECTOR = 1664
 
 
 def starts(widths):
@@ -152,17 +153,15 @@ def tile_moe_sup_glu_silu_kernel(
                 gathered[:, u * SLOTS + a : u * SLOTS + a + n], window.indirect(offs_sb[:, a // 16 : (a + n) // 16])
             )
 
-        def first_half(u, acts):
-            apart = keep.tile([P, 2, HALF], BF16, name="apart%d" % u, align_bytes=64)
+        def first_half(u, acts, apart):
             a_accs = [first_layer(0, 2 * u + e, 0) for e in range(2)]
             for e in range(2):
                 b_acc = first_layer(1, 2 * u + e, 0)
                 nc.scalar.activation(acts[e], a_accs[e][:], SILU)
                 nc.vector.tensor_tensor(apart[:, e, :], b_acc[:], acts[e], MULT)
-            return apart
 
         def lay_out(copy, u, apart):
-            copy(pairs[u][:, 0:HALF, :], apart[:].rearrange("p e n -> p n e"))
+            copy(pairs[u][:, 0:HALF, :], apart.rearrange("p e n -> p n e"))
 
         def second_half(u, widths):
             acts = keep.tile([P, 2, HALF], F32, name="acts%d" % u)
@@ -191,19 +190,30 @@ def tile_moe_sup_glu_silu_kernel(
                 )
 
         first_acts = keep.tile([P, 2, HALF], F32, name="first_acts", tag="early")
-        lay_out(nc.vector.tensor_copy, 0, first_half(0, [first_acts[:, e, :] for e in range(2)]))
+        planes = keep.tile([P, 2 * T], BF16, name="planes", align_bytes=64)
+        by_plane = planes[:].rearrange("p (e t) -> p e t", e=2)
+        first_half(0, [first_acts[:, e, :] for e in range(2)], by_plane[:, :, 0:HALF])
+        lay_out(nc.vector.tensor_copy, 0, by_plane[:, :, 0:HALF])
         second_half(0, (256, 128, 128))
+        for a in (HALF, HALF + 256):
+            nc.scalar.copy(by_plane[:, :, a : a + 256], pairs[0][:, a : a + 256, :].rearrange("p t e -> p e t"))
         for m in range(2):
             pick_words(m, 2, 2)
             pick_plane(m, 2, 2)
         ident = keep.tile([P, P], F32, name="ident", tag="early")
         make_identity(nc, ident[:])
         gather(0, 0, 768)
-        apart = first_half(1, [gathered[:, a : a + HALF].bitcast(F32) for a in (1536, 768)])
-        gather(0, 768, 768)
-        gather(0, 1536, 512)
-        lay_out(nc.scalar.copy, 1, apart)
+        spare = keep.tile([P, HALF], F32, name="spare")
+        apart = keep.tile([P, 2, HALF], BF16, name="apart", align_bytes=64)
+        first_half(1, [spare[:], gathered[:, 1216 : 1216 + HALF].bitcast(F32)], apart[:])
+        gather(0, 768, 512)
+        gather(0, 1280, 384)
+        lay_out(nc.scalar.copy, 1, apart[:])
         second_half(1, (256, 256))
+        by_value = gathered[:, ON_VECTOR:SLOTS].bitcast(BF16).rearrange("p (n e) -> p n e", e=2)
+        for e in range(2):
+            window = planes[:, e * T : (e + 1) * T]
+            nc.scalar.activation(by_value[:, :, e], window.indirect(offs_sb[:, ON_VECTOR // 16 : SLOTS // 16]), COPY)
 
         woven = keep.tile([P, 2 * SLOTS], U32, name="woven", align_bytes=64)
         both = gathered[:].rearrange("p (u n) -> p n u", u=2)
@@ -236,7 +246,7 @@ def tile_moe_sup_glu_silu_kernel(
             weave(a, n, woven[:, 2 * a : 2 * (a + n)])
         for a, n in ((0, 256), (256, 256), (512, 512), (1024, 512), (1536, 256), (1792, 128), (1920, 128)):
             acc = second_layer(a, n, woven[:, 2 * a : 2 * (a + n)])
-            if a >= 1536:
+            if a + n == SLOTS:
                 nc.vector.tensor_copy(y[:, a : a + n], acc[:, 0:n])
             else:
                 nc.scalar.copy(y[:, a : a + n], acc[:, 0:n])

@@ -22,10 +22,10 @@ COPY = mybir.ActivationFunctionType.Copy
 P = 128
 PASSES = K // 512
 HALF = 512
+QUARTER = 256
 WARM_PASSES = 3
 SLOTS = E * C
 TURNED = 512
-ON_VECTOR = 1664
 
 
 def starts(widths):
@@ -163,10 +163,10 @@ def tile_moe_sup_glu_silu_kernel(
         def lay_out(copy, u, apart):
             copy(pairs[u][:, 0:HALF, :], apart.rearrange("p e n -> p n e"))
 
-        def second_half(u, widths):
-            acts = keep.tile([P, 2, HALF], F32, name="acts%d" % u)
+        def second_half(u, acts, widths):
             for e in range(2):
-                nc.scalar.activation(acts[:, e, :], first_layer(0, 2 * u + e, 1)[:], SILU)
+                sums = first_layer(0, 2 * u + e, 1)[:].rearrange("p (b n) -> p b n", b=2)
+                nc.scalar.activation(acts[:, :, e, :], sums, SILU)
             for a, n in zip(starts(widths), widths):
                 acc = psum.tile([P, HALF], F32, name="acc")
                 for e in range(2):
@@ -185,7 +185,7 @@ def tile_moe_sup_glu_silu_kernel(
                 nc.vector.tensor_tensor(
                     pairs[u][:, HALF + a : HALF + a + n, :],
                     acc[:, 0 : 2 * n].rearrange("p (e n) -> p n e", e=2),
-                    acts[:, :, a : a + n].rearrange("p e n -> p n e"),
+                    acts[:, a // QUARTER, :, a % QUARTER : a % QUARTER + n].rearrange("p e n -> p n e"),
                     MULT,
                 )
 
@@ -194,7 +194,8 @@ def tile_moe_sup_glu_silu_kernel(
         by_plane = planes[:].rearrange("p (e t) -> p e t", e=2)
         first_half(0, [first_acts[:, e, :] for e in range(2)], by_plane[:, :, 0:HALF])
         lay_out(nc.vector.tensor_copy, 0, by_plane[:, :, 0:HALF])
-        second_half(0, (256, 128, 128))
+        second_acts = keep.tile([P, 2, 2, QUARTER], F32, name="second_acts")
+        second_half(0, second_acts[:], (256, 128, 128))
         for a in (HALF, HALF + 256):
             nc.scalar.copy(by_plane[:, :, a : a + 256], pairs[0][:, a : a + 256, :].rearrange("p t e -> p e t"))
         for m in range(2):
@@ -202,18 +203,23 @@ def tile_moe_sup_glu_silu_kernel(
             pick_plane(m, 2, 2)
         ident = keep.tile([P, P], F32, name="ident", tag="early")
         make_identity(nc, ident[:])
+
+        def gather_planes(a, n):
+            by_value = gathered[:, a : a + n].bitcast(BF16).rearrange("p (n e) -> p n e", e=2)
+            for e in range(2):
+                window = planes[:, e * T : (e + 1) * T]
+                nc.scalar.activation(by_value[:, :, e], window.indirect(offs_sb[:, a // 16 : (a + n) // 16]), COPY)
+
         gather(0, 0, 768)
-        spare = keep.tile([P, HALF], F32, name="spare")
-        apart = keep.tile([P, 2, HALF], BF16, name="apart", align_bytes=64)
-        first_half(1, [spare[:], gathered[:, 1216 : 1216 + HALF].bitcast(F32)], apart[:])
+        later_acts = keep.tile([P, 2, HALF], F32, name="later_acts")
+        apart = gathered[:, 768:1280].bitcast(BF16).rearrange("p (e n) -> p e n", e=2)
+        first_half(1, [later_acts[:, e, :] for e in range(2)], apart)
+        gather_planes(1280, 384)
+        lay_out(nc.vector.tensor_copy, 1, apart)
         gather(0, 768, 512)
-        gather(0, 1280, 384)
-        lay_out(nc.scalar.copy, 1, apart[:])
-        second_half(1, (256, 256))
-        by_value = gathered[:, ON_VECTOR:SLOTS].bitcast(BF16).rearrange("p (n e) -> p n e", e=2)
-        for e in range(2):
-            window = planes[:, e * T : (e + 1) * T]
-            nc.scalar.activation(by_value[:, :, e], window.indirect(offs_sb[:, ON_VECTOR // 16 : SLOTS // 16]), COPY)
+        last_acts = gathered[:, 1664 : 1664 + T].bitcast(F32).rearrange("p (b e n) -> p b e n", b=2, e=2)
+        second_half(1, last_acts, (256, 256))
+        gather_planes(1664, 384)
 
         woven = keep.tile([P, 2 * SLOTS], U32, name="woven", align_bytes=64)
         both = gathered[:].rearrange("p (u n) -> p n u", u=2)
@@ -223,11 +229,10 @@ def tile_moe_sup_glu_silu_kernel(
 
         y = keep.tile([P, SLOTS], F32, name="y")
 
-        def second_layer(a, n, source):
+        def second_layer(acc, a, n, source):
             codes = keep.tile([P, n], U32, name="codes%d" % a, align_bytes=64)
             h_plane = keep.tile([P, n], U8, name="h_plane%d" % a, align_bytes=64)
             nc.vector.quantize_mx(out=codes[:].bitcast(FP8X4), scales=h_plane[:], in_=source.bitcast(BF16))
-            acc = psum.tile([P, HALF], F32, name="acc")
             for k in range(n // C):
                 e = a // C + k
                 nc.tensor.matmul_mx(
@@ -239,13 +244,15 @@ def tile_moe_sup_glu_silu_kernel(
                     start=True,
                     stop=True,
                 )
-            return acc
 
-        for a, n in ((0, 512), (512, 512), (1024, 512), (1536, 256), (1792, 256)):
+        for a, n in ((0, 768), (768, 512), (1280, 512), (1792, 256)):
             gather(1, a, n)
             weave(a, n, woven[:, 2 * a : 2 * (a + n)])
-        for a, n in ((0, 256), (256, 256), (512, 512), (1024, 512), (1536, 256), (1792, 128), (1920, 128)):
-            acc = second_layer(a, n, woven[:, 2 * a : 2 * (a + n)])
+        for a, n in ((0, 512), (512, 512), (1024, 512), (1536, 256), (1792, 128), (1920, 128)):
+            acc = psum.tile([P, HALF], F32, name="acc")
+            step = min(n, QUARTER)
+            for k in range(0, n, step):
+                second_layer(acc[:, k : k + step], a + k, step, woven[:, 2 * (a + k) : 2 * (a + k + step)])
             if a + n == SLOTS:
                 nc.vector.tensor_copy(y[:, a : a + n], acc[:, 0:n])
             else:
@@ -293,12 +300,10 @@ def tile_moe_sup_glu_silu_kernel(
             nc.vector.tensor_tensor(total[:], shares[0][:, a : a + n], shares[1][:, a : a + n], ADD)
             nc.sync.dma_start(out=out[:, TURNED + a : TURNED + a + n], in_=total[:])
 
-        weighted(0, 0, 256)
+        weighted(0, 0, 512)
         weighted(1, 0, 256)
-        weighted(0, 256, 128)
-        combine(0, 256)
         weighted(1, 256, 128)
-        weighted(0, 384, 128)
+        combine(0, 256)
         weighted(1, 384, 128)
         combine(256, 128)
         combine(384, 128)

@@ -23,7 +23,7 @@ P = 128
 PASSES = K // 512
 HALF = 512
 QUARTER = 256
-WARM_PASSES = 3
+WARM_PASSES = 4
 SLOTS = E * C
 TURNED = 512
 
@@ -91,9 +91,9 @@ def tile_moe_sup_glu_silu_kernel(
             nc.tensor.matmul_mx(
                 out=warm_acc[:],
                 lhsT=x_halves[0][:, 0, 0:P].bitcast(FP8X4),
-                lhsT_scale=raw_scales[0][:, 0, 0:P],
+                lhsT_scale=raw_words[0][:, 1, 0 : P // 4].bitcast(U8),
                 rhs=raw_words[0][:, 0, :].bitcast(FP4X4),
-                rhs_scale=raw_scales[0][:, 0, :],
+                rhs_scale=raw_words[0][:, 1, 0:P].bitcast(U8),
                 start=True,
                 stop=True,
             )
@@ -212,14 +212,14 @@ def tile_moe_sup_glu_silu_kernel(
 
         gather(0, 0, 768)
         later_acts = keep.tile([P, 2, HALF], F32, name="later_acts")
-        apart = gathered[:, 768:1280].bitcast(BF16).rearrange("p (e n) -> p e n", e=2)
+        apart = gathered[:, 1152 : 1152 + HALF].bitcast(BF16).rearrange("p (e n) -> p e n", e=2)
         first_half(1, [later_acts[:, e, :] for e in range(2)], apart)
-        gather_planes(1280, 384)
+        gather_planes(768, 384)
         lay_out(nc.vector.tensor_copy, 1, apart)
-        gather(0, 768, 512)
+        gather(0, 1152, 384)
         last_acts = gathered[:, 1664 : 1664 + T].bitcast(F32).rearrange("p (b e n) -> p b e n", b=2, e=2)
-        second_half(1, last_acts, (256, 256))
-        gather_planes(1664, 384)
+        second_half(1, last_acts, (256, 128, 128))
+        gather_planes(1536, 512)
 
         woven = keep.tile([P, 2 * SLOTS], U32, name="woven", align_bytes=64)
         both = gathered[:].rearrange("p (u n) -> p n u", u=2)
@@ -253,7 +253,7 @@ def tile_moe_sup_glu_silu_kernel(
             step = min(n, QUARTER)
             for k in range(0, n, step):
                 second_layer(acc[:, k : k + step], a + k, step, woven[:, 2 * (a + k) : 2 * (a + k + step)])
-            if a + n == SLOTS:
+            if n < HALF:
                 nc.vector.tensor_copy(y[:, a : a + n], acc[:, 0:n])
             else:
                 nc.scalar.copy(y[:, a : a + n], acc[:, 0:n])

@@ -26,6 +26,7 @@ QUARTER = 256
 WARM_PASSES = 4
 SLOTS = E * C
 TURNED = 512
+LATE = 1408
 
 
 def starts(widths):
@@ -121,10 +122,14 @@ def tile_moe_sup_glu_silu_kernel(
             for e in range(count):
                 picked_words[(m, first + e)] = words[:, e, :]
 
-        for m in range(2):
-            pick_words(m, 0, 2)
-            pick_plane(m, 0, 1)
-            pick_plane(m, 1, 1)
+        pick_words(0, 0, 2)
+        pick_plane(0, 0, 1)
+        pick_plane(0, 1, 1)
+        pick_words(0, 2, 2)
+        pick_plane(0, 2, 2)
+        pick_words(1, 0, 2)
+        pick_plane(1, 0, 1)
+        pick_plane(1, 1, 1)
 
         def first_layer_pass(acc, m, j, h, s):
             words, plane = picked_words[(m, j)], picked_plane[(m, j)]
@@ -144,21 +149,26 @@ def tile_moe_sup_glu_silu_kernel(
                 first_layer_pass(acc, m, j, h, s)
             return acc
 
-        pairs = [keep.tile([P, T, 2], BF16, name="pairs%d" % u, align_bytes=64) for u in range(2)]
-        gathered = keep.tile([P, 2 * SLOTS], U32, name="gathered", align_bytes=64)
+        pairs = [keep.tile([P, T, 2], BF16, name="pairs%d" % u, tag="pairs%d" % u, align_bytes=64) for u in range(2)]
+        gathered = {0: keep.tile([P, 2 * LATE], U32, name="gathered", align_bytes=64)}
+
+        def words_of(a, n):
+            first = LATE if a >= LATE else 0
+            return gathered[first][:].rearrange("p (u n) -> p u n", u=2)[:, :, a - first : a - first + n]
 
         def gather(u, a, n):
             window = pairs[u][:].rearrange("p t e -> p (t e)").bitcast(U32)
-            nc.vector.tensor_copy(
-                gathered[:, u * SLOTS + a : u * SLOTS + a + n], window.indirect(offs_sb[:, a // 16 : (a + n) // 16])
-            )
+            nc.vector.tensor_copy(words_of(a, n)[:, u, :], window.indirect(offs_sb[:, a // 16 : (a + n) // 16]))
 
-        def first_half(u, acts, apart):
-            a_accs = [first_layer(0, 2 * u + e, 0) for e in range(2)]
+        first_acts = [keep.tile([P, HALF], F32, name="first_act%d" % j, tag="first_act%d" % j) for j in range(4)]
+
+        def first_silu(j):
+            nc.scalar.activation(first_acts[j][:], first_layer(0, j, 0)[:], SILU)
+
+        def first_half(u, apart):
             for e in range(2):
-                b_acc = first_layer(1, 2 * u + e, 0)
-                nc.scalar.activation(acts[e], a_accs[e][:], SILU)
-                nc.vector.tensor_tensor(apart[:, e, :], b_acc[:], acts[e], MULT)
+                j = 2 * u + e
+                nc.vector.tensor_tensor(apart[:, e, :], first_layer(1, j, 0)[:], first_acts[j][:], MULT)
 
         def lay_out(copy, u, apart):
             copy(pairs[u][:, 0:HALF, :], apart.rearrange("p e n -> p n e"))
@@ -189,43 +199,43 @@ def tile_moe_sup_glu_silu_kernel(
                     MULT,
                 )
 
-        first_acts = keep.tile([P, 2, HALF], F32, name="first_acts", tag="early")
         planes = keep.tile([P, 2 * T], BF16, name="planes", align_bytes=64)
         by_plane = planes[:].rearrange("p (e t) -> p e t", e=2)
-        first_half(0, [first_acts[:, e, :] for e in range(2)], by_plane[:, :, 0:HALF])
+        for j in range(3):
+            first_silu(j)
+        first_half(0, by_plane[:, :, 0:HALF])
         lay_out(nc.vector.tensor_copy, 0, by_plane[:, :, 0:HALF])
         second_acts = keep.tile([P, 2, 2, QUARTER], F32, name="second_acts")
         second_half(0, second_acts[:], (256, 128, 128))
         for a in (HALF, HALF + 256):
             nc.scalar.copy(by_plane[:, :, a : a + 256], pairs[0][:, a : a + 256, :].rearrange("p t e -> p e t"))
-        for m in range(2):
-            pick_words(m, 2, 2)
-            pick_plane(m, 2, 2)
-        ident = keep.tile([P, P], F32, name="ident", tag="early")
+        pick_words(1, 2, 2)
+        pick_plane(1, 2, 2)
+        ident = keep.tile([P, P], F32, name="ident", tag="first_act1")
         make_identity(nc, ident[:])
 
         def gather_planes(a, n):
-            by_value = gathered[:, a : a + n].bitcast(BF16).rearrange("p (n e) -> p n e", e=2)
+            by_value = words_of(a, n)[:, 0, :].bitcast(BF16).rearrange("p (n e) -> p n e", e=2)
             for e in range(2):
                 window = planes[:, e * T : (e + 1) * T]
                 nc.scalar.activation(by_value[:, :, e], window.indirect(offs_sb[:, a // 16 : (a + n) // 16]), COPY)
 
         gather(0, 0, 768)
-        later_acts = keep.tile([P, 2, HALF], F32, name="later_acts")
-        apart = gathered[:, 1152 : 1152 + HALF].bitcast(BF16).rearrange("p (e n) -> p e n", e=2)
-        first_half(1, [later_acts[:, e, :] for e in range(2)], apart)
+        apart = gathered[0][:, 1152 : 1152 + HALF].bitcast(BF16).rearrange("p (e n) -> p e n", e=2)
+        first_silu(3)
+        first_half(1, apart)
         gather_planes(768, 384)
         lay_out(nc.vector.tensor_copy, 1, apart)
-        gather(0, 1152, 384)
-        last_acts = gathered[:, 1664 : 1664 + T].bitcast(F32).rearrange("p (b e n) -> p b e n", b=2, e=2)
-        second_half(1, last_acts, (256, 128, 128))
-        gather_planes(1536, 512)
+        gather(0, 1152, 256)
+        last_acts = keep.tile([P, 2, 2, QUARTER], F32, name="last_acts")
+        second_half(1, last_acts[:], (256, 128, 128))
+        gathered[LATE] = keep.tile([P, 2 * (SLOTS - LATE)], U32, name="late", tag="pairs0", align_bytes=64)
+        gather_planes(LATE, SLOTS - LATE)
 
         woven = keep.tile([P, 2 * SLOTS], U32, name="woven", align_bytes=64)
-        both = gathered[:].rearrange("p (u n) -> p n u", u=2)
 
         def weave(a, n, target):
-            nc.scalar.copy(target.rearrange("p (n u) -> p n u", u=2), both[:, a : a + n, :])
+            nc.scalar.copy(target.rearrange("p (n u) -> p n u", u=2), words_of(a, n).rearrange("p u n -> p n u"))
 
         y = keep.tile([P, SLOTS], F32, name="y")
 
@@ -245,7 +255,7 @@ def tile_moe_sup_glu_silu_kernel(
                     stop=True,
                 )
 
-        for a, n in ((0, 768), (768, 512), (1280, 512), (1792, 256)):
+        for a, n in ((0, 768), (768, 640), (1408, 384), (1792, 256)):
             gather(1, a, n)
             weave(a, n, woven[:, 2 * a : 2 * (a + n)])
         for a, n in ((0, 512), (512, 512), (1024, 512), (1536, 256), (1792, 128), (1920, 128)):

@@ -235,7 +235,8 @@ def tile_moe_sup_glu_silu_kernel(
         woven = keep.tile([P, 2 * SLOTS], U32, name="woven", align_bytes=64)
 
         def weave(a, n, target):
-            nc.scalar.copy(target.rearrange("p (n u) -> p n u", u=2), words_of(a, n).rearrange("p u n -> p n u"))
+            copy = nc.gpsimd.tensor_copy if a == 0 else nc.scalar.copy
+            copy(target.rearrange("p (n u) -> p n u", u=2), words_of(a, n).rearrange("p u n -> p n u"))
 
         y = keep.tile([P, SLOTS], F32, name="y")
 

@@ -26,7 +26,8 @@ QUARTER = 256
 WARM_PASSES = 4
 SLOTS = E * C
 TURNED = 512
-LATE = 1408
+LATE = 1536
+SHARED = 1344
 
 
 def starts(widths):
@@ -149,8 +150,13 @@ def tile_moe_sup_glu_silu_kernel(
                 first_layer_pass(acc, m, j, h, s)
             return acc
 
-        pairs = [keep.tile([P, T, 2], BF16, name="pairs%d" % u, tag="pairs%d" % u, align_bytes=64) for u in range(2)]
-        gathered = {0: keep.tile([P, 2 * LATE], U32, name="gathered", align_bytes=64)}
+        pairs = [keep.tile([P, T, 2], BF16, name="pairs%d" % u, align_bytes=64) for u in range(2)]
+        planes = [keep.tile([P, 2 * T], BF16, name="planes%d" % u, align_bytes=64) for u in range(2)]
+        by_plane = [t[:].rearrange("p (e t) -> p e t", e=2) for t in planes]
+        gathered = {
+            0: keep.tile([P, 2 * LATE], U32, name="gathered", align_bytes=64),
+            LATE: keep.tile([P, 2 * (SLOTS - LATE)], U32, name="late", align_bytes=64),
+        }
 
         def words_of(a, n):
             first = LATE if a >= LATE else 0
@@ -160,23 +166,31 @@ def tile_moe_sup_glu_silu_kernel(
             window = pairs[u][:].rearrange("p t e -> p (t e)").bitcast(U32)
             nc.vector.tensor_copy(words_of(a, n)[:, u, :], window.indirect(offs_sb[:, a // 16 : (a + n) // 16]))
 
+        def gather_planes(u, a, n):
+            by_value = words_of(a, n)[:, u, :].bitcast(BF16).rearrange("p (n e) -> p n e", e=2)
+            for e in range(2):
+                window = planes[u][:, e * T : (e + 1) * T]
+                nc.scalar.activation(by_value[:, :, e], window.indirect(offs_sb[:, a // 16 : (a + n) // 16]), COPY)
+
         first_acts = [keep.tile([P, HALF], F32, name="first_act%d" % j, tag="first_act%d" % j) for j in range(4)]
+        second_acts = [keep.tile([P, 2, 2, QUARTER], F32, name="second_acts%d" % u) for u in range(2)]
 
         def first_silu(j):
             nc.scalar.activation(first_acts[j][:], first_layer(0, j, 0)[:], SILU)
 
-        def first_half(u, apart):
-            for e in range(2):
-                j = 2 * u + e
-                nc.vector.tensor_tensor(apart[:, e, :], first_layer(1, j, 0)[:], first_acts[j][:], MULT)
-
-        def lay_out(copy, u, apart):
-            copy(pairs[u][:, 0:HALF, :], apart.rearrange("p e n -> p n e"))
-
-        def second_half(u, acts, widths):
+        def second_silus(u):
             for e in range(2):
                 sums = first_layer(0, 2 * u + e, 1)[:].rearrange("p (b n) -> p b n", b=2)
-                nc.scalar.activation(acts[:, :, e, :], sums, SILU)
+                nc.scalar.activation(second_acts[u][:, :, e, :], sums, SILU)
+
+        def first_half(u, copy):
+            for e in range(2):
+                j = 2 * u + e
+                nc.vector.tensor_tensor(by_plane[u][:, e, 0:HALF], first_layer(1, j, 0)[:], first_acts[j][:], MULT)
+            copy(pairs[u][:, 0:HALF, :], by_plane[u][:, :, 0:HALF].rearrange("p e n -> p n e"))
+
+        def second_half(u, widths, copy):
+            acts = second_acts[u]
             for a, n in zip(starts(widths), widths):
                 acc = psum.tile([P, HALF], F32, name="acc")
                 for e in range(2):
@@ -198,44 +212,32 @@ def tile_moe_sup_glu_silu_kernel(
                     acts[:, a // QUARTER, :, a % QUARTER : a % QUARTER + n].rearrange("p e n -> p n e"),
                     MULT,
                 )
+                made = slice(HALF + a, HALF + a + n)
+                copy(by_plane[u][:, :, made], pairs[u][:, made, :].rearrange("p t e -> p e t"))
 
-        planes = keep.tile([P, 2 * T], BF16, name="planes", align_bytes=64)
-        by_plane = planes[:].rearrange("p (e t) -> p e t", e=2)
         for j in range(3):
             first_silu(j)
-        first_half(0, by_plane[:, :, 0:HALF])
-        lay_out(nc.vector.tensor_copy, 0, by_plane[:, :, 0:HALF])
-        second_acts = keep.tile([P, 2, 2, QUARTER], F32, name="second_acts")
-        second_half(0, second_acts[:], (256, 128, 128))
-        for a in (HALF, HALF + 256):
-            nc.scalar.copy(by_plane[:, :, a : a + 256], pairs[0][:, a : a + 256, :].rearrange("p t e -> p e t"))
+        first_half(0, nc.vector.tensor_copy)
+        second_silus(0)
+        second_half(0, (256, 128, 128), nc.gpsimd.tensor_copy)
         pick_words(1, 2, 2)
         pick_plane(1, 2, 2)
-        ident = keep.tile([P, P], F32, name="ident", tag="first_act1")
+        ident = keep.tile([P, P], F32, name="ident", tag="first_act0")
         make_identity(nc, ident[:])
 
-        def gather_planes(a, n):
-            by_value = words_of(a, n)[:, 0, :].bitcast(BF16).rearrange("p (n e) -> p n e", e=2)
-            for e in range(2):
-                window = planes[:, e * T : (e + 1) * T]
-                nc.scalar.activation(by_value[:, :, e], window.indirect(offs_sb[:, a // 16 : (a + n) // 16]), COPY)
-
-        gather(0, 0, 768)
-        apart = gathered[0][:, 1152 : 1152 + HALF].bitcast(BF16).rearrange("p (e n) -> p e n", e=2)
         first_silu(3)
-        first_half(1, apart)
-        gather_planes(768, 384)
-        lay_out(nc.vector.tensor_copy, 1, apart)
-        gather(0, 1152, 256)
-        last_acts = keep.tile([P, 2, 2, QUARTER], F32, name="last_acts")
-        second_half(1, last_acts[:], (256, 128, 128))
-        gathered[LATE] = keep.tile([P, 2 * (SLOTS - LATE)], U32, name="late", tag="pairs0", align_bytes=64)
-        gather_planes(LATE, SLOTS - LATE)
+        second_silus(1)
+        gather(0, 0, 768)
+        gather(0, 768, SHARED - 768)
+        gather_planes(0, SHARED, LATE - SHARED)
+        gather_planes(0, LATE, SLOTS - LATE)
+        first_half(1, nc.gpsimd.tensor_copy)
+        second_half(1, (256, 128, 128), nc.scalar.copy)
 
         woven = keep.tile([P, 2 * SLOTS], U32, name="woven", align_bytes=64)
 
-        def weave(a, n, target):
-            copy = nc.gpsimd.tensor_copy if a == 0 else nc.scalar.copy
+        def weave(copy, a, n):
+            target = woven[:, 2 * a : 2 * (a + n)]
             copy(target.rearrange("p (n u) -> p n u", u=2), words_of(a, n).rearrange("p u n -> p n u"))
 
         y = keep.tile([P, SLOTS], F32, name="y")
@@ -256,10 +258,15 @@ def tile_moe_sup_glu_silu_kernel(
                     stop=True,
                 )
 
-        for a, n in ((0, 768), (768, 640), (1408, 384), (1792, 256)):
-            gather(1, a, n)
-            weave(a, n, woven[:, 2 * a : 2 * (a + n)])
-        for a, n in ((0, 512), (512, 512), (1024, 512), (1536, 256), (1792, 128), (1920, 128)):
+        for a in range(0, LATE, QUARTER):
+            gather(1, a, QUARTER)
+        gather_planes(1, LATE, SLOTS - LATE)
+        for a in range(0, 1024, QUARTER):
+            weave(nc.gpsimd.tensor_copy, a, QUARTER)
+        weave(nc.scalar.copy, LATE, SLOTS - LATE)
+        for a in range(1024, LATE, QUARTER):
+            weave(nc.scalar.copy, a, QUARTER)
+        for a, n in ((0, 512), (512, 512), (1536, 512), (1024, 256), (1280, 128), (1408, 128)):
             acc = psum.tile([P, HALF], F32, name="acc")
             step = min(n, QUARTER)
             for k in range(0, n, step):

@@ -26,8 +26,8 @@ QUARTER = 256
 WARM_PASSES = 4
 SLOTS = E * C
 TURNED = 512
+EARLY = 1152
 LATE = 1536
-SHARED = 1344
 
 
 def starts(widths):
@@ -150,48 +150,48 @@ def tile_moe_sup_glu_silu_kernel(
                 first_layer_pass(acc, m, j, h, s)
             return acc
 
-        pairs = [keep.tile([P, T, 2], BF16, name="pairs%d" % u, align_bytes=64) for u in range(2)]
+        pairs = [keep.tile([P, T, 2], BF16, name="pairs%d" % u, tag="pairs%d" % u, align_bytes=64) for u in range(2)]
         planes = [keep.tile([P, 2 * T], BF16, name="planes%d" % u, align_bytes=64) for u in range(2)]
         by_plane = [t[:].rearrange("p (e t) -> p e t", e=2) for t in planes]
         gathered = {
-            0: keep.tile([P, 2 * LATE], U32, name="gathered", align_bytes=64),
-            LATE: keep.tile([P, 2 * (SLOTS - LATE)], U32, name="late", align_bytes=64),
+            0: keep.tile([P, 2 * EARLY], U32, name="gathered", align_bytes=64),
+            EARLY: keep.tile([P, 2 * (LATE - EARLY)], U32, name="early", align_bytes=64),
         }
 
         def words_of(a, n):
-            first = LATE if a >= LATE else 0
+            first = max(b for b in gathered if b <= a)
             return gathered[first][:].rearrange("p (u n) -> p u n", u=2)[:, :, a - first : a - first + n]
 
         def gather(u, a, n):
             window = pairs[u][:].rearrange("p t e -> p (t e)").bitcast(U32)
             nc.vector.tensor_copy(words_of(a, n)[:, u, :], window.indirect(offs_sb[:, a // 16 : (a + n) // 16]))
 
-        def gather_planes(u, a, n):
+        def gather_planes(u, a, n, which=range(2)):
             by_value = words_of(a, n)[:, u, :].bitcast(BF16).rearrange("p (n e) -> p n e", e=2)
-            for e in range(2):
+            for e in which:
                 window = planes[u][:, e * T : (e + 1) * T]
                 nc.scalar.activation(by_value[:, :, e], window.indirect(offs_sb[:, a // 16 : (a + n) // 16]), COPY)
 
-        first_acts = [keep.tile([P, HALF], F32, name="first_act%d" % j, tag="first_act%d" % j) for j in range(4)]
+        act_tiles = [keep.tile([P, HALF], F32, name="first_act%d" % j, tag="first_act%d" % j) for j in range(3)]
+        first_acts = [t[:] for t in act_tiles] + [gathered[0][:, 768 : 768 + HALF].bitcast(F32)]
         second_acts = [keep.tile([P, 2, 2, QUARTER], F32, name="second_acts%d" % u) for u in range(2)]
 
         def first_silu(j):
-            nc.scalar.activation(first_acts[j][:], first_layer(0, j, 0)[:], SILU)
+            nc.scalar.activation(first_acts[j], first_layer(0, j, 0)[:], SILU)
 
-        def second_silus(u):
-            for e in range(2):
-                sums = first_layer(0, 2 * u + e, 1)[:].rearrange("p (b n) -> p b n", b=2)
-                nc.scalar.activation(second_acts[u][:, :, e, :], sums, SILU)
+        def second_silu(u, e):
+            sums = first_layer(0, 2 * u + e, 1)[:].rearrange("p (b n) -> p b n", b=2)
+            nc.scalar.activation(second_acts[u][:, :, e, :], sums, SILU)
 
         def first_half(u, copy):
             for e in range(2):
                 j = 2 * u + e
-                nc.vector.tensor_tensor(by_plane[u][:, e, 0:HALF], first_layer(1, j, 0)[:], first_acts[j][:], MULT)
+                nc.vector.tensor_tensor(by_plane[u][:, e, 0:HALF], first_layer(1, j, 0)[:], first_acts[j], MULT)
             copy(pairs[u][:, 0:HALF, :], by_plane[u][:, :, 0:HALF].rearrange("p e n -> p n e"))
 
-        def second_half(u, widths, copy):
+        def second_half(u, widths, copies):
             acts = second_acts[u]
-            for a, n in zip(starts(widths), widths):
+            for a, n, copy in zip(starts(widths), widths, copies):
                 acc = psum.tile([P, HALF], F32, name="acc")
                 for e in range(2):
                     words, plane = picked_words[(1, 2 * u + e)], picked_plane[(1, 2 * u + e)]
@@ -218,21 +218,24 @@ def tile_moe_sup_glu_silu_kernel(
         for j in range(3):
             first_silu(j)
         first_half(0, nc.vector.tensor_copy)
-        second_silus(0)
-        second_half(0, (256, 128, 128), nc.gpsimd.tensor_copy)
+        second_silu(0, 0)
+        second_silu(0, 1)
+        second_half(0, (256, 128, 128), [nc.gpsimd.tensor_copy] * 3)
         pick_words(1, 2, 2)
         pick_plane(1, 2, 2)
         ident = keep.tile([P, P], F32, name="ident", tag="first_act0")
         make_identity(nc, ident[:])
 
         first_silu(3)
-        second_silus(1)
+        second_silu(1, 0)
         gather(0, 0, 768)
-        gather(0, 768, SHARED - 768)
-        gather_planes(0, SHARED, LATE - SHARED)
-        gather_planes(0, LATE, SLOTS - LATE)
         first_half(1, nc.gpsimd.tensor_copy)
-        second_half(1, (256, 128, 128), nc.scalar.copy)
+        second_silu(1, 1)
+        gather_planes(0, EARLY, LATE - EARLY)
+        gather(0, 768, EARLY - 768)
+        gathered[LATE] = keep.tile([P, 2 * (SLOTS - LATE)], U32, name="late", tag="pairs0", align_bytes=64)
+        gather_planes(0, LATE, SLOTS - LATE)
+        second_half(1, (256, 128, 128), [nc.gpsimd.tensor_copy] * 3)
 
         woven = keep.tile([P, 2 * SLOTS], U32, name="woven", align_bytes=64)
 
@@ -258,14 +261,16 @@ def tile_moe_sup_glu_silu_kernel(
                     stop=True,
                 )
 
-        for a in range(0, LATE, QUARTER):
-            gather(1, a, QUARTER)
-        gather_planes(1, LATE, SLOTS - LATE)
-        for a in range(0, 1024, QUARTER):
-            weave(nc.gpsimd.tensor_copy, a, QUARTER)
-        weave(nc.scalar.copy, LATE, SLOTS - LATE)
-        for a in range(1024, LATE, QUARTER):
-            weave(nc.scalar.copy, a, QUARTER)
+        chunks = ((0, 256), (256, 288), (544, 288), (832, 320), (EARLY, LATE - EARLY))
+        for a, n in chunks:
+            gather(1, a, n)
+        gather_planes(1, LATE, SLOTS - LATE, (0,))
+        gather_planes(1, LATE, 256, (1,))
+        gather_planes(1, LATE + 256, 256, (1,))
+        for a, n in chunks[:4]:
+            weave(nc.gpsimd.tensor_copy, a, n)
+        for a, n in ((LATE, 256), (LATE + 256, 256)) + chunks[4:]:
+            weave(nc.scalar.copy, a, n)
         for a, n in ((0, 512), (512, 512), (1536, 512), (1024, 256), (1280, 128), (1408, 128)):
             acc = psum.tile([P, HALF], F32, name="acc")
             step = min(n, QUARTER)

@@ -26,7 +26,7 @@ QUARTER = 256
 WARM_PASSES = 4
 SLOTS = E * C
 TURNED = 512
-EARLY = 1152
+EARLY = 1024
 LATE = 1536
 
 
@@ -154,7 +154,7 @@ def tile_moe_sup_glu_silu_kernel(
         planes = [keep.tile([P, 2 * T], BF16, name="planes%d" % u, align_bytes=64) for u in range(2)]
         by_plane = [t[:].rearrange("p (e t) -> p e t", e=2) for t in planes]
         gathered = {
-            0: keep.tile([P, 2 * EARLY], U32, name="gathered", align_bytes=64),
+            0: keep.tile([P, 2 * EARLY], U32, name="gathered", tag="gathered", align_bytes=64),
             EARLY: keep.tile([P, 2 * (LATE - EARLY)], U32, name="early", align_bytes=64),
         }
 
@@ -212,8 +212,8 @@ def tile_moe_sup_glu_silu_kernel(
                     acts[:, a // QUARTER, :, a % QUARTER : a % QUARTER + n].rearrange("p e n -> p n e"),
                     MULT,
                 )
-                made = slice(HALF + a, HALF + a + n)
-                copy(by_plane[u][:, :, made], pairs[u][:, made, :].rearrange("p t e -> p e t"))
+                fresh = slice(HALF + a, HALF + a + n)
+                copy(by_plane[u][:, :, fresh], pairs[u][:, fresh, :].rearrange("p t e -> p e t"))
 
         for j in range(3):
             first_silu(j)
@@ -229,9 +229,10 @@ def tile_moe_sup_glu_silu_kernel(
         first_silu(3)
         second_silu(1, 0)
         gather(0, 0, 768)
+        gather(0, EARLY, 128)
         first_half(1, nc.gpsimd.tensor_copy)
         second_silu(1, 1)
-        gather_planes(0, EARLY, LATE - EARLY)
+        gather_planes(0, EARLY + 128, LATE - EARLY - 128)
         gather(0, 768, EARLY - 768)
         gathered[LATE] = keep.tile([P, 2 * (SLOTS - LATE)], U32, name="late", tag="pairs0", align_bytes=64)
         gather_planes(0, LATE, SLOTS - LATE)
@@ -245,41 +246,47 @@ def tile_moe_sup_glu_silu_kernel(
 
         y = keep.tile([P, SLOTS], F32, name="y")
 
-        def second_layer(acc, a, n, source):
-            codes = keep.tile([P, n], U32, name="codes%d" % a, align_bytes=64)
+        def quantise(a, n):
+            codes = all_codes[:, a : a + n]
             h_plane = keep.tile([P, n], U8, name="h_plane%d" % a, align_bytes=64)
-            nc.vector.quantize_mx(out=codes[:].bitcast(FP8X4), scales=h_plane[:], in_=source.bitcast(BF16))
+            source = woven[:, 2 * a : 2 * (a + n)]
+            nc.vector.quantize_mx(out=codes.bitcast(FP8X4), scales=h_plane[:], in_=source.bitcast(BF16))
+            for k in range(n // C):
+                made[a // C + k] = (codes[:, k * C : (k + 1) * C], h_plane[:, k * C : (k + 1) * C])
+
+        def second_layer(a, n, copy):
+            acc = psum.tile([P, HALF], F32, name="acc")
             for k in range(n // C):
                 e = a // C + k
                 nc.tensor.matmul_mx(
                     out=acc[:, k * C : (k + 1) * C],
                     lhsT=w2_sb[:, e, :].bitcast(FP4X4),
                     lhsT_scale=w2_plane[:, e, :],
-                    rhs=codes[:, k * C : (k + 1) * C].bitcast(FP8X4),
-                    rhs_scale=h_plane[:, k * C : (k + 1) * C],
+                    rhs=made[e][0].bitcast(FP8X4),
+                    rhs_scale=made[e][1],
                     start=True,
                     stop=True,
                 )
+            copy(y[:, a : a + n], acc[:, 0:n])
 
-        chunks = ((0, 256), (256, 288), (544, 288), (832, 320), (EARLY, LATE - EARLY))
+        made = {}
+        chunks = ((0, 256), (256, 384), (640, 384), (EARLY, LATE - EARLY))
         for a, n in chunks:
             gather(1, a, n)
         gather_planes(1, LATE, SLOTS - LATE, (0,))
         gather_planes(1, LATE, 256, (1,))
         gather_planes(1, LATE + 256, 256, (1,))
-        for a, n in chunks[:4]:
+        for a, n in chunks[:3]:
             weave(nc.gpsimd.tensor_copy, a, n)
-        for a, n in ((LATE, 256), (LATE + 256, 256)) + chunks[4:]:
+        for a, n in ((LATE, 256), (LATE + 256, 256)) + chunks[3:]:
             weave(nc.scalar.copy, a, n)
-        for a, n in ((0, 512), (512, 512), (1536, 512), (1024, 256), (1280, 128), (1408, 128)):
-            acc = psum.tile([P, HALF], F32, name="acc")
-            step = min(n, QUARTER)
-            for k in range(0, n, step):
-                second_layer(acc[:, k : k + step], a + k, step, woven[:, 2 * (a + k) : 2 * (a + k + step)])
-            if n < HALF:
-                nc.vector.tensor_copy(y[:, a : a + n], acc[:, 0:n])
-            else:
-                nc.scalar.copy(y[:, a : a + n], acc[:, 0:n])
+        all_codes = keep.tile([P, SLOTS], U32, name="all_codes", tag="gathered", align_bytes=64)
+        for a, n in ((0, 256), (256, 256), (512, 256), (768, 256), (1536, 256), (1792, 256), (1024, 256), (1280, 128), (1408, 128)):
+            quantise(a, n)
+        for a in (0, 512, 1536):
+            second_layer(a, HALF, nc.scalar.copy)
+        for a, n in ((1024, 256), (1280, 128), (1408, 128)):
+            second_layer(a, n, nc.vector.tensor_copy)
 
         def slots_of(r, a, n):
             return y[:].indirect(pos_sb[r][:, a // 16 : (a + n) // 16])

@@ -23,7 +23,7 @@ P = 128
 PASSES = K // 512
 HALF = 512
 QUARTER = 256
-WARM_PASSES = 4
+WARM_PASSES = 3
 SLOTS = E * C
 TURNED = 512
 EARLY = 1024
@@ -56,8 +56,12 @@ def tile_moe_sup_glu_silu_kernel(
         for plane in (raw_scales[0], x_planes[0], raw_scales[1], x_planes[1], w2_plane):
             nc.vector.memset(plane[:].bitcast(I32), 0)
 
-        raw_words = [keep.tile([P, PASSES, H // 2], I32, name="raw_words%d" % m, align_bytes=64) for m in range(2)]
-        x_halves = [keep.tile([P, PASSES, HALF], I32, name="x_half%d" % h, align_bytes=64) for h in range(2)]
+        w1_first = keep.tile([P, 1, H // 2], I32, name="w1_first", align_bytes=64)
+        w1_rest = keep.tile([P, PASSES - 1, H // 2], I32, name="w1_rest", align_bytes=64)
+        w3_raw = keep.tile([P, PASSES, H // 2], I32, name="w3_raw", align_bytes=64)
+        x_first = [keep.tile([P, HALF], I32, name="x_first%d" % s, align_bytes=64) for s in range(PASSES)]
+        x_second = keep.tile([P, PASSES, HALF], I32, name="x_second", align_bytes=64)
+        x_passes = [[t[:] for t in x_first], [x_second[:, s, :] for s in range(PASSES)]]
         w2_sb = keep.tile([P, E, N // 2], I32, name="w2_sb", align_bytes=64)
         gate_sb = [keep.tile([P, T - TURNED], F32, name="gate_sb%d" % r) for r in range(2)]
         gate_cols = [keep.tile([P, TURNED // P], F32, name="gate_cols%d" % r) for r in range(2)]
@@ -67,16 +71,19 @@ def tile_moe_sup_glu_silu_kernel(
         x_rows = x_scales.bitcast(I32).rearrange(by_row, r=4)
         on_sync = [nc.sync] * 4
         first_rows = x_rows[:, :, :, 0 : HALF // 4]
-        nc.sync.dma_start(out=raw_words[0][:], in_=w1_words.bitcast(I32).rearrange("s p w -> p s w"))
-        nc.sync.dma_start(out=x_halves[0][:, :, 0:P], in_=x_view[:, :, 0:P])
+        w1_view = w1_words.bitcast(I32).rearrange("s p w -> p s w")
+        nc.sync.dma_start(out=x_first[0][:, 0:P], in_=x_view[:, 0, 0:P])
+        nc.sync.dma_start(out=w1_first[:], in_=w1_view[:, 0:1, :])
         load_scale_rows(on_sync, raw_scales[0], w1_scales.bitcast(I32).rearrange(by_row, r=4))
-        load_scale_rows(on_sync, x_planes[0], first_rows, (0,))
-        nc.sync.dma_start(out=x_halves[0][:, :, P:HALF], in_=x_view[:, :, P:HALF])
-        load_scale_rows(on_sync, x_planes[0], first_rows, (1, 2, 3))
-        nc.sync.dma_start(out=raw_words[1][:], in_=w3_words.bitcast(I32).rearrange("s p w -> p s w"))
+        nc.sync.dma_start(out=x_first[0][:, P:HALF], in_=x_view[:, 0, P:HALF])
+        nc.sync.dma_start(out=w1_rest[:], in_=w1_view[:, 1:PASSES, :])
+        load_scale_rows(on_sync, x_planes[0], first_rows)
+        for s in range(1, PASSES):
+            nc.sync.dma_start(out=x_first[s][:], in_=x_view[:, s, 0:HALF])
         load_scale_rows(on_sync, raw_scales[1], w3_scales.bitcast(I32).rearrange(by_row, r=4))
-        nc.sync.dma_start(out=x_halves[1][:], in_=x_view[:, :, HALF:T])
+        nc.sync.dma_start(out=w3_raw[:], in_=w3_words.bitcast(I32).rearrange("s p w -> p s w"))
         load_scale_rows(on_sync, x_planes[1], x_rows[:, :, :, HALF // 4 : T // 4])
+        nc.sync.dma_start(out=x_second[:], in_=x_view[:, :, HALF:T])
         nc.sync.dma_start(offs_sb[:], offs)
         load_scale_rows(on_sync, w2_plane, w2_scales.bitcast(I32).rearrange("e o (q r) w -> r q (e o) w", r=4))
         nc.sync.dma_start(out=w2_sb[:], in_=w2_words.bitcast(I32).rearrange("e o p w -> p (e o) w"))
@@ -92,10 +99,10 @@ def tile_moe_sup_glu_silu_kernel(
         for k in range(WARM_PASSES):
             nc.tensor.matmul_mx(
                 out=warm_acc[:],
-                lhsT=x_halves[0][:, 0, 0:P].bitcast(FP8X4),
-                lhsT_scale=raw_words[0][:, 1, 0 : P // 4].bitcast(U8),
-                rhs=raw_words[0][:, 0, :].bitcast(FP4X4),
-                rhs_scale=raw_words[0][:, 1, 0:P].bitcast(U8),
+                lhsT=x_first[0][:, 0:P].bitcast(FP8X4),
+                lhsT_scale=w1_first[:, 0, 0 : P // 4].bitcast(U8),
+                rhs=w1_first[:, 0, :].bitcast(FP4X4),
+                rhs_scale=w1_first[:, 0, 0:P].bitcast(U8),
                 start=True,
                 stop=True,
             )
@@ -103,42 +110,46 @@ def tile_moe_sup_glu_silu_kernel(
         picked_words = {}
         picked_plane = {}
 
-        def pick_plane(m, first, count):
-            plane = keep.tile([P, count, PASSES * P], U8, name="plane%d_%d" % (m, first), align_bytes=64)
-            source = raw_scales[m][:].rearrange("p s c -> p (s c)").rearrange("p (b i j) -> p b j i", i=16, j=4)
+        def pick_plane(m, first, count, first_pass, passes):
+            name = "plane%d_%d_%d" % (m, first, first_pass)
+            plane = keep.tile([P, count, passes * P], U8, name=name, align_bytes=64)
+            rows = raw_scales[m][:, first_pass : first_pass + passes, :]
+            source = rows.rearrange("p s c -> p (s c)").rearrange("p (b i j) -> p b j i", i=16, j=4)
             nc.vector.tensor_copy(
                 out=plane[:].rearrange("p e (b i) -> p b e i", i=16), in_=source[:, :, first : first + count, :]
             )
             for e in range(count):
-                picked_plane[(m, first + e)] = plane[:, e, :]
+                for s in range(passes):
+                    picked_plane[(m, first + e, first_pass + s)] = plane[:, e, P * s : P * (s + 1)]
 
-        def pick_words(m, first, count):
-            words = keep.tile([P, count, PASSES * 2 * P], U8, name="words%d_%d" % (m, first), align_bytes=64)
-            flat = raw_words[m][:].bitcast(U16).rearrange("p s c -> p (s c)")
+        def pick_words(raw, m, first, count, first_pass):
+            passes = raw.shape[1]
+            words = keep.tile([P, count, passes * 2 * P], U8, name="words%d_%d_%d" % (m, first, first_pass), align_bytes=64)
+            flat = raw[:].bitcast(U16).rearrange("p s c -> p (s c)")
             source = flat.rearrange("p (b i j) -> p b j i", i=8, j=4)
             nc.vector.tensor_copy(
                 out=words[:].bitcast(U16).rearrange("p e (b i) -> p b e i", i=8),
                 in_=source[:, :, first : first + count, :],
             )
             for e in range(count):
-                picked_words[(m, first + e)] = words[:, e, :]
+                for s in range(passes):
+                    picked_words[(m, first + e, first_pass + s)] = words[:, e, 2 * P * s : 2 * P * (s + 1)]
 
-        pick_words(0, 0, 2)
-        pick_plane(0, 0, 1)
-        pick_plane(0, 1, 1)
-        pick_words(0, 2, 2)
-        pick_plane(0, 2, 2)
-        pick_words(1, 0, 2)
-        pick_plane(1, 0, 1)
-        pick_plane(1, 1, 1)
+        pick_words(w1_first, 0, 0, 4, 0)
+        pick_plane(0, 0, 4, 0, 1)
+        pick_plane(0, 0, 4, 1, 1)
+        pick_words(w1_rest, 0, 0, 4, 1)
+        pick_plane(0, 0, 4, 2, 1)
+        pick_plane(1, 0, 2, 0, PASSES)
+        pick_words(w3_raw, 1, 0, 1, 0)
+        pick_words(w3_raw, 1, 1, 1, 0)
 
         def first_layer_pass(acc, m, j, h, s):
-            words, plane = picked_words[(m, j)], picked_plane[(m, j)]
             nc.tensor.matmul_mx(
                 out=acc[:],
-                lhsT=words[:, 2 * P * s : 2 * P * (s + 1)].bitcast(FP4X4),
-                lhsT_scale=plane[:, P * s : P * (s + 1)],
-                rhs=x_halves[h][:, s, :].bitcast(FP8X4),
+                lhsT=picked_words[(m, j, s)].bitcast(FP4X4),
+                lhsT_scale=picked_plane[(m, j, s)],
+                rhs=x_passes[h][s].bitcast(FP8X4),
                 rhs_scale=x_planes[h][:, s, :],
                 start=(s == 0),
                 stop=(s == PASSES - 1),
@@ -194,14 +205,13 @@ def tile_moe_sup_glu_silu_kernel(
             for a, n, copy in zip(starts(widths), widths, copies):
                 acc = psum.tile([P, HALF], F32, name="acc")
                 for e in range(2):
-                    words, plane = picked_words[(1, 2 * u + e)], picked_plane[(1, 2 * u + e)]
                     for t in range(a, a + n, P):
                         for s in range(PASSES):
                             nc.tensor.matmul_mx(
                                 out=acc[:, e * n + t - a : e * n + t - a + P],
-                                lhsT=words[:, 2 * P * s : 2 * P * (s + 1)].bitcast(FP4X4),
-                                lhsT_scale=plane[:, P * s : P * (s + 1)],
-                                rhs=x_halves[1][:, s, t : t + P].bitcast(FP8X4),
+                                lhsT=picked_words[(1, 2 * u + e, s)].bitcast(FP4X4),
+                                lhsT_scale=picked_plane[(1, 2 * u + e, s)],
+                                rhs=x_second[:, s, t : t + P].bitcast(FP8X4),
                                 rhs_scale=x_planes[1][:, s, t : t + P],
                                 start=(s == 0),
                                 stop=(s == PASSES - 1),
@@ -215,14 +225,18 @@ def tile_moe_sup_glu_silu_kernel(
                 fresh = slice(HALF + a, HALF + a + n)
                 copy(by_plane[u][:, :, fresh], pairs[u][:, fresh, :].rearrange("p t e -> p e t"))
 
+        opening = [psum.tile([P, HALF], F32, name="acc") for j in range(3)]
+        for s in range(PASSES):
+            for j in range(3):
+                first_layer_pass(opening[j], 0, j, 0, s)
         for j in range(3):
-            first_silu(j)
+            nc.scalar.activation(first_acts[j], opening[j][:], SILU)
         first_half(0, nc.vector.tensor_copy)
         second_silu(0, 0)
         second_silu(0, 1)
         second_half(0, (256, 128, 128), [nc.gpsimd.tensor_copy] * 3)
-        pick_words(1, 2, 2)
-        pick_plane(1, 2, 2)
+        pick_words(w3_raw, 1, 2, 2, 0)
+        pick_plane(1, 2, 2, 0, PASSES)
         ident = keep.tile([P, P], F32, name="ident", tag="first_act0")
         make_identity(nc, ident[:])
 

@@ -22,16 +22,13 @@ COPY = mybir.ActivationFunctionType.Copy
 P = 128
 PASSES = K // 512
 HALF = 512
-QUARTER = 256
 WARM_PASSES = 3
 SLOTS = E * C
 TURNED = 512
 EARLY = 1024
+AHEAD = 256
+SHARED = 1376
 LATE = 1536
-
-
-def starts(widths):
-    return [sum(widths[:i]) for i in range(len(widths))]
 
 
 def load_scale_rows(queues, plane, rows, which=range(4)):
@@ -162,12 +159,14 @@ def tile_moe_sup_glu_silu_kernel(
             return acc
 
         pairs = [keep.tile([P, T, 2], BF16, name="pairs%d" % u, tag="pairs%d" % u, align_bytes=64) for u in range(2)]
-        planes = [keep.tile([P, 2 * T], BF16, name="planes%d" % u, align_bytes=64) for u in range(2)]
-        by_plane = [t[:].rearrange("p (e t) -> p e t", e=2) for t in planes]
+        both = [keep.tile([P, 2 * T], BF16, name="planes%d" % u, align_bytes=64) for u in range(2)]
         gathered = {
             0: keep.tile([P, 2 * EARLY], U32, name="gathered", tag="gathered", align_bytes=64),
             EARLY: keep.tile([P, 2 * (LATE - EARLY)], U32, name="early", align_bytes=64),
         }
+
+        def plane_of(j):
+            return both[j // 2][:, (j % 2) * T : (j % 2 + 1) * T]
 
         def words_of(a, n):
             first = max(b for b in gathered if b <= a)
@@ -177,80 +176,65 @@ def tile_moe_sup_glu_silu_kernel(
             window = pairs[u][:].rearrange("p t e -> p (t e)").bitcast(U32)
             nc.vector.tensor_copy(words_of(a, n)[:, u, :], window.indirect(offs_sb[:, a // 16 : (a + n) // 16]))
 
-        def gather_planes(u, a, n, which=range(2)):
-            by_value = words_of(a, n)[:, u, :].bitcast(BF16).rearrange("p (n e) -> p n e", e=2)
-            for e in which:
-                window = planes[u][:, e * T : (e + 1) * T]
-                nc.scalar.activation(by_value[:, :, e], window.indirect(offs_sb[:, a // 16 : (a + n) // 16]), COPY)
+        def gather_plane(j, a, n):
+            by_value = words_of(a, n)[:, j // 2, :].bitcast(BF16).rearrange("p (n e) -> p n e", e=2)
+            nc.scalar.activation(by_value[:, :, j % 2], plane_of(j).indirect(offs_sb[:, a // 16 : (a + n) // 16]), COPY)
 
-        act_tiles = [keep.tile([P, HALF], F32, name="first_act%d" % j, tag="first_act%d" % j) for j in range(3)]
-        first_acts = [t[:] for t in act_tiles] + [gathered[0][:, 768 : 768 + HALF].bitcast(F32)]
-        second_acts = [keep.tile([P, 2, 2, QUARTER], F32, name="second_acts%d" % u) for u in range(2)]
+        acts = {(3, 0): gathered[EARLY][:, SHARED - EARLY : SHARED - EARLY + HALF].bitcast(F32)}
 
-        def first_silu(j):
-            nc.scalar.activation(first_acts[j], first_layer(0, j, 0)[:], SILU)
+        def silu_of(j, h, acc):
+            if (j, h) not in acts:
+                acts[(j, h)] = keep.tile([P, HALF], F32, name="act%d_%d" % (j, h), tag="act%d_%d" % (j, h))[:]
+            nc.scalar.activation(acts[(j, h)], acc[:], SILU)
 
-        def second_silu(u, e):
-            sums = first_layer(0, 2 * u + e, 1)[:].rearrange("p (b n) -> p b n", b=2)
-            nc.scalar.activation(second_acts[u][:, :, e, :], sums, SILU)
+        def silu(j, h):
+            silu_of(j, h, first_layer(0, j, h))
 
-        def first_half(u, copy):
-            for e in range(2):
-                j = 2 * u + e
-                nc.vector.tensor_tensor(by_plane[u][:, e, 0:HALF], first_layer(1, j, 0)[:], first_acts[j], MULT)
-            copy(pairs[u][:, 0:HALF, :], by_plane[u][:, :, 0:HALF].rearrange("p e n -> p n e"))
+        def product(j, h, cuts=(0, HALF)):
+            acc = first_layer(1, j, h)
+            for a, b in zip(cuts, cuts[1:]):
+                nc.vector.tensor_tensor(plane_of(j)[:, h * HALF + a : h * HALF + b], acc[:, a:b], acts[(j, h)][:, a:b], MULT)
 
-        def second_half(u, widths, copies):
-            acts = second_acts[u]
-            for a, n, copy in zip(starts(widths), widths, copies):
-                acc = psum.tile([P, HALF], F32, name="acc")
-                for e in range(2):
-                    for t in range(a, a + n, P):
-                        for s in range(PASSES):
-                            nc.tensor.matmul_mx(
-                                out=acc[:, e * n + t - a : e * n + t - a + P],
-                                lhsT=picked_words[(1, 2 * u + e, s)].bitcast(FP4X4),
-                                lhsT_scale=picked_plane[(1, 2 * u + e, s)],
-                                rhs=x_second[:, s, t : t + P].bitcast(FP8X4),
-                                rhs_scale=x_planes[1][:, s, t : t + P],
-                                start=(s == 0),
-                                stop=(s == PASSES - 1),
-                            )
-                nc.vector.tensor_tensor(
-                    pairs[u][:, HALF + a : HALF + a + n, :],
-                    acc[:, 0 : 2 * n].rearrange("p (e n) -> p n e", e=2),
-                    acts[:, a // QUARTER, :, a % QUARTER : a % QUARTER + n].rearrange("p e n -> p n e"),
-                    MULT,
-                )
-                fresh = slice(HALF + a, HALF + a + n)
-                copy(by_plane[u][:, :, fresh], pairs[u][:, fresh, :].rearrange("p t e -> p e t"))
+        def pair_up(copy, u, a, n):
+            copy(pairs[u][:, a : a + n, :], both[u][:].rearrange("p (e t) -> p t e", e=2)[:, a : a + n, :])
+
+        def last_product(u):
+            product(2 * u + 1, 1, (0, AHEAD, HALF))
+            pair_up(nc.vector.tensor_copy, u, HALF, AHEAD)
+            pair_up(nc.vector.tensor_copy, u, HALF + AHEAD, HALF - AHEAD)
 
         opening = [psum.tile([P, HALF], F32, name="acc") for j in range(3)]
         for s in range(PASSES):
             for j in range(3):
                 first_layer_pass(opening[j], 0, j, 0, s)
         for j in range(3):
-            nc.scalar.activation(first_acts[j], opening[j][:], SILU)
-        first_half(0, nc.vector.tensor_copy)
-        second_silu(0, 0)
-        second_silu(0, 1)
-        second_half(0, (256, 128, 128), [nc.gpsimd.tensor_copy] * 3)
+            silu_of(j, 0, opening[j])
+        product(0, 0)
+        product(1, 0)
+        pair_up(nc.vector.tensor_copy, 0, 0, HALF)
+        silu(0, 1)
+        silu(1, 1)
+        product(0, 1)
+        last_product(0)
         pick_words(w3_raw, 1, 2, 2, 0)
         pick_plane(1, 2, 2, 0, PASSES)
-        ident = keep.tile([P, P], F32, name="ident", tag="first_act0")
+        ident = keep.tile([P, P], F32, name="ident", tag="act0_0")
         make_identity(nc, ident[:])
 
-        first_silu(3)
-        second_silu(1, 0)
         gather(0, 0, 768)
-        gather(0, EARLY, 128)
-        first_half(1, nc.gpsimd.tensor_copy)
-        second_silu(1, 1)
-        gather_planes(0, EARLY + 128, LATE - EARLY - 128)
-        gather(0, 768, EARLY - 768)
+        silu(3, 0)
+        silu(2, 1)
+        product(2, 0)
+        product(3, 0)
+        pair_up(nc.gpsimd.tensor_copy, 1, 0, HALF)
+        silu(3, 1)
+        gather(0, SHARED, LATE - SHARED)
+        product(2, 1)
+        last_product(1)
         gathered[LATE] = keep.tile([P, 2 * (SLOTS - LATE)], U32, name="late", tag="pairs0", align_bytes=64)
-        gather_planes(0, LATE, SLOTS - LATE)
-        second_half(1, (256, 128, 128), [nc.gpsimd.tensor_copy] * 3)
+        for a, n in ((768, EARLY - 768), (EARLY, SHARED - EARLY), (LATE, SLOTS - LATE)):
+            for j in range(2):
+                gather_plane(j, a, n)
 
         woven = keep.tile([P, 2 * SLOTS], U32, name="woven", align_bytes=64)
 
@@ -287,9 +271,9 @@ def tile_moe_sup_glu_silu_kernel(
         chunks = ((0, 256), (256, 384), (640, 384), (EARLY, LATE - EARLY))
         for a, n in chunks:
             gather(1, a, n)
-        gather_planes(1, LATE, SLOTS - LATE, (0,))
-        gather_planes(1, LATE, 256, (1,))
-        gather_planes(1, LATE + 256, 256, (1,))
+        gather_plane(2, LATE, SLOTS - LATE)
+        gather_plane(3, LATE, 256)
+        gather_plane(3, LATE + 256, 256)
         for a, n in chunks[:3]:
             weave(nc.gpsimd.tensor_copy, a, n)
         for a, n in ((LATE, 256), (LATE + 256, 256)) + chunks[3:]:

@@ -22,6 +22,7 @@ COPY = mybir.ActivationFunctionType.Copy
 P = 128
 PASSES = K // 512
 HALF = 512
+QUARTER = 256
 WARM_PASSES = 3
 SLOTS = E * C
 TURNED = 512
@@ -203,6 +204,40 @@ def tile_moe_sup_glu_silu_kernel(
             pair_up(nc.vector.tensor_copy, u, HALF, AHEAD)
             pair_up(nc.vector.tensor_copy, u, HALF + AHEAD, HALF - AHEAD)
 
+        late_acts = keep.tile([P, 2, 2, QUARTER], F32, name="late_acts")
+
+        def late_silu(e):
+            sums = first_layer(0, 2 + e, 1)[:].rearrange("p (b n) -> p b n", b=2)
+            nc.scalar.activation(late_acts[:, :, e, :], sums, SILU)
+
+        def last_pair(widths):
+            a = 0
+            for n in widths:
+                acc = psum.tile([P, HALF], F32, name="acc")
+                for e in range(2):
+                    for t in range(a, a + n, P):
+                        for s in range(PASSES):
+                            nc.tensor.matmul_mx(
+                                out=acc[:, e * n + t - a : e * n + t - a + P],
+                                lhsT=picked_words[(1, 2 + e, s)].bitcast(FP4X4),
+                                lhsT_scale=picked_plane[(1, 2 + e, s)],
+                                rhs=x_second[:, s, t : t + P].bitcast(FP8X4),
+                                rhs_scale=x_planes[1][:, s, t : t + P],
+                                start=(s == 0),
+                                stop=(s == PASSES - 1),
+                            )
+                fresh = slice(HALF + a, HALF + a + n)
+                nc.vector.tensor_tensor(
+                    pairs[1][:, fresh, :],
+                    acc[:, 0 : 2 * n].rearrange("p (e n) -> p n e", e=2),
+                    late_acts[:, a // QUARTER, :, a % QUARTER : a % QUARTER + n].rearrange("p e n -> p n e"),
+                    MULT,
+                )
+                nc.gpsimd.tensor_copy(
+                    both[1][:].rearrange("p (e t) -> p e t", e=2)[:, :, fresh], pairs[1][:, fresh, :].rearrange("p t e -> p e t")
+                )
+                a = a + n
+
         opening = [psum.tile([P, HALF], F32, name="acc") for j in range(3)]
         for s in range(PASSES):
             for j in range(3):
@@ -223,14 +258,13 @@ def tile_moe_sup_glu_silu_kernel(
 
         gather(0, 0, 768)
         silu(3, 0)
-        silu(2, 1)
+        late_silu(0)
         product(2, 0)
         product(3, 0)
         pair_up(nc.gpsimd.tensor_copy, 1, 0, HALF)
-        silu(3, 1)
+        late_silu(1)
         gather(0, SHARED, LATE - SHARED)
-        product(2, 1)
-        last_product(1)
+        last_pair((256, 128, 128))
         gathered[LATE] = keep.tile([P, 2 * (SLOTS - LATE)], U32, name="late", tag="pairs0", align_bytes=64)
         for a, n in ((768, EARLY - 768), (EARLY, SHARED - EARLY), (LATE, SLOTS - LATE)):
             for j in range(2):

@@ -28,8 +28,9 @@ SLOTS = E * C
 TURNED = 512
 EARLY = 1024
 AHEAD = 256
-SHARED = 1376
-LATE = 1536
+SHARED = 1248
+LATE = 1376
+OWN = 1824
 
 
 def load_scale_rows(queues, plane, rows, which=range(4)):
@@ -163,7 +164,7 @@ def tile_moe_sup_glu_silu_kernel(
         both = [keep.tile([P, 2 * T], BF16, name="planes%d" % u, align_bytes=64) for u in range(2)]
         gathered = {
             0: keep.tile([P, 2 * EARLY], U32, name="gathered", tag="gathered", align_bytes=64),
-            EARLY: keep.tile([P, 2 * (LATE - EARLY)], U32, name="early", align_bytes=64),
+            EARLY: keep.tile([P, SHARED - EARLY + HALF], U32, name="early", align_bytes=64),
         }
 
         def plane_of(j):
@@ -171,7 +172,8 @@ def tile_moe_sup_glu_silu_kernel(
 
         def words_of(a, n):
             first = max(b for b in gathered if b <= a)
-            return gathered[first][:].rearrange("p (u n) -> p u n", u=2)[:, :, a - first : a - first + n]
+            held = min(b for b in (EARLY, LATE, SLOTS) if b > first) - first
+            return gathered[first][:, 0 : 2 * held].rearrange("p (u n) -> p u n", u=2)[:, :, a - first : a - first + n]
 
         def gather(u, a, n):
             window = pairs[u][:].rearrange("p t e -> p (t e)").bitcast(U32)
@@ -256,7 +258,7 @@ def tile_moe_sup_glu_silu_kernel(
         ident = keep.tile([P, P], F32, name="ident", tag="act0_0")
         make_identity(nc, ident[:])
 
-        gather(0, 0, 768)
+        gather(0, 0, 640)
         silu(3, 0)
         late_silu(0)
         product(2, 0)
@@ -266,7 +268,7 @@ def tile_moe_sup_glu_silu_kernel(
         gather(0, SHARED, LATE - SHARED)
         last_pair((256, 128, 128))
         gathered[LATE] = keep.tile([P, 2 * (SLOTS - LATE)], U32, name="late", tag="pairs0", align_bytes=64)
-        for a, n in ((768, EARLY - 768), (EARLY, SHARED - EARLY), (LATE, SLOTS - LATE)):
+        for a, n in ((640, EARLY - 640), (EARLY, SHARED - EARLY), (LATE, SLOTS - LATE)):
             for j in range(2):
                 gather_plane(j, a, n)
 
@@ -302,22 +304,22 @@ def tile_moe_sup_glu_silu_kernel(
             copy(y[:, a : a + n], acc[:, 0:n])
 
         made = {}
-        chunks = ((0, 256), (256, 384), (640, 384), (EARLY, LATE - EARLY))
-        for a, n in chunks:
+        chunks = ((0, 256), (256, 384), (640, 384))
+        for a, n in chunks + ((EARLY, LATE - EARLY), (OWN, SLOTS - OWN)):
             gather(1, a, n)
-        gather_plane(2, LATE, SLOTS - LATE)
-        gather_plane(3, LATE, 256)
-        gather_plane(3, LATE + 256, 256)
-        for a, n in chunks[:3]:
+        gather_plane(2, LATE, OWN - LATE)
+        gather_plane(3, LATE, 288)
+        gather_plane(3, LATE + 288, OWN - LATE - 288)
+        for a, n in chunks:
             weave(nc.gpsimd.tensor_copy, a, n)
-        for a, n in ((LATE, 256), (LATE + 256, 256)) + chunks[3:]:
+        for a, n in ((LATE, 288), (LATE + 288, OWN - LATE - 288), (EARLY, LATE - EARLY), (OWN, SLOTS - OWN)):
             weave(nc.scalar.copy, a, n)
         all_codes = keep.tile([P, SLOTS], U32, name="all_codes", tag="gathered", align_bytes=64)
-        for a, n in ((0, 256), (256, 256), (512, 256), (768, 256), (1536, 256), (1792, 256), (1024, 256), (1280, 128), (1408, 128)):
+        for a, n in ((0, 256), (256, 256), (512, 256), (768, 256), (1408, 256), (1664, 128), (1024, 256), (1280, 128), (1792, 128), (1920, 128)):
             quantise(a, n)
-        for a in (0, 512, 1536):
-            second_layer(a, HALF, nc.scalar.copy)
-        for a, n in ((1024, 256), (1280, 128), (1408, 128)):
+        for a, n in ((0, 512), (512, 512), (1408, 384)):
+            second_layer(a, n, nc.scalar.copy)
+        for a, n in ((1024, 384), (1792, 128), (1920, 128)):
             second_layer(a, n, nc.vector.tensor_copy)
 
         def slots_of(r, a, n):

@@ -23,19 +23,29 @@ P = 128
 PASSES = K // 512
 HALF = 512
 QUARTER = 256
-WARM_PASSES = 3
 SLOTS = E * C
+WARM_PASSES = 3
+OPENING_SUMS = 3
+
+FIRST = 640
+WOVEN_ASIDE = 1024
+SECOND = 896
+LATE = 1536
+ASIDE_PIECES = ((0, 256), (256, 384), (640, 384))
+LAST_WIDTHS = (256, 128, 128)
+QUANTISE_PIECES = (
+    (0, 256), (256, 256), (512, 256), (768, 256),
+    (1536, 256), (1792, 256),
+    (1024, 256), (1280, 128), (1408, 128),
+)
+SCALAR_BANKS = ((0, 512), (512, 512), (1536, 256))
+VECTOR_BANKS = ((1792, 256), (1024, 256), (1280, 128), (1408, 128))
 TURNED = 512
-EARLY = 1024
-AHEAD = 256
-SHARED = 1248
-LATE = 1376
-OWN = 1824
 
 
-def load_scale_rows(queues, plane, rows, which=range(4)):
-    for r in which:
-        queues[r].dma_start(out=plane[r:P:32, :, :].bitcast(I32), in_=rows[r])
+def load_scale_rows(nc, plane, rows):
+    for r in range(4):
+        nc.sync.dma_start(out=plane[r:P:32, :, :].bitcast(I32), in_=rows[r])
 
 
 def tile_moe_sup_glu_silu_kernel(
@@ -46,21 +56,21 @@ def tile_moe_sup_glu_silu_kernel(
         keep = ctx.enter_context(tc.tile_pool(name="keep", bufs=1))
         psum = ctx.enter_context(tc.psum_pool(name="psum", bufs=8))
 
-        offs_sb = keep.tile([P, E * C // 16], U16, name="offs_sb")
+        offs_sb = keep.tile([P, SLOTS // 16], U16, name="offs_sb")
         pos_sb = [keep.tile([P, T // 16], U16, name="pos_sb%d" % r) for r in range(2)]
 
         raw_scales = [keep.tile([P, PASSES, H], U8, name="raw_scales%d" % m, align_bytes=64) for m in range(2)]
         x_planes = [keep.tile([P, PASSES, HALF], U8, name="x_plane%d" % h, align_bytes=64) for h in range(2)]
         w2_plane = keep.tile([P, E, N], U8, name="w2_plane", align_bytes=64)
-        for plane in (raw_scales[0], x_planes[0], raw_scales[1], x_planes[1], w2_plane):
-            nc.vector.memset(plane[:].bitcast(I32), 0)
+        for scale_plane in (raw_scales[0], x_planes[0], raw_scales[1], x_planes[1], w2_plane):
+            nc.vector.memset(scale_plane[:].bitcast(I32), 0)
 
         w1_first = keep.tile([P, 1, H // 2], I32, name="w1_first", align_bytes=64)
         w1_rest = keep.tile([P, PASSES - 1, H // 2], I32, name="w1_rest", align_bytes=64)
         w3_raw = keep.tile([P, PASSES, H // 2], I32, name="w3_raw", align_bytes=64)
         x_first = [keep.tile([P, HALF], I32, name="x_first%d" % s, align_bytes=64) for s in range(PASSES)]
         x_second = keep.tile([P, PASSES, HALF], I32, name="x_second", align_bytes=64)
-        x_passes = [[t[:] for t in x_first], [x_second[:, s, :] for s in range(PASSES)]]
+        x_passes = [[words[:] for words in x_first], [x_second[:, s, :] for s in range(PASSES)]]
         w2_sb = keep.tile([P, E, N // 2], I32, name="w2_sb", align_bytes=64)
         gate_sb = [keep.tile([P, T - TURNED], F32, name="gate_sb%d" % r) for r in range(2)]
         gate_cols = [keep.tile([P, TURNED // P], F32, name="gate_cols%d" % r) for r in range(2)]
@@ -68,23 +78,21 @@ def tile_moe_sup_glu_silu_kernel(
         x_view = x_words.rearrange("s p t d -> p s (t d)").bitcast(I32)
         by_row = "a (q r) w -> r q a w"
         x_rows = x_scales.bitcast(I32).rearrange(by_row, r=4)
-        on_sync = [nc.sync] * 4
-        first_rows = x_rows[:, :, :, 0 : HALF // 4]
         w1_view = w1_words.bitcast(I32).rearrange("s p w -> p s w")
         nc.sync.dma_start(out=x_first[0][:, 0:P], in_=x_view[:, 0, 0:P])
         nc.sync.dma_start(out=w1_first[:], in_=w1_view[:, 0:1, :])
-        load_scale_rows(on_sync, raw_scales[0], w1_scales.bitcast(I32).rearrange(by_row, r=4))
+        load_scale_rows(nc, raw_scales[0], w1_scales.bitcast(I32).rearrange(by_row, r=4))
         nc.sync.dma_start(out=x_first[0][:, P:HALF], in_=x_view[:, 0, P:HALF])
         nc.sync.dma_start(out=w1_rest[:], in_=w1_view[:, 1:PASSES, :])
-        load_scale_rows(on_sync, x_planes[0], first_rows)
+        load_scale_rows(nc, x_planes[0], x_rows[:, :, :, 0 : HALF // 4])
         for s in range(1, PASSES):
             nc.sync.dma_start(out=x_first[s][:], in_=x_view[:, s, 0:HALF])
-        load_scale_rows(on_sync, raw_scales[1], w3_scales.bitcast(I32).rearrange(by_row, r=4))
+        load_scale_rows(nc, raw_scales[1], w3_scales.bitcast(I32).rearrange(by_row, r=4))
         nc.sync.dma_start(out=w3_raw[:], in_=w3_words.bitcast(I32).rearrange("s p w -> p s w"))
-        load_scale_rows(on_sync, x_planes[1], x_rows[:, :, :, HALF // 4 : T // 4])
+        load_scale_rows(nc, x_planes[1], x_rows[:, :, :, HALF // 4 : T // 4])
         nc.sync.dma_start(out=x_second[:], in_=x_view[:, :, HALF:T])
         nc.sync.dma_start(offs_sb[:], offs)
-        load_scale_rows(on_sync, w2_plane, w2_scales.bitcast(I32).rearrange("e o (q r) w -> r q (e o) w", r=4))
+        load_scale_rows(nc, w2_plane, w2_scales.bitcast(I32).rearrange("e o (q r) w -> r q (e o) w", r=4))
         nc.sync.dma_start(out=w2_sb[:], in_=w2_words.bitcast(I32).rearrange("e o p w -> p (e o) w"))
         nc.sync.dma_start(pos_sb[0][:], pos1)
         nc.sync.dma_start(pos_sb[1][:], pos2)
@@ -107,49 +115,49 @@ def tile_moe_sup_glu_silu_kernel(
             )
 
         picked_words = {}
-        picked_plane = {}
+        picked_scales = {}
 
-        def pick_plane(m, first, count, first_pass, passes):
-            name = "plane%d_%d_%d" % (m, first, first_pass)
-            plane = keep.tile([P, count, passes * P], U8, name=name, align_bytes=64)
+        def pick_scales(m, first, count, first_pass, passes):
+            name = "scales%d_%d_%d" % (m, first, first_pass)
+            picked = keep.tile([P, count, passes * P], U8, name=name, align_bytes=64)
             rows = raw_scales[m][:, first_pass : first_pass + passes, :]
             source = rows.rearrange("p s c -> p (s c)").rearrange("p (b i j) -> p b j i", i=16, j=4)
             nc.vector.tensor_copy(
-                out=plane[:].rearrange("p e (b i) -> p b e i", i=16), in_=source[:, :, first : first + count, :]
+                out=picked[:].rearrange("p e (b i) -> p b e i", i=16), in_=source[:, :, first : first + count, :]
             )
             for e in range(count):
                 for s in range(passes):
-                    picked_plane[(m, first + e, first_pass + s)] = plane[:, e, P * s : P * (s + 1)]
+                    picked_scales[(m, first + e, first_pass + s)] = picked[:, e, P * s : P * (s + 1)]
 
         def pick_words(raw, m, first, count, first_pass):
             passes = raw.shape[1]
-            words = keep.tile([P, count, passes * 2 * P], U8, name="words%d_%d_%d" % (m, first, first_pass), align_bytes=64)
-            flat = raw[:].bitcast(U16).rearrange("p s c -> p (s c)")
-            source = flat.rearrange("p (b i j) -> p b j i", i=8, j=4)
+            name = "words%d_%d_%d" % (m, first, first_pass)
+            picked = keep.tile([P, count, passes * 2 * P], U8, name=name, align_bytes=64)
+            source = raw[:].bitcast(U16).rearrange("p s c -> p (s c)").rearrange("p (b i j) -> p b j i", i=8, j=4)
             nc.vector.tensor_copy(
-                out=words[:].bitcast(U16).rearrange("p e (b i) -> p b e i", i=8),
+                out=picked[:].bitcast(U16).rearrange("p e (b i) -> p b e i", i=8),
                 in_=source[:, :, first : first + count, :],
             )
             for e in range(count):
                 for s in range(passes):
-                    picked_words[(m, first + e, first_pass + s)] = words[:, e, 2 * P * s : 2 * P * (s + 1)]
+                    picked_words[(m, first + e, first_pass + s)] = picked[:, e, 2 * P * s : 2 * P * (s + 1)]
 
         pick_words(w1_first, 0, 0, 4, 0)
-        pick_plane(0, 0, 4, 0, 1)
-        pick_plane(0, 0, 4, 1, 1)
+        pick_scales(0, 0, 4, 0, 1)
+        pick_scales(0, 0, 4, 1, 1)
         pick_words(w1_rest, 0, 0, 4, 1)
-        pick_plane(0, 0, 4, 2, 1)
-        pick_plane(1, 0, 2, 0, PASSES)
+        pick_scales(0, 0, 4, 2, 1)
+        pick_scales(1, 0, 2, 0, PASSES)
         pick_words(w3_raw, 1, 0, 1, 0)
         pick_words(w3_raw, 1, 1, 1, 0)
 
-        def first_layer_pass(acc, m, j, h, s):
+        def first_layer_pass(acc, m, j, h, s, a, n):
             nc.tensor.matmul_mx(
-                out=acc[:],
+                out=acc,
                 lhsT=picked_words[(m, j, s)].bitcast(FP4X4),
-                lhsT_scale=picked_plane[(m, j, s)],
-                rhs=x_passes[h][s].bitcast(FP8X4),
-                rhs_scale=x_planes[h][:, s, :],
+                lhsT_scale=picked_scales[(m, j, s)],
+                rhs=x_passes[h][s][:, a : a + n].bitcast(FP8X4),
+                rhs_scale=x_planes[h][:, s, a : a + n],
                 start=(s == 0),
                 stop=(s == PASSES - 1),
             )
@@ -157,33 +165,33 @@ def tile_moe_sup_glu_silu_kernel(
         def first_layer(m, j, h):
             acc = psum.tile([P, HALF], F32, name="acc")
             for s in range(PASSES):
-                first_layer_pass(acc, m, j, h, s)
+                first_layer_pass(acc[:], m, j, h, s, 0, HALF)
             return acc
 
         pairs = [keep.tile([P, T, 2], BF16, name="pairs%d" % u, tag="pairs%d" % u, align_bytes=64) for u in range(2)]
-        both = [keep.tile([P, 2 * T], BF16, name="planes%d" % u, align_bytes=64) for u in range(2)]
+        planes = [keep.tile([P, 2 * T], BF16, name="planes%d" % u, align_bytes=64) for u in range(2)]
         gathered = {
-            0: keep.tile([P, 2 * EARLY], U32, name="gathered", tag="gathered", align_bytes=64),
-            EARLY: keep.tile([P, SHARED - EARLY + HALF], U32, name="early", align_bytes=64),
+            0: keep.tile([P, 2 * WOVEN_ASIDE], U32, name="gathered", tag="gathered", align_bytes=64),
+            WOVEN_ASIDE: keep.tile([P, 2 * (LATE - WOVEN_ASIDE)], U32, name="gathered_mid", align_bytes=64),
         }
 
         def plane_of(j):
-            return both[j // 2][:, (j % 2) * T : (j % 2 + 1) * T]
+            return planes[j // 2][:, (j % 2) * T : (j % 2 + 1) * T]
 
         def words_of(a, n):
             first = max(b for b in gathered if b <= a)
-            held = min(b for b in (EARLY, LATE, SLOTS) if b > first) - first
+            held = min(b for b in (WOVEN_ASIDE, LATE, SLOTS) if b > first) - first
             return gathered[first][:, 0 : 2 * held].rearrange("p (u n) -> p u n", u=2)[:, :, a - first : a - first + n]
 
-        def gather(u, a, n):
+        def gather_pair(u, a, n):
             window = pairs[u][:].rearrange("p t e -> p (t e)").bitcast(U32)
             nc.vector.tensor_copy(words_of(a, n)[:, u, :], window.indirect(offs_sb[:, a // 16 : (a + n) // 16]))
 
         def gather_plane(j, a, n):
-            by_value = words_of(a, n)[:, j // 2, :].bitcast(BF16).rearrange("p (n e) -> p n e", e=2)
-            nc.scalar.activation(by_value[:, :, j % 2], plane_of(j).indirect(offs_sb[:, a // 16 : (a + n) // 16]), COPY)
+            halves = words_of(a, n)[:, j // 2, :].bitcast(BF16).rearrange("p (n e) -> p n e", e=2)
+            nc.scalar.activation(halves[:, :, j % 2], plane_of(j).indirect(offs_sb[:, a // 16 : (a + n) // 16]), COPY)
 
-        acts = {(3, 0): gathered[EARLY][:, SHARED - EARLY : SHARED - EARLY + HALF].bitcast(F32)}
+        acts = {(3, 0): gathered[0][:, SECOND : SECOND + HALF].bitcast(F32)}
 
         def silu_of(j, h, acc):
             if (j, h) not in acts:
@@ -199,12 +207,7 @@ def tile_moe_sup_glu_silu_kernel(
                 nc.vector.tensor_tensor(plane_of(j)[:, h * HALF + a : h * HALF + b], acc[:, a:b], acts[(j, h)][:, a:b], MULT)
 
         def pair_up(copy, u, a, n):
-            copy(pairs[u][:, a : a + n, :], both[u][:].rearrange("p (e t) -> p t e", e=2)[:, a : a + n, :])
-
-        def last_product(u):
-            product(2 * u + 1, 1, (0, AHEAD, HALF))
-            pair_up(nc.vector.tensor_copy, u, HALF, AHEAD)
-            pair_up(nc.vector.tensor_copy, u, HALF + AHEAD, HALF - AHEAD)
+            copy(pairs[u][:, a : a + n, :], planes[u][:].rearrange("p (e t) -> p t e", e=2)[:, a : a + n, :])
 
         late_acts = keep.tile([P, 2, 2, QUARTER], F32, name="late_acts")
 
@@ -212,22 +215,14 @@ def tile_moe_sup_glu_silu_kernel(
             sums = first_layer(0, 2 + e, 1)[:].rearrange("p (b n) -> p b n", b=2)
             nc.scalar.activation(late_acts[:, :, e, :], sums, SILU)
 
-        def last_pair(widths):
+        def late_products():
             a = 0
-            for n in widths:
+            for n in LAST_WIDTHS:
                 acc = psum.tile([P, HALF], F32, name="acc")
                 for e in range(2):
-                    for t in range(a, a + n, P):
+                    for t in range(0, n, P):
                         for s in range(PASSES):
-                            nc.tensor.matmul_mx(
-                                out=acc[:, e * n + t - a : e * n + t - a + P],
-                                lhsT=picked_words[(1, 2 + e, s)].bitcast(FP4X4),
-                                lhsT_scale=picked_plane[(1, 2 + e, s)],
-                                rhs=x_second[:, s, t : t + P].bitcast(FP8X4),
-                                rhs_scale=x_planes[1][:, s, t : t + P],
-                                start=(s == 0),
-                                stop=(s == PASSES - 1),
-                            )
+                            first_layer_pass(acc[:, e * n + t : e * n + t + P], 1, 2 + e, 1, s, a + t, P)
                 fresh = slice(HALF + a, HALF + a + n)
                 nc.vector.tensor_tensor(
                     pairs[1][:, fresh, :],
@@ -236,41 +231,54 @@ def tile_moe_sup_glu_silu_kernel(
                     MULT,
                 )
                 nc.gpsimd.tensor_copy(
-                    both[1][:].rearrange("p (e t) -> p e t", e=2)[:, :, fresh], pairs[1][:, fresh, :].rearrange("p t e -> p e t")
+                    planes[1][:].rearrange("p (e t) -> p e t", e=2)[:, :, fresh],
+                    pairs[1][:, fresh, :].rearrange("p t e -> p e t"),
                 )
                 a = a + n
 
-        opening = [psum.tile([P, HALF], F32, name="acc") for j in range(3)]
+        opening = [psum.tile([P, HALF], F32, name="acc") for j in range(OPENING_SUMS)]
         for s in range(PASSES):
-            for j in range(3):
-                first_layer_pass(opening[j], 0, j, 0, s)
-        for j in range(3):
+            for j in range(OPENING_SUMS):
+                first_layer_pass(opening[j][:], 0, j, 0, s, 0, HALF)
+        for j in range(OPENING_SUMS):
             silu_of(j, 0, opening[j])
         product(0, 0)
         product(1, 0)
         pair_up(nc.vector.tensor_copy, 0, 0, HALF)
         silu(0, 1)
-        silu(1, 1)
         product(0, 1)
-        last_product(0)
+        ahead_offs = offs_sb[:, FIRST // 16 : SECOND // 16]
+        singles = keep.tile([P, 5 * P], BF16, name="singles")
+        blocks = singles[:].rearrange("p (b n) -> p b n", n=P)
+        nc.vector.tensor_copy(singles[:, 0 : 2 * P], planes[0][:].indirect(ahead_offs))
+        silu(1, 1)
+        product(1, 1, (0, QUARTER, HALF))
+        pair_up(nc.vector.tensor_copy, 0, HALF, QUARTER)
+        pair_up(nc.vector.tensor_copy, 0, HALF + QUARTER, QUARTER)
         pick_words(w3_raw, 1, 2, 2, 0)
-        pick_plane(1, 2, 2, 0, PASSES)
+        pick_scales(1, 2, 2, 0, PASSES)
         ident = keep.tile([P, P], F32, name="ident", tag="act0_0")
         make_identity(nc, ident[:])
 
-        gather(0, 0, 640)
+        gather_pair(0, 0, FIRST)
+        gather_plane(0, WOVEN_ASIDE, P)
+        gather_plane(0, WOVEN_ASIDE + P, LATE - WOVEN_ASIDE - P)
+        nc.scalar.activation(blocks[:, 2:5:2, :], plane_of(1).indirect(ahead_offs), COPY)
+        for b in range(2):
+            words = words_of(FIRST + b * P, P)[:, 0, :].bitcast(BF16).rearrange("p (n e) -> p n e", e=2)
+            nc.gpsimd.tensor_copy(words, blocks[:, b : 3 + 2 * b : 2 + b, :].rearrange("p e n -> p n e"))
         silu(3, 0)
         late_silu(0)
         product(2, 0)
         product(3, 0)
         pair_up(nc.gpsimd.tensor_copy, 1, 0, HALF)
         late_silu(1)
-        gather(0, SHARED, LATE - SHARED)
-        last_pair((256, 128, 128))
-        gathered[LATE] = keep.tile([P, 2 * (SLOTS - LATE)], U32, name="late", tag="pairs0", align_bytes=64)
-        for a, n in ((640, EARLY - 640), (EARLY, SHARED - EARLY), (LATE, SLOTS - LATE)):
-            for j in range(2):
-                gather_plane(j, a, n)
+        gather_pair(0, SECOND, WOVEN_ASIDE - SECOND)
+        late_products()
+        gathered[LATE] = keep.tile([P, 2 * (SLOTS - LATE)], U32, name="gathered_late", tag="pairs0", align_bytes=64)
+        gather_plane(1, WOVEN_ASIDE, LATE - WOVEN_ASIDE)
+        for j in range(2):
+            gather_plane(j, LATE, SLOTS - LATE)
 
         woven = keep.tile([P, 2 * SLOTS], U32, name="woven", align_bytes=64)
 
@@ -279,14 +287,28 @@ def tile_moe_sup_glu_silu_kernel(
             copy(target.rearrange("p (n u) -> p n u", u=2), words_of(a, n).rearrange("p u n -> p n u"))
 
         y = keep.tile([P, SLOTS], F32, name="y")
+        quantised = {}
 
-        def quantise(a, n):
-            codes = all_codes[:, a : a + n]
-            h_plane = keep.tile([P, n], U8, name="h_plane%d" % a, align_bytes=64)
-            source = woven[:, 2 * a : 2 * (a + n)]
-            nc.vector.quantize_mx(out=codes.bitcast(FP8X4), scales=h_plane[:], in_=source.bitcast(BF16))
+        vector_rest = ((WOVEN_ASIDE, QUARTER), (WOVEN_ASIDE + QUARTER, QUARTER))
+        own_pieces = ((LATE, QUARTER), (LATE + QUARTER, QUARTER))
+        for a, n in ASIDE_PIECES + ((WOVEN_ASIDE, LATE - WOVEN_ASIDE),):
+            gather_pair(1, a, n)
+        gather_plane(2, LATE, SLOTS - LATE)
+        for a, n in own_pieces:
+            gather_plane(3, a, n)
+        for a, n in ASIDE_PIECES:
+            weave(nc.gpsimd.tensor_copy, a, n)
+        for a, n in own_pieces + vector_rest:
+            weave(nc.scalar.copy, a, n)
+
+        codes = keep.tile([P, SLOTS], U32, name="codes", tag="gathered", align_bytes=64)
+        for a, n in QUANTISE_PIECES:
+            h_scales = keep.tile([P, n], U8, name="h_scales%d" % a, align_bytes=64)
+            nc.vector.quantize_mx(
+                out=codes[:, a : a + n].bitcast(FP8X4), scales=h_scales[:], in_=woven[:, 2 * a : 2 * (a + n)].bitcast(BF16)
+            )
             for k in range(n // C):
-                made[a // C + k] = (codes[:, k * C : (k + 1) * C], h_plane[:, k * C : (k + 1) * C])
+                quantised[a // C + k] = (codes[:, a + k * C : a + (k + 1) * C], h_scales[:, k * C : (k + 1) * C])
 
         def second_layer(a, n, copy):
             acc = psum.tile([P, HALF], F32, name="acc")
@@ -296,30 +318,16 @@ def tile_moe_sup_glu_silu_kernel(
                     out=acc[:, k * C : (k + 1) * C],
                     lhsT=w2_sb[:, e, :].bitcast(FP4X4),
                     lhsT_scale=w2_plane[:, e, :],
-                    rhs=made[e][0].bitcast(FP8X4),
-                    rhs_scale=made[e][1],
+                    rhs=quantised[e][0].bitcast(FP8X4),
+                    rhs_scale=quantised[e][1],
                     start=True,
                     stop=True,
                 )
             copy(y[:, a : a + n], acc[:, 0:n])
 
-        made = {}
-        chunks = ((0, 256), (256, 384), (640, 384))
-        for a, n in chunks + ((EARLY, LATE - EARLY), (OWN, SLOTS - OWN)):
-            gather(1, a, n)
-        gather_plane(2, LATE, OWN - LATE)
-        gather_plane(3, LATE, 288)
-        gather_plane(3, LATE + 288, OWN - LATE - 288)
-        for a, n in chunks:
-            weave(nc.gpsimd.tensor_copy, a, n)
-        for a, n in ((LATE, 288), (LATE + 288, OWN - LATE - 288), (EARLY, LATE - EARLY), (OWN, SLOTS - OWN)):
-            weave(nc.scalar.copy, a, n)
-        all_codes = keep.tile([P, SLOTS], U32, name="all_codes", tag="gathered", align_bytes=64)
-        for a, n in ((0, 256), (256, 256), (512, 256), (768, 256), (1408, 256), (1664, 128), (1024, 256), (1280, 128), (1792, 128), (1920, 128)):
-            quantise(a, n)
-        for a, n in ((0, 512), (512, 512), (1408, 384)):
+        for a, n in SCALAR_BANKS:
             second_layer(a, n, nc.scalar.copy)
-        for a, n in ((1024, 384), (1792, 128), (1920, 128)):
+        for a, n in VECTOR_BANKS:
             second_layer(a, n, nc.vector.tensor_copy)
 
         def slots_of(r, a, n):
@@ -337,22 +345,22 @@ def tile_moe_sup_glu_silu_kernel(
                 nc.scalar.activation(weighed[:, t : t + P], turned[:, t : t + P], COPY, scale=gate_cols[r][:, c : c + 1])
             return weighed
 
-        def turn_back(a, n, shares):
+        def turn_back(a, n, weighed):
             acc = psum.tile([P, HALF], F32, name="acc")
             for t in range(0, n, P):
                 for r in range(2):
                     nc.tensor.matmul(
-                        acc[:, t : t + P], shares[r][:, t : t + P], ident[:], start=(r == 0), stop=(r == 1), is_transpose=True
+                        acc[:, t : t + P], weighed[r][:, t : t + P], ident[:], start=(r == 0), stop=(r == 1), is_transpose=True
                     )
             total = keep.tile([P, n], F32, name="total%d" % a)
             nc.scalar.copy(total[:], acc[:, 0:n])
             nc.scalar.dma_start(out=out[:, a : a + n], in_=total[:])
 
         nc.vector.tensor_copy(fetched[0][:], slots_of(0, 0, TURNED))
-        first = turn_and_weigh(0, 0, TURNED)
-        for a in range(0, TURNED, 256):
-            nc.vector.tensor_copy(fetched[1][:, a : a + 256], slots_of(1, a, 256))
-            turn_back(a, 256, [first[:, a : a + 256], turn_and_weigh(1, a, 256)[:]])
+        first_choice = turn_and_weigh(0, 0, TURNED)
+        for a in range(0, TURNED, QUARTER):
+            nc.vector.tensor_copy(fetched[1][:, a : a + QUARTER], slots_of(1, a, QUARTER))
+            turn_back(a, QUARTER, [first_choice[:, a : a + QUARTER], turn_and_weigh(1, a, QUARTER)[:]])
 
         shares = [keep.tile([P, T - TURNED], F32, name="share%d" % r) for r in range(2)]
 
@@ -364,10 +372,10 @@ def tile_moe_sup_glu_silu_kernel(
             nc.vector.tensor_tensor(total[:], shares[0][:, a : a + n], shares[1][:, a : a + n], ADD)
             nc.sync.dma_start(out=out[:, TURNED + a : TURNED + a + n], in_=total[:])
 
-        weighted(0, 0, 512)
-        weighted(1, 0, 256)
-        weighted(1, 256, 128)
-        combine(0, 256)
-        weighted(1, 384, 128)
-        combine(256, 128)
-        combine(384, 128)
+        weighted(0, 0, T - TURNED)
+        weighted(1, 0, QUARTER)
+        weighted(1, QUARTER, P)
+        combine(0, QUARTER)
+        weighted(1, QUARTER + P, P)
+        combine(QUARTER, P)
+        combine(QUARTER + P, P)

@@ -1,7 +1,6 @@
 from contextlib import ExitStack
 
 import concourse.mybir as mybir
-from concourse.masks import make_identity
 
 K, T, E, C, H, N = 1536, 1024, 16, 128, 512, 128
 FLOPS = 2 * (2 * K * H * T + H * N * E * C)
@@ -40,7 +39,7 @@ QUANTISE_PIECES = (
 )
 SCALAR_BANKS = ((0, 512), (512, 512), (1536, 256))
 VECTOR_BANKS = ((1792, 256), (1024, 256), (1280, 128), (1408, 128))
-TURNED = 512
+FUSED = 768
 
 
 def load_scale_rows(nc, plane, rows):
@@ -72,8 +71,7 @@ def tile_moe_sup_glu_silu_kernel(
         x_second = keep.tile([P, PASSES, HALF], I32, name="x_second", align_bytes=64)
         x_passes = [[words[:] for words in x_first], [x_second[:, s, :] for s in range(PASSES)]]
         w2_sb = keep.tile([P, E, N // 2], I32, name="w2_sb", align_bytes=64)
-        gate_sb = [keep.tile([P, T - TURNED], F32, name="gate_sb%d" % r) for r in range(2)]
-        gate_cols = [keep.tile([P, TURNED // P], F32, name="gate_cols%d" % r) for r in range(2)]
+        gate_sb = keep.tile([P, 2, T], F32, name="gate_sb")
 
         x_view = x_words.rearrange("s p t d -> p s (t d)").bitcast(I32)
         by_row = "a (q r) w -> r q a w"
@@ -96,11 +94,7 @@ def tile_moe_sup_glu_silu_kernel(
         nc.sync.dma_start(out=w2_sb[:], in_=w2_words.bitcast(I32).rearrange("e o p w -> p (e o) w"))
         nc.sync.dma_start(pos_sb[0][:], pos1)
         nc.sync.dma_start(pos_sb[1][:], pos2)
-        for r in range(2):
-            nc.sync.dma_start(out=gate_sb[r][:], in_=gate[r, :, TURNED:T])
-        with nc.allow_non_contiguous_dma(reason="one gate value a partition"):
-            for r in range(2):
-                nc.sync.dma_start(out=gate_cols[r][:], in_=gate[r, 0, 0:TURNED].rearrange("(c p) -> p c", p=P))
+        nc.sync.dma_start(out=gate_sb[:], in_=gate.rearrange("r p t -> p r t"))
 
         warm_acc = psum.tile([P, HALF], F32, name="acc")
         for k in range(WARM_PASSES):
@@ -257,8 +251,6 @@ def tile_moe_sup_glu_silu_kernel(
         pair_up(nc.vector.tensor_copy, 0, HALF + QUARTER, QUARTER)
         pick_words(w3_raw, 1, 2, 2, 0)
         pick_scales(1, 2, 2, 0, PASSES)
-        ident = keep.tile([P, P], F32, name="ident", tag="act0_0")
-        make_identity(nc, ident[:])
 
         gather_pair(0, 0, FIRST)
         gather_plane(0, WOVEN_ASIDE, P)
@@ -333,49 +325,34 @@ def tile_moe_sup_glu_silu_kernel(
         def slots_of(r, a, n):
             return y[:].indirect(pos_sb[r][:, a // 16 : (a + n) // 16])
 
-        fetched = [keep.tile([P, TURNED], F32, name="fetched%d" % r) for r in range(2)]
+        fetched = keep.tile([P, 2, T], F32, name="fetched")
+        shares = keep.tile([P, 2, T], F32, name="shares")
 
-        def turn_and_weigh(r, a, n):
-            turned = psum.tile([P, HALF], F32, name="acc")
-            for t in range(0, n, P):
-                nc.tensor.transpose(turned[:, t : t + P], fetched[r][:, a + t : a + t + P], ident[:])
-            weighed = keep.tile([P, n], F32, name="weighed%d_%d" % (r, a))
-            for t in range(0, n, P):
-                c = (a + t) // P
-                nc.scalar.activation(weighed[:, t : t + P], turned[:, t : t + P], COPY, scale=gate_cols[r][:, c : c + 1])
-            return weighed
+        def fused(a, n):
+            nc.vector.tensor_tensor(shares[:, 0, a : a + n], slots_of(0, a, n), gate_sb[:, 0, a : a + n], MULT)
 
-        def turn_back(a, n, weighed):
-            acc = psum.tile([P, HALF], F32, name="acc")
-            for t in range(0, n, P):
-                for r in range(2):
-                    nc.tensor.matmul(
-                        acc[:, t : t + P], weighed[r][:, t : t + P], ident[:], start=(r == 0), stop=(r == 1), is_transpose=True
-                    )
-            total = keep.tile([P, n], F32, name="total%d" % a)
-            nc.scalar.copy(total[:], acc[:, 0:n])
-            nc.scalar.dma_start(out=out[:, a : a + n], in_=total[:])
+        def fetch(r, a, n):
+            nc.scalar.activation(fetched[:, r, a : a + n], slots_of(r, a, n), COPY)
 
-        nc.vector.tensor_copy(fetched[0][:], slots_of(0, 0, TURNED))
-        first_choice = turn_and_weigh(0, 0, TURNED)
-        for a in range(0, TURNED, QUARTER):
-            nc.vector.tensor_copy(fetched[1][:, a : a + QUARTER], slots_of(1, a, QUARTER))
-            turn_back(a, QUARTER, [first_choice[:, a : a + QUARTER], turn_and_weigh(1, a, QUARTER)[:]])
-
-        shares = [keep.tile([P, T - TURNED], F32, name="share%d" % r) for r in range(2)]
-
-        def weighted(r, a, n):
-            nc.vector.tensor_tensor(shares[r][:, a : a + n], slots_of(r, TURNED + a, n), gate_sb[r][:, a : a + n], MULT)
+        def weigh(r, a, n):
+            nc.vector.tensor_tensor(shares[:, r, a : a + n], fetched[:, r, a : a + n], gate_sb[:, r, a : a + n], MULT)
 
         def combine(a, n):
-            total = keep.tile([P, n], F32, name="total%d" % (TURNED + a))
-            nc.vector.tensor_tensor(total[:], shares[0][:, a : a + n], shares[1][:, a : a + n], ADD)
-            nc.sync.dma_start(out=out[:, TURNED + a : TURNED + a + n], in_=total[:])
+            total = keep.tile([P, n], F32, name="total%d" % a)
+            nc.vector.tensor_tensor(total[:], shares[:, 0, a : a + n], shares[:, 1, a : a + n], ADD)
+            nc.sync.dma_start(out=out[:, a : a + n], in_=total[:])
 
-        weighted(0, 0, T - TURNED)
-        weighted(1, 0, QUARTER)
-        weighted(1, QUARTER, P)
-        combine(0, QUARTER)
-        weighted(1, QUARTER + P, P)
-        combine(QUARTER, P)
-        combine(QUARTER + P, P)
+        piece = FUSED // 2
+        fused(0, piece)
+        fused(piece, piece)
+        fetch(1, 0, piece)
+        fetch(1, piece, piece)
+        fetch(0, FUSED, T - FUSED)
+        fetch(1, FUSED, T - FUSED)
+        weigh(1, 0, piece)
+        weigh(1, piece, piece)
+        combine(0, piece)
+        weigh(0, FUSED, T - FUSED)
+        weigh(1, FUSED, T - FUSED)
+        combine(piece, piece)
+        combine(FUSED, T - FUSED)

@@ -26,19 +26,19 @@ SLOTS = E * C
 WARM_PASSES = 3
 OPENING_SUMS = 3
 
-FIRST = 640
+FIRST = 384
 WOVEN_ASIDE = 1024
-SECOND = 896
+MIDDLE = 1408
 LATE = 1536
 ASIDE_PIECES = ((0, 256), (256, 384), (640, 384))
 LAST_WIDTHS = (256, 128, 128)
 QUANTISE_PIECES = (
     (0, 256), (256, 256), (512, 256), (768, 256),
-    (1536, 256), (1792, 256),
-    (1024, 256), (1280, 128), (1408, 128),
+    (1024, 256), (1536, 256), (1792, 256),
+    (1280, 128), (1408, 128),
 )
-SCALAR_BANKS = ((0, 512), (512, 512), (1536, 256))
-VECTOR_BANKS = ((1792, 256), (1024, 256), (1280, 128), (1408, 128))
+SCALAR_BANKS = ((0, 512), (512, 512), (1024, 256), (1536, 256))
+VECTOR_BANKS = ((1792, 256), (1280, 128), (1408, 128))
 FUSED = 768
 
 
@@ -108,16 +108,23 @@ def tile_moe_sup_glu_silu_kernel(
                 stop=True,
             )
 
+        gathered = {}
+
+        def make_gathered(first, last, tag):
+            gathered[first] = keep.tile([P, 2 * (last - first)], U32, name="gathered%d" % first, tag=tag, align_bytes=64)
+
+        make_gathered(0, WOVEN_ASIDE, "gathered0")
+
         picked_words = {}
         picked_scales = {}
 
         def pick_scales(m, first, count, first_pass, passes):
             name = "scales%d_%d_%d" % (m, first, first_pass)
-            picked = keep.tile([P, count, passes * P], U8, name=name, align_bytes=64)
+            picked = keep.tile([P, count, passes * P], U8, name=name, tag=name, align_bytes=64)
             rows = raw_scales[m][:, first_pass : first_pass + passes, :]
             source = rows.rearrange("p s c -> p (s c)").rearrange("p (b i j) -> p b j i", i=16, j=4)
             nc.vector.tensor_copy(
-                out=picked[:].rearrange("p e (b i) -> p b e i", i=16), in_=source[:, :, first : first + count, :]
+                out=picked[:, :, :].rearrange("p e (b i) -> p b e i", i=16), in_=source[:, :, first : first + count, :]
             )
             for e in range(count):
                 for s in range(passes):
@@ -140,7 +147,8 @@ def tile_moe_sup_glu_silu_kernel(
         pick_scales(0, 0, 4, 0, 1)
         pick_scales(0, 0, 4, 1, 1)
         pick_words(w1_rest, 0, 0, 4, 1)
-        pick_scales(0, 0, 4, 2, 1)
+        for j in range(4):
+            pick_scales(0, j, 1, 2, 1)
         pick_scales(1, 0, 2, 0, PASSES)
         pick_words(w3_raw, 1, 0, 1, 0)
         pick_words(w3_raw, 1, 1, 1, 0)
@@ -156,26 +164,20 @@ def tile_moe_sup_glu_silu_kernel(
                 stop=(s == PASSES - 1),
             )
 
-        def first_layer(m, j, h):
+        def first_layer(m, j, h, a=0, n=HALF):
             acc = psum.tile([P, HALF], F32, name="acc")
             for s in range(PASSES):
-                first_layer_pass(acc[:], m, j, h, s, 0, HALF)
+                first_layer_pass(acc[:, 0:n], m, j, h, s, a, n)
             return acc
 
         pairs = [keep.tile([P, T, 2], BF16, name="pairs%d" % u, tag="pairs%d" % u, align_bytes=64) for u in range(2)]
         planes = [keep.tile([P, 2 * T], BF16, name="planes%d" % u, align_bytes=64) for u in range(2)]
-        gathered = {
-            0: keep.tile([P, 2 * WOVEN_ASIDE], U32, name="gathered", tag="gathered", align_bytes=64),
-            WOVEN_ASIDE: keep.tile([P, 2 * (LATE - WOVEN_ASIDE)], U32, name="gathered_mid", align_bytes=64),
-        }
-
         def plane_of(j):
             return planes[j // 2][:, (j % 2) * T : (j % 2 + 1) * T]
 
         def words_of(a, n):
             first = max(b for b in gathered if b <= a)
-            held = min(b for b in (WOVEN_ASIDE, LATE, SLOTS) if b > first) - first
-            return gathered[first][:, 0 : 2 * held].rearrange("p (u n) -> p u n", u=2)[:, :, a - first : a - first + n]
+            return gathered[first][:].rearrange("p (u n) -> p u n", u=2)[:, :, a - first : a - first + n]
 
         def gather_pair(u, a, n):
             window = pairs[u][:].rearrange("p t e -> p (t e)").bitcast(U32)
@@ -185,20 +187,19 @@ def tile_moe_sup_glu_silu_kernel(
             halves = words_of(a, n)[:, j // 2, :].bitcast(BF16).rearrange("p (n e) -> p n e", e=2)
             nc.scalar.activation(halves[:, :, j % 2], plane_of(j).indirect(offs_sb[:, a // 16 : (a + n) // 16]), COPY)
 
-        acts = {(3, 0): gathered[0][:, SECOND : SECOND + HALF].bitcast(F32)}
+        acts = {(3, 0): gathered[0][:, FIRST : FIRST + HALF].bitcast(F32)}
 
         def silu_of(j, h, acc):
             if (j, h) not in acts:
-                acts[(j, h)] = keep.tile([P, HALF], F32, name="act%d_%d" % (j, h), tag="act%d_%d" % (j, h))[:]
+                acts[(j, h)] = keep.tile([P, HALF], F32, name="act%d_%d" % (j, h), tag="act%d_%d" % (j, h), align_bytes=64)[:]
             nc.scalar.activation(acts[(j, h)], acc[:], SILU)
 
         def silu(j, h):
             silu_of(j, h, first_layer(0, j, h))
 
-        def product(j, h, cuts=(0, HALF)):
+        def product(j, h):
             acc = first_layer(1, j, h)
-            for a, b in zip(cuts, cuts[1:]):
-                nc.vector.tensor_tensor(plane_of(j)[:, h * HALF + a : h * HALF + b], acc[:, a:b], acts[(j, h)][:, a:b], MULT)
+            nc.vector.tensor_tensor(plane_of(j)[:, h * HALF : (h + 1) * HALF], acc[:], acts[(j, h)], MULT)
 
         def pair_up(copy, u, a, n):
             copy(pairs[u][:, a : a + n, :], planes[u][:].rearrange("p (e t) -> p t e", e=2)[:, a : a + n, :])
@@ -214,9 +215,8 @@ def tile_moe_sup_glu_silu_kernel(
             for n in LAST_WIDTHS:
                 acc = psum.tile([P, HALF], F32, name="acc")
                 for e in range(2):
-                    for t in range(0, n, P):
-                        for s in range(PASSES):
-                            first_layer_pass(acc[:, e * n + t : e * n + t + P], 1, 2 + e, 1, s, a + t, P)
+                    for s in range(PASSES):
+                        first_layer_pass(acc[:, e * n : (e + 1) * n], 1, 2 + e, 1, s, a, n)
                 fresh = slice(HALF + a, HALF + a + n)
                 nc.vector.tensor_tensor(
                     pairs[1][:, fresh, :],
@@ -241,34 +241,31 @@ def tile_moe_sup_glu_silu_kernel(
         pair_up(nc.vector.tensor_copy, 0, 0, HALF)
         silu(0, 1)
         product(0, 1)
-        ahead_offs = offs_sb[:, FIRST // 16 : SECOND // 16]
-        singles = keep.tile([P, 5 * P], BF16, name="singles")
-        blocks = singles[:].rearrange("p (b n) -> p b n", n=P)
-        nc.vector.tensor_copy(singles[:, 0 : 2 * P], planes[0][:].indirect(ahead_offs))
-        silu(1, 1)
-        product(1, 1, (0, QUARTER, HALF))
-        pair_up(nc.vector.tensor_copy, 0, HALF, QUARTER)
-        pair_up(nc.vector.tensor_copy, 0, HALF + QUARTER, QUARTER)
+        nc.vector.tensor_copy(pairs[0][:, HALF:T, 0], plane_of(0)[:, HALF:T])
+        for a in (0, QUARTER):
+            act = keep.tile([P, QUARTER], F32, name="act_quarter%d" % a)
+            nc.scalar.activation(act[:], first_layer(0, 1, 1, a, QUARTER)[:, 0:QUARTER], SILU)
+            fresh = slice(HALF + a, HALF + a + QUARTER)
+            nc.vector.tensor_tensor(pairs[0][:, fresh, 1], first_layer(1, 1, 1, a, QUARTER)[:, 0:QUARTER], act[:], MULT)
+            nc.gpsimd.tensor_copy(plane_of(1)[:, fresh], pairs[0][:, fresh, 1])
         pick_words(w3_raw, 1, 2, 2, 0)
         pick_scales(1, 2, 2, 0, PASSES)
 
+        make_gathered(WOVEN_ASIDE, MIDDLE, "scales0_1_2")
         gather_pair(0, 0, FIRST)
-        gather_plane(0, WOVEN_ASIDE, P)
-        gather_plane(0, WOVEN_ASIDE + P, LATE - WOVEN_ASIDE - P)
-        nc.scalar.activation(blocks[:, 2:5:2, :], plane_of(1).indirect(ahead_offs), COPY)
-        for b in range(2):
-            words = words_of(FIRST + b * P, P)[:, 0, :].bitcast(BF16).rearrange("p (n e) -> p n e", e=2)
-            nc.gpsimd.tensor_copy(words, blocks[:, b : 3 + 2 * b : 2 + b, :].rearrange("p e n -> p n e"))
         silu(3, 0)
-        late_silu(0)
         product(2, 0)
+        make_gathered(MIDDLE, LATE, "act2_0")
         product(3, 0)
         pair_up(nc.gpsimd.tensor_copy, 1, 0, HALF)
+        late_silu(0)
         late_silu(1)
-        gather_pair(0, SECOND, WOVEN_ASIDE - SECOND)
+        for a, b in ((WOVEN_ASIDE, MIDDLE), (MIDDLE, LATE)):
+            for j in range(2):
+                gather_plane(j, a, b - a)
+        gather_pair(0, FIRST, WOVEN_ASIDE - FIRST)
         late_products()
-        gathered[LATE] = keep.tile([P, 2 * (SLOTS - LATE)], U32, name="gathered_late", tag="pairs0", align_bytes=64)
-        gather_plane(1, WOVEN_ASIDE, LATE - WOVEN_ASIDE)
+        make_gathered(LATE, SLOTS, "scales0_3_2")
         for j in range(2):
             gather_plane(j, LATE, SLOTS - LATE)
 
@@ -281,19 +278,18 @@ def tile_moe_sup_glu_silu_kernel(
         y = keep.tile([P, SLOTS], F32, name="y")
         quantised = {}
 
-        vector_rest = ((WOVEN_ASIDE, QUARTER), (WOVEN_ASIDE + QUARTER, QUARTER))
-        own_pieces = ((LATE, QUARTER), (LATE + QUARTER, QUARTER))
-        for a, n in ASIDE_PIECES + ((WOVEN_ASIDE, LATE - WOVEN_ASIDE),):
+        for a, n in ASIDE_PIECES + ((WOVEN_ASIDE, MIDDLE - WOVEN_ASIDE), (MIDDLE, LATE - MIDDLE)):
             gather_pair(1, a, n)
+        weave(nc.vector.tensor_copy, WOVEN_ASIDE, QUARTER)
         gather_plane(2, LATE, SLOTS - LATE)
-        for a, n in own_pieces:
-            gather_plane(3, a, n)
+        for a in (LATE, LATE + QUARTER):
+            gather_plane(3, a, QUARTER)
         for a, n in ASIDE_PIECES:
             weave(nc.gpsimd.tensor_copy, a, n)
-        for a, n in own_pieces + vector_rest:
+        for a, n in ((LATE, QUARTER), (LATE + QUARTER, QUARTER), (WOVEN_ASIDE + QUARTER, P), (MIDDLE, P)):
             weave(nc.scalar.copy, a, n)
 
-        codes = keep.tile([P, SLOTS], U32, name="codes", tag="gathered", align_bytes=64)
+        codes = keep.tile([P, SLOTS], U32, name="codes", tag="gathered0", align_bytes=64)
         for a, n in QUANTISE_PIECES:
             h_scales = keep.tile([P, n], U8, name="h_scales%d" % a, align_bytes=64)
             nc.vector.quantize_mx(

@@ -88,7 +88,8 @@ def tile_moe_sup_glu_silu_kernel(
         load_scale_rows(nc, raw_scales[1], w3_scales.bitcast(I32).rearrange(by_row, r=4))
         nc.sync.dma_start(out=w3_raw[:], in_=w3_words.bitcast(I32).rearrange("s p w -> p s w"))
         load_scale_rows(nc, x_planes[1], x_rows[:, :, :, HALF // 4 : T // 4])
-        nc.sync.dma_start(out=x_second[:], in_=x_view[:, :, HALF:T])
+        for a in (0, QUARTER):
+            nc.sync.dma_start(out=x_second[:, :, a : a + QUARTER], in_=x_view[:, :, HALF + a : HALF + a + QUARTER])
         nc.sync.dma_start(offs_sb[:], offs)
         load_scale_rows(nc, w2_plane, w2_scales.bitcast(I32).rearrange("e o (q r) w -> r q (e o) w", r=4))
         nc.sync.dma_start(out=w2_sb[:], in_=w2_words.bitcast(I32).rearrange("e o p w -> p (e o) w"))
@@ -239,14 +240,14 @@ def tile_moe_sup_glu_silu_kernel(
         product(0, 0)
         product(1, 0)
         pair_up(nc.vector.tensor_copy, 0, 0, HALF)
-        silu(0, 1)
-        product(0, 1)
-        nc.vector.tensor_copy(pairs[0][:, HALF:T, 0], plane_of(0)[:, HALF:T])
         for a in (0, QUARTER):
-            act = keep.tile([P, QUARTER], F32, name="act_quarter%d" % a)
-            nc.scalar.activation(act[:], first_layer(0, 1, 1, a, QUARTER)[:, 0:QUARTER], SILU)
             fresh = slice(HALF + a, HALF + a + QUARTER)
-            nc.vector.tensor_tensor(pairs[0][:, fresh, 1], first_layer(1, 1, 1, a, QUARTER)[:, 0:QUARTER], act[:], MULT)
+            for j, target in ((0, plane_of(0)[:, fresh]), (1, pairs[0][:, fresh, 1])):
+                act = keep.tile([P, QUARTER], F32, name="act_quarter%d_%d" % (j, a))
+                nc.scalar.activation(act[:], first_layer(0, j, 1, a, QUARTER)[:, 0:QUARTER], SILU)
+                nc.vector.tensor_tensor(target, first_layer(1, j, 1, a, QUARTER)[:, 0:QUARTER], act[:], MULT)
+                if j == 0:
+                    nc.vector.tensor_copy(pairs[0][:, fresh, 0], target)
             nc.gpsimd.tensor_copy(plane_of(1)[:, fresh], pairs[0][:, fresh, 1])
         pick_words(w3_raw, 1, 2, 2, 0)
         pick_scales(1, 2, 2, 0, PASSES)

@@ -34,11 +34,11 @@ ASIDE_PIECES = ((0, 256), (256, 384), (640, 384))
 LAST_WIDTHS = (256, 128, 128)
 QUANTISE_PIECES = (
     (0, 256), (256, 256), (512, 256), (768, 256),
-    (1024, 256), (1536, 256), (1792, 256),
+    (1536, 256), (1792, 256), (1024, 256),
     (1280, 128), (1408, 128),
 )
-SCALAR_BANKS = ((0, 512), (512, 512), (1024, 256), (1536, 256))
-VECTOR_BANKS = ((1792, 256), (1280, 128), (1408, 128))
+SCALAR_BANKS = ((0, 512), (512, 512), (1536, 512))
+VECTOR_BANKS = ((1024, 256), (1280, 128), (1408, 128))
 FUSED = 768
 
 
@@ -58,19 +58,19 @@ def tile_moe_sup_glu_silu_kernel(
         offs_sb = keep.tile([P, SLOTS // 16], U16, name="offs_sb")
         pos_sb = [keep.tile([P, T // 16], U16, name="pos_sb%d" % r) for r in range(2)]
 
-        raw_scales = [keep.tile([P, PASSES, H], U8, name="raw_scales%d" % m, align_bytes=64) for m in range(2)]
-        x_planes = [keep.tile([P, PASSES, HALF], U8, name="x_plane%d" % h, align_bytes=64) for h in range(2)]
-        w2_plane = keep.tile([P, E, N], U8, name="w2_plane", align_bytes=64)
+        raw_scales = [keep.tile([P, PASSES, H], U8, name="raw_scales%d" % m, align_bytes=256) for m in range(2)]
+        x_planes = [keep.tile([P, PASSES, HALF], U8, name="x_plane%d" % h, align_bytes=256) for h in range(2)]
+        w2_plane = keep.tile([P, E, N], U8, name="w2_plane", align_bytes=256)
         for scale_plane in (raw_scales[0], x_planes[0], raw_scales[1], x_planes[1], w2_plane):
             nc.vector.memset(scale_plane[:].bitcast(I32), 0)
 
-        w1_first = keep.tile([P, 1, H // 2], I32, name="w1_first", align_bytes=64)
-        w1_rest = keep.tile([P, PASSES - 1, H // 2], I32, name="w1_rest", align_bytes=64)
-        w3_raw = keep.tile([P, PASSES, H // 2], I32, name="w3_raw", align_bytes=64)
-        x_first = [keep.tile([P, HALF], I32, name="x_first%d" % s, align_bytes=64) for s in range(PASSES)]
-        x_second = keep.tile([P, PASSES, HALF], I32, name="x_second", align_bytes=64)
+        w1_first = keep.tile([P, 1, H // 2], I32, name="w1_first", align_bytes=256)
+        w1_rest = keep.tile([P, PASSES - 1, H // 2], I32, name="w1_rest", align_bytes=256)
+        w3_raw = keep.tile([P, PASSES, H // 2], I32, name="w3_raw", align_bytes=256)
+        x_first = [keep.tile([P, HALF], I32, name="x_first%d" % s, align_bytes=256) for s in range(PASSES)]
+        x_second = keep.tile([P, PASSES, HALF], I32, name="x_second", align_bytes=256)
         x_passes = [[words[:] for words in x_first], [x_second[:, s, :] for s in range(PASSES)]]
-        w2_sb = keep.tile([P, E, N // 2], I32, name="w2_sb", align_bytes=64)
+        w2_sb = keep.tile([P, E, N // 2], I32, name="w2_sb", align_bytes=256)
         gate_sb = keep.tile([P, 2, T], F32, name="gate_sb")
 
         x_view = x_words.rearrange("s p t d -> p s (t d)").bitcast(I32)
@@ -112,7 +112,7 @@ def tile_moe_sup_glu_silu_kernel(
         gathered = {}
 
         def make_gathered(first, last, tag):
-            gathered[first] = keep.tile([P, 2 * (last - first)], U32, name="gathered%d" % first, tag=tag, align_bytes=64)
+            gathered[first] = keep.tile([P, 2 * (last - first)], U32, name="gathered%d" % first, tag=tag, align_bytes=256)
 
         make_gathered(0, WOVEN_ASIDE, "gathered0")
 
@@ -121,7 +121,7 @@ def tile_moe_sup_glu_silu_kernel(
 
         def pick_scales(m, first, count, first_pass, passes):
             name = "scales%d_%d_%d" % (m, first, first_pass)
-            picked = keep.tile([P, count, passes * P], U8, name=name, tag=name, align_bytes=64)
+            picked = keep.tile([P, count, passes * P], U8, name=name, tag=name, align_bytes=256)
             rows = raw_scales[m][:, first_pass : first_pass + passes, :]
             source = rows.rearrange("p s c -> p (s c)").rearrange("p (b i j) -> p b j i", i=16, j=4)
             nc.vector.tensor_copy(
@@ -134,7 +134,7 @@ def tile_moe_sup_glu_silu_kernel(
         def pick_words(raw, m, first, count, first_pass):
             passes = raw.shape[1]
             name = "words%d_%d_%d" % (m, first, first_pass)
-            picked = keep.tile([P, count, passes * 2 * P], U8, name=name, align_bytes=64)
+            picked = keep.tile([P, count, passes * 2 * P], U8, name=name, align_bytes=256)
             source = raw[:].bitcast(U16).rearrange("p s c -> p (s c)").rearrange("p (b i j) -> p b j i", i=8, j=4)
             nc.vector.tensor_copy(
                 out=picked[:].bitcast(U16).rearrange("p e (b i) -> p b e i", i=8),
@@ -171,8 +171,8 @@ def tile_moe_sup_glu_silu_kernel(
                 first_layer_pass(acc[:, 0:n], m, j, h, s, a, n)
             return acc
 
-        pairs = [keep.tile([P, T, 2], BF16, name="pairs%d" % u, tag="pairs%d" % u, align_bytes=64) for u in range(2)]
-        planes = [keep.tile([P, 2 * T], BF16, name="planes%d" % u, align_bytes=64) for u in range(2)]
+        pairs = [keep.tile([P, T, 2], BF16, name="pairs%d" % u, tag="pairs%d" % u, align_bytes=256) for u in range(2)]
+        planes = [keep.tile([P, 2 * T], BF16, name="planes%d" % u, align_bytes=256) for u in range(2)]
         def plane_of(j):
             return planes[j // 2][:, (j % 2) * T : (j % 2 + 1) * T]
 
@@ -192,7 +192,7 @@ def tile_moe_sup_glu_silu_kernel(
 
         def silu_of(j, h, acc):
             if (j, h) not in acts:
-                acts[(j, h)] = keep.tile([P, HALF], F32, name="act%d_%d" % (j, h), tag="act%d_%d" % (j, h), align_bytes=64)[:]
+                acts[(j, h)] = keep.tile([P, HALF], F32, name="act%d_%d" % (j, h), tag="act%d_%d" % (j, h), align_bytes=256)[:]
             nc.scalar.activation(acts[(j, h)], acc[:], SILU)
 
         def silu(j, h):
@@ -225,11 +225,13 @@ def tile_moe_sup_glu_silu_kernel(
                     late_acts[:, a // QUARTER, :, a % QUARTER : a % QUARTER + n].rearrange("p e n -> p n e"),
                     MULT,
                 )
-                nc.gpsimd.tensor_copy(
-                    planes[1][:].rearrange("p (e t) -> p e t", e=2)[:, :, fresh],
-                    pairs[1][:, fresh, :].rearrange("p t e -> p e t"),
-                )
                 a = a + n
+                if a % QUARTER == 0:
+                    whole = slice(HALF + a - QUARTER, HALF + a)
+                    nc.gpsimd.tensor_copy(
+                        planes[1][:].rearrange("p (e t) -> p e t", e=2)[:, :, whole],
+                        pairs[1][:, whole, :].rearrange("p t e -> p e t"),
+                    )
 
         opening = [psum.tile([P, HALF], F32, name="acc") for j in range(OPENING_SUMS)]
         for s in range(PASSES):
@@ -270,7 +272,7 @@ def tile_moe_sup_glu_silu_kernel(
         for j in range(2):
             gather_plane(j, LATE, SLOTS - LATE)
 
-        woven = keep.tile([P, 2 * SLOTS], U32, name="woven", align_bytes=64)
+        woven = keep.tile([P, 2 * SLOTS], U32, name="woven", align_bytes=256)
 
         def weave(copy, a, n):
             target = woven[:, 2 * a : 2 * (a + n)]
@@ -281,18 +283,18 @@ def tile_moe_sup_glu_silu_kernel(
 
         for a, n in ASIDE_PIECES + ((WOVEN_ASIDE, MIDDLE - WOVEN_ASIDE), (MIDDLE, LATE - MIDDLE)):
             gather_pair(1, a, n)
-        weave(nc.vector.tensor_copy, WOVEN_ASIDE, QUARTER)
+        weave(nc.vector.tensor_copy, WOVEN_ASIDE, P)
         gather_plane(2, LATE, SLOTS - LATE)
         for a in (LATE, LATE + QUARTER):
             gather_plane(3, a, QUARTER)
         for a, n in ASIDE_PIECES:
             weave(nc.gpsimd.tensor_copy, a, n)
-        for a, n in ((LATE, QUARTER), (LATE + QUARTER, QUARTER), (WOVEN_ASIDE + QUARTER, P), (MIDDLE, P)):
+        for a, n in ((LATE, QUARTER), (LATE + QUARTER, QUARTER), (WOVEN_ASIDE + P, QUARTER), (MIDDLE, P)):
             weave(nc.scalar.copy, a, n)
 
-        codes = keep.tile([P, SLOTS], U32, name="codes", tag="gathered0", align_bytes=64)
+        codes = keep.tile([P, SLOTS], U32, name="codes", tag="gathered0", align_bytes=256)
         for a, n in QUANTISE_PIECES:
-            h_scales = keep.tile([P, n], U8, name="h_scales%d" % a, align_bytes=64)
+            h_scales = keep.tile([P, n], U8, name="h_scales%d" % a, align_bytes=256)
             nc.vector.quantize_mx(
                 out=codes[:, a : a + n].bitcast(FP8X4), scales=h_scales[:], in_=woven[:, 2 * a : 2 * (a + n)].bitcast(BF16)
             )

from contextlib import ExitStack

import concourse.mybir as mybir

K, T, E, C, H, N = 1536, 1024, 16, 128, 512, 128
FLOPS = 2 * (2 * K * H * T + H * N * E * C)

F32 = mybir.dt.float32
BF16 = mybir.dt.bfloat16
I32 = mybir.dt.int32
U32 = mybir.dt.uint32
U16 = mybir.dt.uint16
U8 = mybir.dt.uint8
FP8X4 = mybir.dt.float8_e4m3fn_x4
FP4X4 = mybir.dt.float4_e2m1fn_x4
MULT = mybir.AluOpType.mult
ADD = mybir.AluOpType.add
SILU = mybir.ActivationFunctionType.Silu
COPY = mybir.ActivationFunctionType.Copy

P = 128
PASSES = K // 512
HALF = 512
QUARTER = 256
SLOTS = E * C
WARM_PASSES = 3
OPENING_SUMS = 3

FIRST = 384
WOVEN_ASIDE = 1024
MIDDLE = 1408
LATE = 1536
ASIDE_PIECES = ((0, 256), (256, 384), (640, 384))
LAST_WIDTHS = (256, 128, 128)
QUANTISE_PIECES = (
    (0, 256), (256, 256), (512, 256), (768, 256),
    (1536, 256), (1792, 256), (1024, 256),
    (1280, 128), (1408, 128),
)
SCALAR_BANKS = ((0, 512), (512, 512), (1536, 512))
VECTOR_BANKS = ((1024, 256), (1280, 128), (1408, 128))
FUSED = 768


def load_scale_rows(nc, plane, rows):
    for r in range(4):
        nc.sync.dma_start(out=plane[r:P:32, :, :].bitcast(I32), in_=rows[r])


def tile_moe_sup_glu_silu_kernel(
    tc, x_words, x_scales, w1_words, w1_scales, w3_words, w3_scales, w2_words, w2_scales, gate, offs, pos1, pos2, out
):
    nc = tc.nc
    with ExitStack() as ctx:
        keep = ctx.enter_context(tc.tile_pool(name="keep", bufs=1))
        psum = ctx.enter_context(tc.psum_pool(name="psum", bufs=8))

        offs_sb = keep.tile([P, SLOTS // 16], U16, name="offs_sb")
        pos_sb = [keep.tile([P, T // 16], U16, name="pos_sb%d" % r) for r in range(2)]

        raw_scales = [keep.tile([P, PASSES, H], U8, name="raw_scales%d" % m, align_bytes=256) for m in range(2)]
        x_planes = [keep.tile([P, PASSES, HALF], U8, name="x_plane%d" % h, align_bytes=256) for h in range(2)]
        w2_plane = keep.tile([P, E, N], U8, name="w2_plane", align_bytes=256)
        for scale_plane in (raw_scales[0], x_planes[0], raw_scales[1], x_planes[1], w2_plane):
            nc.vector.memset(scale_plane[:].bitcast(I32), 0)

        w1_first = keep.tile([P, 1, H // 2], I32, name="w1_first", align_bytes=256)
        w1_rest = keep.tile([P, PASSES - 1, H // 2], I32, name="w1_rest", align_bytes=256)
        w3_raw = keep.tile([P, PASSES, H // 2], I32, name="w3_raw", align_bytes=256)
        x_first = [keep.tile([P, HALF], I32, name="x_first%d" % s, align_bytes=256) for s in range(PASSES)]
        x_second = keep.tile([P, PASSES, HALF], I32, name="x_second", align_bytes=256)
        x_passes = [[words[:] for words in x_first], [x_second[:, s, :] for s in range(PASSES)]]
        w2_sb = keep.tile([P, E, N // 2], I32, name="w2_sb", align_bytes=256)
        gate_sb = keep.tile([P, 2, T], F32, name="gate_sb")

        x_view = x_words.rearrange("s p t d -> p s (t d)").bitcast(I32)
        by_row = "a (q r) w -> r q a w"
        x_rows = x_scales.bitcast(I32).rearrange(by_row, r=4)
        w1_view = w1_words.bitcast(I32).rearrange("s p w -> p s w")
        nc.sync.dma_start(out=x_first[0][:, 0:P], in_=x_view[:, 0, 0:P])
        nc.sync.dma_start(out=w1_first[:], in_=w1_view[:, 0:1, :])
        load_scale_rows(nc, raw_scales[0], w1_scales.bitcast(I32).rearrange(by_row, r=4))
        nc.sync.dma_start(out=x_first[0][:, P:HALF], in_=x_view[:, 0, P:HALF])
        nc.sync.dma_start(out=w1_rest[:], in_=w1_view[:, 1:PASSES, :])
        load_scale_rows(nc, x_planes[0], x_rows[:, :, :, 0 : HALF // 4])
        for s in range(1, PASSES):
            nc.sync.dma_start(out=x_first[s][:], in_=x_view[:, s, 0:HALF])
        load_scale_rows(nc, raw_scales[1], w3_scales.bitcast(I32).rearrange(by_row, r=4))
        nc.sync.dma_start(out=w3_raw[:], in_=w3_words.bitcast(I32).rearrange("s p w -> p s w"))
        load_scale_rows(nc, x_planes[1], x_rows[:, :, :, HALF // 4 : T // 4])
        for a in (0, QUARTER):
            nc.sync.dma_start(out=x_second[:, :, a : a + QUARTER], in_=x_view[:, :, HALF + a : HALF + a + QUARTER])
        nc.sync.dma_start(offs_sb[:], offs)
        load_scale_rows(nc, w2_plane, w2_scales.bitcast(I32).rearrange("e o (q r) w -> r q (e o) w", r=4))
        nc.sync.dma_start(out=w2_sb[:], in_=w2_words.bitcast(I32).rearrange("e o p w -> p (e o) w"))
        nc.sync.dma_start(pos_sb[0][:], pos1)
        nc.sync.dma_start(pos_sb[1][:], pos2)
        nc.sync.dma_start(out=gate_sb[:], in_=gate.rearrange("r p t -> p r t"))

        warm_acc = psum.tile([P, HALF], F32, name="acc")
        for k in range(WARM_PASSES):
            nc.tensor.matmul_mx(
                out=warm_acc[:],
                lhsT=x_first[0][:, 0:P].bitcast(FP8X4),
                lhsT_scale=w1_first[:, 0, 0 : P // 4].bitcast(U8),
                rhs=w1_first[:, 0, :].bitcast(FP4X4),
                rhs_scale=w1_first[:, 0, 0:P].bitcast(U8),
                start=True,
                stop=True,
            )

        gathered = {}

        def make_gathered(first, last, tag):
            gathered[first] = keep.tile([P, 2 * (last - first)], U32, name="gathered%d" % first, tag=tag, align_bytes=256)

        make_gathered(0, WOVEN_ASIDE, "gathered0")

        picked_words = {}
        picked_scales = {}

        def pick_scales(m, first, count, first_pass, passes):
            name = "scales%d_%d_%d" % (m, first, first_pass)
            picked = keep.tile([P, count, passes * P], U8, name=name, tag=name, align_bytes=256)
            rows = raw_scales[m][:, first_pass : first_pass + passes, :]
            source = rows.rearrange("p s c -> p (s c)").rearrange("p (b i j) -> p b j i", i=16, j=4)
            nc.vector.tensor_copy(
                out=picked[:, :, :].rearrange("p e (b i) -> p b e i", i=16), in_=source[:, :, first : first + count, :]
            )
            for e in range(count):
                for s in range(passes):
                    picked_scales[(m, first + e, first_pass + s)] = picked[:, e, P * s : P * (s + 1)]

        def pick_words(raw, m, first, count, first_pass):
            passes = raw.shape[1]
            name = "words%d_%d_%d" % (m, first, first_pass)
            picked = keep.tile([P, count, passes * 2 * P], U8, name=name, align_bytes=256)
            source = raw[:].bitcast(U16).rearrange("p s c -> p (s c)").rearrange("p (b i j) -> p b j i", i=8, j=4)
            nc.vector.tensor_copy(
                out=picked[:].bitcast(U16).rearrange("p e (b i) -> p b e i", i=8),
                in_=source[:, :, first : first + count, :],
            )
            for e in range(count):
                for s in range(passes):
                    picked_words[(m, first + e, first_pass + s)] = picked[:, e, 2 * P * s : 2 * P * (s + 1)]

        pick_words(w1_first, 0, 0, 4, 0)
        pick_scales(0, 0, 4, 0, 1)
        pick_scales(0, 0, 4, 1, 1)
        pick_words(w1_rest, 0, 0, 4, 1)
        for j in range(4):
            pick_scales(0, j, 1, 2, 1)
        pick_scales(1, 0, 2, 0, PASSES)
        pick_words(w3_raw, 1, 0, 1, 0)
        pick_words(w3_raw, 1, 1, 1, 0)

        def first_layer_pass(acc, m, j, h, s, a, n):
            nc.tensor.matmul_mx(
                out=acc,
                lhsT=picked_words[(m, j, s)].bitcast(FP4X4),
                lhsT_scale=picked_scales[(m, j, s)],
                rhs=x_passes[h][s][:, a : a + n].bitcast(FP8X4),
                rhs_scale=x_planes[h][:, s, a : a + n],
                start=(s == 0),
                stop=(s == PASSES - 1),
            )

        def first_layer(m, j, h, a=0, n=HALF):
            acc = psum.tile([P, HALF], F32, name="acc")
            for s in range(PASSES):
                first_layer_pass(acc[:, 0:n], m, j, h, s, a, n)
            return acc

        pairs = [keep.tile([P, T, 2], BF16, name="pairs%d" % u, tag="pairs%d" % u, align_bytes=256) for u in range(2)]
        planes = [keep.tile([P, 2 * T], BF16, name="planes%d" % u, align_bytes=256) for u in range(2)]
        def plane_of(j):
            return planes[j // 2][:, (j % 2) * T : (j % 2 + 1) * T]

        def words_of(a, n):
            first = max(b for b in gathered if b <= a)
            return gathered[first][:].rearrange("p (u n) -> p u n", u=2)[:, :, a - first : a - first + n]

        def gather_pair(u, a, n):
            window = pairs[u][:].rearrange("p t e -> p (t e)").bitcast(U32)
            nc.vector.tensor_copy(words_of(a, n)[:, u, :], window.indirect(offs_sb[:, a // 16 : (a + n) // 16]))

        def gather_plane(j, a, n):
            halves = words_of(a, n)[:, j // 2, :].bitcast(BF16).rearrange("p (n e) -> p n e", e=2)
            nc.scalar.activation(halves[:, :, j % 2], plane_of(j).indirect(offs_sb[:, a // 16 : (a + n) // 16]), COPY)

        acts = {(3, 0): gathered[0][:, FIRST : FIRST + HALF].bitcast(F32)}

        def silu_of(j, h, acc):
            if (j, h) not in acts:
                acts[(j, h)] = keep.tile([P, HALF], F32, name="act%d_%d" % (j, h), tag="act%d_%d" % (j, h), align_bytes=256)[:]
            nc.scalar.activation(acts[(j, h)], acc[:], SILU)

        def silu(j, h):
            silu_of(j, h, first_layer(0, j, h))

        def product(j, h):
            acc = first_layer(1, j, h)
            nc.vector.tensor_tensor(plane_of(j)[:, h * HALF : (h + 1) * HALF], acc[:], acts[(j, h)], MULT)

        def pair_up(copy, u, a, n):
            copy(pairs[u][:, a : a + n, :], planes[u][:].rearrange("p (e t) -> p t e", e=2)[:, a : a + n, :])

        late_acts = keep.tile([P, 2, 2, QUARTER], F32, name="late_acts")

        def late_silu(e):
            sums = first_layer(0, 2 + e, 1)[:].rearrange("p (b n) -> p b n", b=2)
            nc.scalar.activation(late_acts[:, :, e, :], sums, SILU)

        def late_products():
            a = 0
            for n in LAST_WIDTHS:
                acc = psum.tile([P, HALF], F32, name="acc")
                for e in range(2):
                    for s in range(PASSES):
                        first_layer_pass(acc[:, e * n : (e + 1) * n], 1, 2 + e, 1, s, a, n)
                fresh = slice(HALF + a, HALF + a + n)
                nc.vector.tensor_tensor(
                    pairs[1][:, fresh, :],
                    acc[:, 0 : 2 * n].rearrange("p (e n) -> p n e", e=2),
                    late_acts[:, a // QUARTER, :, a % QUARTER : a % QUARTER + n].rearrange("p e n -> p n e"),
                    MULT,
                )
                a = a + n
                if a % QUARTER == 0:
                    whole = slice(HALF + a - QUARTER, HALF + a)
                    nc.gpsimd.tensor_copy(
                        planes[1][:].rearrange("p (e t) -> p e t", e=2)[:, :, whole],
                        pairs[1][:, whole, :].rearrange("p t e -> p e t"),
                    )

        opening = [psum.tile([P, HALF], F32, name="acc") for j in range(OPENING_SUMS)]
        for s in range(PASSES):
            for j in range(OPENING_SUMS):
                first_layer_pass(opening[j][:], 0, j, 0, s, 0, HALF)
        for j in range(OPENING_SUMS):
            silu_of(j, 0, opening[j])
        product(0, 0)
        product(1, 0)
        pair_up(nc.vector.tensor_copy, 0, 0, HALF)
        for a in (0, QUARTER):
            fresh = slice(HALF + a, HALF + a + QUARTER)
            for j, target in ((0, plane_of(0)[:, fresh]), (1, pairs[0][:, fresh, 1])):
                act = keep.tile([P, QUARTER], F32, name="act_quarter%d_%d" % (j, a))
                nc.scalar.activation(act[:], first_layer(0, j, 1, a, QUARTER)[:, 0:QUARTER], SILU)
                nc.vector.tensor_tensor(target, first_layer(1, j, 1, a, QUARTER)[:, 0:QUARTER], act[:], MULT)
                if j == 0:
                    nc.vector.tensor_copy(pairs[0][:, fresh, 0], target)
            nc.gpsimd.tensor_copy(plane_of(1)[:, fresh], pairs[0][:, fresh, 1])
        pick_words(w3_raw, 1, 2, 2, 0)
        pick_scales(1, 2, 2, 0, PASSES)

        make_gathered(WOVEN_ASIDE, MIDDLE, "scales0_1_2")
        gather_pair(0, 0, FIRST)
        silu(3, 0)
        product(2, 0)
        make_gathered(MIDDLE, LATE, "act2_0")
        product(3, 0)
        pair_up(nc.gpsimd.tensor_copy, 1, 0, HALF)
        late_silu(0)
        late_silu(1)
        for a, b in ((WOVEN_ASIDE, MIDDLE), (MIDDLE, LATE)):
            for j in range(2):
                gather_plane(j, a, b - a)
        gather_pair(0, FIRST, WOVEN_ASIDE - FIRST)
        late_products()
        make_gathered(LATE, SLOTS, "scales0_3_2")
        for j in range(2):
            gather_plane(j, LATE, SLOTS - LATE)

        woven = keep.tile([P, 2 * SLOTS], U32, name="woven", align_bytes=256)

        def weave(copy, a, n):
            target = woven[:, 2 * a : 2 * (a + n)]
            copy(target.rearrange("p (n u) -> p n u", u=2), words_of(a, n).rearrange("p u n -> p n u"))

        y = keep.tile([P, SLOTS], F32, name="y")
        quantised = {}

        for a, n in ASIDE_PIECES + ((WOVEN_ASIDE, MIDDLE - WOVEN_ASIDE), (MIDDLE, LATE - MIDDLE)):
            gather_pair(1, a, n)
        weave(nc.vector.tensor_copy, WOVEN_ASIDE, P)
        gather_plane(2, LATE, SLOTS - LATE)
        for a in (LATE, LATE + QUARTER):
            gather_plane(3, a, QUARTER)
        for a, n in ASIDE_PIECES:
            weave(nc.gpsimd.tensor_copy, a, n)
        for a, n in ((LATE, QUARTER), (LATE + QUARTER, QUARTER), (WOVEN_ASIDE + P, QUARTER), (MIDDLE, P)):
            weave(nc.scalar.copy, a, n)

        codes = keep.tile([P, SLOTS], U32, name="codes", tag="gathered0", align_bytes=256)
        for a, n in QUANTISE_PIECES:
            h_scales = keep.tile([P, n], U8, name="h_scales%d" % a, align_bytes=256)
            nc.vector.quantize_mx(
                out=codes[:, a : a + n].bitcast(FP8X4), scales=h_scales[:], in_=woven[:, 2 * a : 2 * (a + n)].bitcast(BF16)
            )
            for k in range(n // C):
                quantised[a // C + k] = (codes[:, a + k * C : a + (k + 1) * C], h_scales[:, k * C : (k + 1) * C])

        def second_layer(a, n, copy):
            acc = psum.tile([P, HALF], F32, name="acc")
            for k in range(n // C):
                e = a // C + k
                nc.tensor.matmul_mx(
                    out=acc[:, k * C : (k + 1) * C],
                    lhsT=w2_sb[:, e, :].bitcast(FP4X4),
                    lhsT_scale=w2_plane[:, e, :],
                    rhs=quantised[e][0].bitcast(FP8X4),
                    rhs_scale=quantised[e][1],
                    start=True,
                    stop=True,
                )
            copy(y[:, a : a + n], acc[:, 0:n])

        for a, n in SCALAR_BANKS:
            second_layer(a, n, nc.scalar.copy)
        for a, n in VECTOR_BANKS:
            second_layer(a, n, nc.vector.tensor_copy)

        def slots_of(r, a, n):
            return y[:].indirect(pos_sb[r][:, a // 16 : (a + n) // 16])

        fetched = keep.tile([P, 2, T], F32, name="fetched")
        shares = keep.tile([P, 2, T], F32, name="shares")

        def fused(a, n):
            nc.vector.tensor_tensor(shares[:, 0, a : a + n], slots_of(0, a, n), gate_sb[:, 0, a : a + n], MULT)

        def fetch(r, a, n):
            nc.scalar.activation(fetched[:, r, a : a + n], slots_of(r, a, n), COPY)

        def weigh(r, a, n):
            nc.vector.tensor_tensor(shares[:, r, a : a + n], fetched[:, r, a : a + n], gate_sb[:, r, a : a + n], MULT)

        def combine(a, n):
            total = keep.tile([P, n], F32, name="total%d" % a)
            nc.vector.tensor_tensor(total[:], shares[:, 0, a : a + n], shares[:, 1, a : a + n], ADD)
            nc.sync.dma_start(out=out[:, a : a + n], in_=total[:])

        piece = FUSED // 2
        fused(0, piece)
        fused(piece, piece)
        fetch(1, 0, piece)
        fetch(1, piece, piece)
        fetch(0, FUSED, T - FUSED)
        fetch(1, FUSED, T - FUSED)
        weigh(1, 0, piece)
        weigh(1, piece, piece)
        combine(0, piece)
        weigh(0, FUSED, T - FUSED)
        weigh(1, FUSED, T - FUSED)
        combine(piece, piece)
        combine(FUSED, T - FUSED)
